import numpy as np
import ml_dtypes


def mxq(x, axis, fmt="e4m3"):
    dtype, down = {"e4m3": (ml_dtypes.float8_e4m3fn, 7), "e5m2": (ml_dtypes.float8_e5m2, 14)}[fmt]
    v = np.moveaxis(np.asarray(x, np.float32).astype(ml_dtypes.bfloat16).astype(np.float64), axis, -1)
    blocks = v.reshape(v.shape[:-1] + (-1, 32))
    amax = np.abs(blocks).max(-1, keepdims=True)
    byte = np.maximum(np.where(amax > 0, np.frexp(amax)[1] - 1 + 127, 0) - down, 1)
    scale = np.exp2(byte - 127.0)
    codes = (blocks / scale).astype(np.float32).astype(dtype).astype(np.float64)
    return np.moveaxis((codes * scale).reshape(v.shape), -1, axis)


WIDE = False


def mx_kscale(k):
    if not WIDE:
        return np.ones(k)
    levels = np.array([30, -30])
    if k % 512:
        return np.exp2(np.random.permutation(np.resize(levels, k // 32))).repeat(32)
    a = np.empty((k // 512, 16))
    for p in range(k // 512):
        a[p, :8] = np.random.permutation(np.resize(levels, 8))
        for g in range(8):
            far = levels[np.abs(levels - a[p, g]) >= 10]
            a[p, g + 8] = far[np.random.randint(len(far))]
    return np.exp2(a.ravel()).repeat(32)


def f64(x):
    return np.asarray(x).astype(np.float64)


def striped(idx):
    return np.tile(idx.reshape(-1, 16).T, (8, 1)).astype(np.uint16)


def unstriped(offs):
    return offs[:16].T.reshape(-1).astype(np.int64)


E2M1 = np.array([0.0, 0.5, 1.0, 1.5, 2.0, 3.0, 4.0, 6.0, -0.0, -0.5, -1.0, -1.5, -2.0, -3.0, -4.0, -6.0])


def pack_weight(w, fmt):
    k, n = w.shape
    w = f64(np.asarray(w, np.float32).astype(ml_dtypes.bfloat16)).reshape(k // 32, 32, n)
    amax = np.abs(w).max(1)
    if fmt == "e4m3":
        byte = np.frexp(amax)[1] - 1 + 127 - 7
    else:
        mant, ex = np.frexp(amax / 6.0)
        byte = np.where(mant > 0.5, ex, ex - 1) + 127
    byte = np.clip(np.where(amax > 0, byte, 1), 1, 254)
    scaled = (w * np.exp2(127.0 - byte)[:, None, :]).reshape(k, n).astype(np.float32)
    by_word = np.ascontiguousarray(scaled.reshape(k // 512, 128, 4, n).transpose(0, 1, 3, 2))
    if fmt == "e4m3":
        words = by_word.astype(ml_dtypes.float8_e4m3fn).view(np.uint8)
    else:
        c = by_word.astype(ml_dtypes.float4_e2m1fn).view(np.uint8) & 0xF
        words = (c[..., 0::2] | (c[..., 1::2] << 4)).reshape(k // 512, 128, 2 * n)
    return np.ascontiguousarray(words), np.ascontiguousarray(byte.astype(np.uint8).reshape(k // 512, 16, n))


def unpack_weight(words, scales, fmt):
    g, _, n = scales.shape
    words = np.ascontiguousarray(words).reshape(g, 128, n, -1)
    if fmt == "e4m3":
        vals = words.view(ml_dtypes.float8_e4m3fn).astype(np.float64)
    else:
        nib = np.empty((g, 128, n, 4), np.uint8)
        nib[..., 0::2] = words & 0xF
        nib[..., 1::2] = words >> 4
        vals = E2M1[nib]
    vals = vals * np.repeat(np.exp2(scales.astype(np.float64) - 127.0), 8, axis=1)[..., None]
    return vals.transpose(0, 1, 3, 2).reshape(g * 512, n)


def silu(v):
    return v / (1.0 + np.exp(-np.maximum(v, -700.0)))


def d_silu(v):
    s = 1.0 / (1.0 + np.exp(-np.maximum(v, -700.0)))
    return s * (1.0 + v * (1.0 - s))


K, T, E, C, H, N = 384, 1536, 6, 512, 512, 512


def by_expert(wq, xq):
    return np.concatenate([wq[e].T @ xq[:, e * C:(e + 1) * C] for e in range(E)], axis=1)


def setup_inputs():
    n = np.random.standard_normal
    s = mx_kscale(N)[:, None]
    u = mx_kscale(H)
    first = np.random.permutation(np.repeat(np.arange(E), T // E))
    second = (first + 1 + np.random.permutation(np.repeat(np.arange(E - 1), -(-T // (E - 1)))[:T])) % E
    while np.bincount(second, minlength=E).max() != T // E:
        load = np.bincount(second, minlength=E); hi, lo = int(load.argmax()), int(load.argmin())
        t = np.flatnonzero((second == hi) & (first != lo))[0]; second[t] = lo
    slot_token = np.empty(E * C, np.int64); pos = np.empty((2, T), np.int64); fill = np.zeros(E, np.int64)
    place = np.stack([np.random.permutation(C) for _ in range(E)])
    for r, deal in enumerate((first, second)):
        for t in np.random.permutation(T):
            e = deal[t]; j = e * C + place[e, fill[e]]; fill[e] += 1; slot_token[j] = t; pos[r, t] = j
    g = np.random.uniform(0.2, 0.8, T)
    w_slot = np.empty(E * C); w_slot[pos[0]] = g; w_slot[pos[1]] = 1.0 - g
    w2 = [pack_weight(m, "e2m1") for m in n((E, N, H)) / np.sqrt(N) / s[None] * u[None, None, :]]
    w1 = [pack_weight(m, "e2m1") for m in n((E, H, K)) / np.sqrt(H) / u[None, :, None]]
    w3 = [pack_weight(m, "e2m1") for m in n((E, H, K)) / np.sqrt(H) / u[None, :, None]]
    return {
        "dyT": (n((N, T)) * s).astype(np.float32),
        "a1": n((H, E * C)).astype(np.float32),
        "a3": n((H, E * C)).astype(np.float32),
        "w2_words": np.stack([m[0] for m in w2]),
        "w2_scales": np.stack([m[1] for m in w2]),
        "w1_words": np.stack([m[0] for m in w1]),
        "w1_scales": np.stack([m[1] for m in w1]),
        "w3_words": np.stack([m[0] for m in w3]),
        "w3_scales": np.stack([m[1] for m in w3]),
        "gate": np.tile(w_slot, (N, 1)).astype(np.float32),
        "offs": striped(slot_token),
        "pos1": striped(pos[0]),
        "pos2": striped(pos[1]),
    }


def reference(dyT, a1, a3, w2_words, w2_scales, w1_words, w1_scales, w3_words, w3_scales, gate, offs, pos1, pos2):
    idx = unstriped(offs)
    w2 = np.stack([unpack_weight(w2_words[e], w2_scales[e], "e2m1") for e in range(E)])
    w1 = np.stack([unpack_weight(w1_words[e], w1_scales[e], "e2m1") for e in range(E)])
    w3 = np.stack([unpack_weight(w3_words[e], w3_scales[e], "e2m1") for e in range(E)])
    gq = mxq(f64(gate) * f64(dyT)[:, idx], 0, "e5m2")
    dh = by_expert(w2, gq)
    da1 = dh * f64(a3) * d_silu(f64(a1))
    da3 = dh * silu(f64(a1))
    dx = by_expert(w1, mxq(da1, 0, "e5m2")) + by_expert(w3, mxq(da3, 0, "e5m2"))
    return dx[:, unstriped(pos1)] + dx[:, unstriped(pos2)]

@@ -1,0 +1,275 @@
+from contextlib import ExitStack
+
+import concourse.mybir as mybir
+
+K, T, E, C, H, N = 384, 1536, 6, 512, 512, 512
+S = E * C
+
+FLOPS = 2 * S * (N * H + 2 * H * K)
+BYTES = 4 * (N * T + 2 * H * S + S + K * T) + E * (N * H // 2 + H * K) + E * 16 * (H + 2 * K) + 2 * (S + 2 * T)
+
+F32 = mybir.dt.float32
+BF16 = mybir.dt.bfloat16
+U32 = mybir.dt.uint32
+I32 = mybir.dt.int32
+U16 = mybir.dt.uint16
+U8 = mybir.dt.uint8
+E5M2X4 = mybir.dt.float8_e5m2_x4
+E2M1X4 = mybir.dt.float4_e2m1fn_x4
+
+ADD = mybir.AluOpType.add
+SUB = mybir.AluOpType.subtract
+MULT = mybir.AluOpType.mult
+ACT = mybir.ActivationFunctionType
+
+P = 128
+W = 4
+KT = K // P
+
+
+def tile_moe_bdx_glu_silu_kernel(
+    tc, dyT, a1, a3, w2_words, w2_scales, w1_words, w1_scales, w3_words, w3_scales, gate, offs, pos1, pos2, out
+):
+    nc = tc.nc
+    with ExitStack() as ctx:
+        keep = ctx.enter_context(tc.tile_pool(name="keep", bufs=1))
+        flow = ctx.enter_context(tc.tile_pool(name="flow", bufs=2))
+        psum = ctx.enter_context(tc.psum_pool(name="psum", bufs=1))
+
+        offs_sb = keep.tile([P, S // 16], U16, name="offs_sb")
+        pos1_sb = keep.tile([P, T // 16], U16, name="pos1_sb")
+        pos2_sb = keep.tile([P, T // 16], U16, name="pos2_sb")
+        dy = []
+        for t in range(W):
+            dy_t = keep.tile([P, T], F32, name=f"dy{t}")
+            dy.append(dy_t)
+        gate_sb = keep.tile([P, S], F32, name="gate_sb")
+        w2_sb = keep.tile([P, E, 2 * H], U8, name="w2_sb", align_bytes=64)
+        w1_sb = keep.tile([P, E, 2 * K], U8, name="w1_sb", align_bytes=64)
+        w3_sb = keep.tile([P, E, 2 * K], U8, name="w3_sb", align_bytes=64)
+        w2_sc = keep.tile([P, E, H], U8, name="w2_sc", align_bytes=64)
+        w1_sc = keep.tile([P, E, K], U8, name="w1_sc", align_bytes=64)
+        w3_sc = keep.tile([P, E, K], U8, name="w3_sc", align_bytes=64)
+        w2_raw = flow.tile([P, E, 2 * H], U8, name="w2_raw", tag="dr", bufs=1, align_bytes=64)
+        w2_rawsc = flow.tile([P, E, H], U8, name="w2_rawsc", tag="da3", bufs=1, align_bytes=64)
+
+        warm = keep.tile([P, 1], F32, name="warm")
+        nc.vector.memset(warm[:], 0.0)
+        nc.scalar.activation(warm[:], warm[:], ACT.Silu)
+        nc.gpsimd.memset(w2_rawsc[:].rearrange("p e i -> p (e i)").bitcast(U32), 0)
+        nc.gpsimd.memset(w1_sc[:].rearrange("p e i -> p (e i)").bitcast(U32), 0)
+        nc.gpsimd.memset(w3_sc[:].rearrange("p e i -> p (e i)").bitcast(U32), 0)
+
+        dy_rows = dyT.rearrange("(p t) c -> t p c", t=W)
+        a1_rows = a1.rearrange("(p t) c -> p t c", t=W)
+        a3_rows = a3.rearrange("(p t) c -> p t c", t=W)
+
+        def load_words(dst, words, e0=0, e1=E):
+            nc.sync.dma_start(
+                out=dst[:, e0:e1].bitcast(I32), in_=words[e0:e1, 0].bitcast(I32).rearrange("e p b -> p e b")
+            )
+
+        def load_scales(dst, scales):
+            rows = scales[:, 0].bitcast(I32).rearrange("e f i -> f e i")
+            for q in range(4):
+                nc.sync.dma_start(out=dst[32 * q : 32 * q + 4].bitcast(I32), in_=rows[4 * q : 4 * q + 4])
+
+        a1_t, a3_t = {}, {}
+
+        def load_a1(e):
+            a1_t[e] = flow.tile([P, W, C], F32, name="a1_sb", tag="a1", bufs=3)
+            nc.sync.dma_start(out=a1_t[e][:], in_=a1_rows[:, :, e * C : (e + 1) * C])
+
+        def load_a3(e):
+            a3_t[e] = flow.tile([P, W, C], F32, name="a3_sb", tag="a3")
+            nc.sync.dma_start(out=a3_t[e][:], in_=a3_rows[:, :, e * C : (e + 1) * C])
+
+        def load_gate(c0, c1):
+            nc.sync.dma_start(out=gate_sb[:, c0:c1], in_=gate[:P, c0:c1])
+
+        for e in range(0, E, 2):
+            load_words(w2_raw, w2_words, e, e + 2)
+        nc.sync.dma_start(offs_sb[:], offs)
+        load_gate(0, 2 * C)
+        for t in range(W):
+            nc.sync.dma_start(out=dy[t][:], in_=dy_rows[t])
+        load_a1(0)
+        load_scales(w2_rawsc, w2_scales)
+        load_gate(2 * C, S)
+        load_a3(0)
+        load_a1(1)
+        load_a3(1)
+        load_words(w1_sb, w1_words)
+        load_words(w3_sb, w3_words)
+        load_scales(w1_sc, w1_scales)
+        load_scales(w3_sc, w3_scales)
+        nc.sync.dma_start(pos1_sb[:], pos1)
+        nc.sync.dma_start(pos2_sb[:], pos2)
+        load_a1(2)
+
+        def by_quads(tile3):
+            return tile3.rearrange("p t (c i) -> p c t i", i=4)
+
+        def into_quads(tile2):
+            return tile2.rearrange("p (c i t) -> p c t i", i=4, t=W)
+
+        g_val, g_bf = {}, {}
+
+        def gather(pair):
+            g_val[pair] = flow.tile([P, W, 2 * C], F32, name="g_val", tag="g_val" if pair else "dx0", bufs=1)
+            cols = slice(pair * 2 * C, (pair + 1) * 2 * C)
+            lists = offs_sb[:, cols.start // 16 : cols.stop // 16]
+            for t in range(W):
+                nc.vector.tensor_tensor(g_val[pair][:, t, :], dy[t][:].indirect(lists), gate_sb[:, cols], MULT)
+
+        def round_g(pair):
+            g_bf[pair] = flow.tile([P, 2 * W * C], BF16, name="g_bf", tag="g_bf" if pair else "x", bufs=1, align_bytes=64)
+            for h in range(2):
+                nc.scalar.copy(
+                    into_quads(g_bf[pair][:, h * W * C : (h + 1) * W * C]),
+                    by_quads(g_val[pair][:, :, h * C : (h + 1) * C]),
+                )
+
+        def quantize(bf, tag, bufs=1):
+            width = bf.shape[1] // W
+            codes = flow.tile([P, width], U32, name=tag + "_codes", tag=tag + "_codes", bufs=bufs, align_bytes=64)
+            scales = flow.tile([P, width], U8, name=tag + "_scales", tag=tag + "_scales", bufs=bufs, align_bytes=64)
+            nc.vector.quantize_mx(out=codes[:].bitcast(E5M2X4), scales=scales[:], in_=bf[:])
+            return codes, scales
+
+        th, z = {}, {}
+
+        def acts(e):
+            z[e] = flow.tile([P, W, C], F32, name="z", tag="z")
+            nc.scalar.activation(z[e][:], a1_t[e][:], ACT.Silu, scale=-1.0)
+            nc.scalar.activation(z[e][:], z[e][:], ACT.Identity, bias=1.0, scale=-1.0)
+            th[e] = flow.tile([P, W, C], F32, name="th", tag="th")
+            nc.scalar.activation(th[e][:], a1_t[e][:], ACT.Tanh, scale=0.5)
+
+        x = {}
+
+        share = 240
+
+        def factors_gpsimd(e):
+            x[e] = flow.tile([P, W, C], F32, name="x", tag="x", bufs=1, align_bytes=64)
+            nc.gpsimd.tensor_tensor(x[e][:, :, :share], z[e][:, :, :share], a3_t[e][:, :, :share], MULT)
+
+        def factors_vector(e):
+            nc.vector.tensor_tensor(x[e][:, :, share:], z[e][:, :, share:], a3_t[e][:, :, share:], MULT)
+
+        dh, dr, da1, da3 = {}, {}, {}, {}
+
+        def first(e):
+            dh[e] = []
+            half = slice(e % 2 * C, (e % 2 + 1) * C)
+            for t in range(W):
+                dh_t = psum.tile([P, C], F32, name="dh", tag="dh", bufs=4)
+                dh[e].append(dh_t)
+                nc.tensor.matmul_mx(
+                    out=dh_t[:],
+                    lhsT=w2_sb[:, e, 2 * P * t : 2 * P * (t + 1)].bitcast(E2M1X4),
+                    lhsT_scale=w2_sc[:, e, P * t : P * (t + 1)],
+                    rhs=g_q[e // 2][0][:, half].bitcast(E5M2X4),
+                    rhs_scale=g_q[e // 2][1][:, half],
+                    start=True,
+                    stop=True,
+                )
+
+        def gated(e):
+            dr[e] = flow.tile([P, W, C], F32, name="dr", tag="dr", bufs=1, align_bytes=64)
+            for t in range(W):
+                nc.vector.scalar_tensor_tensor(dr[e][:, t, :], th[e][:, t, :], 1.0, dh[e][t][:], ADD, MULT)
+
+        def deltas(e):
+            da1[e] = flow.tile([P, W * C], BF16, name="da1", tag="da1", bufs=1, align_bytes=64)
+            nc.vector.tensor_tensor(into_quads(da1[e][:]), by_quads(dr[e][:]), by_quads(x[e][:]), MULT)
+            da3[e] = flow.tile([P, W * C], BF16, name="da3", tag="da3", bufs=1, align_bytes=64)
+            nc.vector.tensor_tensor(into_quads(da3[e][:]), by_quads(dr[e][:]), by_quads(a1_t[e][:]), MULT)
+
+        def second(e):
+            acc = []
+            for kt in range(KT):
+                acc_k = psum.tile([P, C], F32, name="acc", tag="acc", bufs=4)
+                acc.append(acc_k)
+            for i, (w, sc, q) in enumerate(((w1_sb, w1_sc, d1_q[e]), (w3_sb, w3_sc, d3_q[e]))):
+                for kt in range(KT):
+                    nc.tensor.matmul_mx(
+                        out=acc[kt][:],
+                        lhsT=w[:, e, 2 * P * kt : 2 * P * (kt + 1)].bitcast(E2M1X4),
+                        lhsT_scale=sc[:, e, P * kt : P * (kt + 1)],
+                        rhs=q[0][:].bitcast(E5M2X4),
+                        rhs_scale=q[1][:],
+                        start=i == 0,
+                        stop=i == 1,
+                    )
+            for kt in range(KT):
+                nc.scalar.activation(dx[kt][:, e * C : (e + 1) * C], acc[kt][:], ACT.Copy, scale=0.5)
+
+        g_q, d1_q, d3_q = {}, {}, {}
+
+        for e in range(0, E, 2):
+            nc.vector.tensor_copy(
+                w2_sb[:, e : e + 2].bitcast(U16).rearrange("p e (t m) -> p e t m", t=W),
+                w2_raw[:, e : e + 2].bitcast(U16).rearrange("p e (m t) -> p e t m", t=W),
+            )
+        acts(0)
+        gather(0)
+        round_g(0)
+        nc.vector.tensor_copy(
+            w2_sc[:].rearrange("p e (t m) -> p e t m", t=W),
+            w2_rawsc[:].rearrange("p e (m t) -> p e t m", t=W),
+        )
+        acts(1)
+        gather(1)
+        g_q[0] = quantize(g_bf[0], "g", 2)
+        first(0)
+        round_g(1)
+        factors_gpsimd(0)
+        factors_vector(0)
+        gated(0)
+        first(1)
+        dx = []
+        for kt in range(KT):
+            dx_t = flow.tile([P, S], F32, name=f"dx{kt}", tag=f"dx{kt}", bufs=1)
+            dx.append(dx_t)
+        for e in range(E):
+            if e + 2 < E:
+                load_a3(e + 2)
+                acts(e + 2)
+            if e + 3 < E:
+                load_a1(e + 3)
+            deltas(e)
+            if e + 1 < E:
+                factors_gpsimd(e + 1)
+                gated(e + 1)
+                factors_vector(e + 1)
+            if e == 0 or e == 2:
+                g_q[e // 2 + 1] = quantize(g_bf[e // 2 + 1], "g", 2)
+            if e + 2 < E:
+                first(e + 2)
+            d1_q[e] = quantize(da1[e], "d1")
+            d3_q[e] = quantize(da3[e], "d3")
+            second(e)
+            if e == 0:
+                gather(2)
+                round_g(2)
+
+        pieces = [(0, 0, T), (1, 0, T), (2, 0, 1024), (2, 1024, T)]
+        y = {}
+
+        def add(kt, c0, c1):
+            y1, y2 = y[kt]
+            adder = nc.vector if (kt, c0, c1) == pieces[-1] else nc.gpsimd
+            adder.tensor_tensor(y1[:, c0:c1], y1[:, c0:c1], y2[:, c0:c1], ADD)
+            nc.sync.dma_start(out=out[kt * P : (kt + 1) * P, c0:c1], in_=y1[:, c0:c1])
+
+        for i, (kt, c0, c1) in enumerate(pieces):
+            if c0 == 0:
+                y1 = flow.tile([P, T], F32, name="y1", tag="z")
+                y2 = flow.tile([P, T], F32, name="y2", tag="th")
+                y[kt] = y1, y2
+            nc.vector.tensor_copy(y1[:, c0:c1], dx[kt][:].indirect(pos1_sb[:, c0 // 16 : c1 // 16]))
+            if i:
+                add(*pieces[i - 1])
+            nc.vector.tensor_copy(y2[:, c0:c1], dx[kt][:].indirect(pos2_sb[:, c0 // 16 : c1 // 16]))
+        add(*pieces[-1])

@@ -1,6 +1,7 @@
 from contextlib import ExitStack
 
 import concourse.mybir as mybir
+from concourse.masks import make_identity
 
 K, T, E, C, H, N = 384, 1536, 6, 512, 512, 512
 S = E * C
@@ -18,13 +19,14 @@ E5M2X4 = mybir.dt.float8_e5m2_x4
 E2M1X4 = mybir.dt.float4_e2m1fn_x4
 
 ADD = mybir.AluOpType.add
-SUB = mybir.AluOpType.subtract
 MULT = mybir.AluOpType.mult
 ACT = mybir.ActivationFunctionType
 
 P = 128
 W = 4
 KT = K // P
+HALF = C // 2
+HALVES = 2 * E
 
 
 def tile_moe_bdx_glu_silu_kernel(
@@ -34,35 +36,28 @@ def tile_moe_bdx_glu_silu_kernel(
     with ExitStack() as ctx:
         keep = ctx.enter_context(tc.tile_pool(name="keep", bufs=1))
         flow = ctx.enter_context(tc.tile_pool(name="flow", bufs=2))
-        psum = ctx.enter_context(tc.psum_pool(name="psum", bufs=1))
+        psum = ctx.enter_context(tc.psum_pool(name="psum", bufs=2))
 
         offs_sb = keep.tile([P, S // 16], U16, name="offs_sb")
         pos1_sb = keep.tile([P, T // 16], U16, name="pos1_sb")
         pos2_sb = keep.tile([P, T // 16], U16, name="pos2_sb")
-        dy = []
-        for t in range(W):
-            dy_t = keep.tile([P, T], F32, name=f"dy{t}")
-            dy.append(dy_t)
-        gate_sb = keep.tile([P, S], F32, name="gate_sb")
+        dy = [flow.tile([P, T], F32, name=f"dy{t}", tag=f"dy{t}" if t else "dx2", bufs=1) for t in range(W)]
+        gate_sb = flow.tile([P, S], F32, name="gate_sb", tag="dx1", bufs=1)
         w2_sb = keep.tile([P, E, 2 * H], U8, name="w2_sb", align_bytes=64)
         w1_sb = keep.tile([P, E, 2 * K], U8, name="w1_sb", align_bytes=64)
         w3_sb = keep.tile([P, E, 2 * K], U8, name="w3_sb", align_bytes=64)
         w2_sc = keep.tile([P, E, H], U8, name="w2_sc", align_bytes=64)
         w1_sc = keep.tile([P, E, K], U8, name="w1_sc", align_bytes=64)
         w3_sc = keep.tile([P, E, K], U8, name="w3_sc", align_bytes=64)
-        w2_raw = flow.tile([P, E, 2 * H], U8, name="w2_raw", tag="dr", bufs=1, align_bytes=64)
-        w2_rawsc = flow.tile([P, E, H], U8, name="w2_rawsc", tag="da3", bufs=1, align_bytes=64)
+        ident = keep.tile([P, P], F32, name="ident")
 
-        warm = keep.tile([P, 1], F32, name="warm")
-        nc.vector.memset(warm[:], 0.0)
-        nc.scalar.activation(warm[:], warm[:], ACT.Silu)
-        nc.gpsimd.memset(w2_rawsc[:].rearrange("p e i -> p (e i)").bitcast(U32), 0)
-        nc.gpsimd.memset(w1_sc[:].rearrange("p e i -> p (e i)").bitcast(U32), 0)
-        nc.gpsimd.memset(w3_sc[:].rearrange("p e i -> p (e i)").bitcast(U32), 0)
+        for plane in (w2_sc, w1_sc, w3_sc):
+            nc.gpsimd.memset(plane[:].rearrange("p e i -> p (e i)").bitcast(U32), 0)
+        make_identity(nc, ident[:])
 
         dy_rows = dyT.rearrange("(p t) c -> t p c", t=W)
-        a1_rows = a1.rearrange("(p t) c -> p t c", t=W)
-        a3_rows = a3.rearrange("(p t) c -> p t c", t=W)
+        a1_rows = a1.rearrange("(j q) c -> q j c", q=P)
+        a3_rows = a3.rearrange("(j q) c -> q j c", q=P)
 
         def load_words(dst, words, e0=0, e1=E):
             nc.sync.dma_start(
@@ -76,36 +71,40 @@ def tile_moe_bdx_glu_silu_kernel(
 
         a1_t, a3_t = {}, {}
 
-        def load_a1(e):
-            a1_t[e] = flow.tile([P, W, C], F32, name="a1_sb", tag="a1", bufs=3)
-            nc.sync.dma_start(out=a1_t[e][:], in_=a1_rows[:, :, e * C : (e + 1) * C])
+        def load_a1(e, c0=0, c1=C):
+            if c0 == 0:
+                a1_t[e] = flow.tile([P, W, C], F32, name="a1_sb", tag="a1", bufs=3)
+            nc.sync.dma_start(out=a1_t[e][:, :, c0:c1], in_=a1_rows[:, :, e * C + c0 : e * C + c1])
 
-        def load_a3(e):
-            a3_t[e] = flow.tile([P, W, C], F32, name="a3_sb", tag="a3")
-            nc.sync.dma_start(out=a3_t[e][:], in_=a3_rows[:, :, e * C : (e + 1) * C])
+        def load_a3(e, c0=0, c1=C):
+            if c0 == 0:
+                a3_t[e] = flow.tile([P, W, C], F32, name="a3_sb", tag="a3")
+            nc.sync.dma_start(out=a3_t[e][:, :, c0:c1], in_=a3_rows[:, :, e * C + c0 : e * C + c1])
 
         def load_gate(c0, c1):
             nc.sync.dma_start(out=gate_sb[:, c0:c1], in_=gate[:P, c0:c1])
 
-        for e in range(0, E, 2):
-            load_words(w2_raw, w2_words, e, e + 2)
         nc.sync.dma_start(offs_sb[:], offs)
         load_gate(0, 2 * C)
         for t in range(W):
             nc.sync.dma_start(out=dy[t][:], in_=dy_rows[t])
-        load_a1(0)
-        load_scales(w2_rawsc, w2_scales)
-        load_gate(2 * C, S)
-        load_a3(0)
+            if t in (1, 2):
+                load_a1(0, (t - 1) * HALF, t * HALF)
+        load_a3(0, 0, HALF)
+        load_words(w2_sb, w2_words, 0, 2)
+        load_scales(w2_sc, w2_scales)
         load_a1(1)
+        load_a3(0, HALF, C)
+        load_gate(2 * C, S)
         load_a3(1)
+        load_a1(2)
+        load_words(w2_sb, w2_words, 2, E)
         load_words(w1_sb, w1_words)
         load_words(w3_sb, w3_words)
         load_scales(w1_sc, w1_scales)
         load_scales(w3_sc, w3_scales)
         nc.sync.dma_start(pos1_sb[:], pos1)
         nc.sync.dma_start(pos2_sb[:], pos2)
-        load_a1(2)
 
         def by_quads(tile3):
             return tile3.rearrange("p t (c i) -> p c t i", i=4)
@@ -113,163 +112,204 @@ def tile_moe_bdx_glu_silu_kernel(
         def into_quads(tile2):
             return tile2.rearrange("p (c i t) -> p c t i", i=4, t=W)
 
-        g_val, g_bf = {}, {}
+        g_val, g_bf, g_q = {}, {}, {}
 
-        def gather(pair):
-            g_val[pair] = flow.tile([P, W, 2 * C], F32, name="g_val", tag="g_val" if pair else "dx0", bufs=1)
-            cols = slice(pair * 2 * C, (pair + 1) * 2 * C)
-            lists = offs_sb[:, cols.start // 16 : cols.stop // 16]
-            for t in range(W):
-                nc.vector.tensor_tensor(g_val[pair][:, t, :], dy[t][:].indirect(lists), gate_sb[:, cols], MULT)
+        def gather(dst, t, c0, c1):
+            nc.vector.tensor_tensor(dst, dy[t][:].indirect(offs_sb[:, c0 // 16 : c1 // 16]), gate_sb[:, c0:c1], MULT)
 
-        def round_g(pair):
-            g_bf[pair] = flow.tile([P, 2 * W * C], BF16, name="g_bf", tag="g_bf" if pair else "x", bufs=1, align_bytes=64)
-            for h in range(2):
-                nc.scalar.copy(
-                    into_quads(g_bf[pair][:, h * W * C : (h + 1) * W * C]),
-                    by_quads(g_val[pair][:, :, h * C : (h + 1) * C]),
-                )
+        def round_g(e):
+            g_bf[e] = flow.tile([P, W * C], BF16, name="g_bf", tag="g_bf", align_bytes=64)
+            nc.scalar.copy(into_quads(g_bf[e][:]), by_quads(g_val[e]))
 
-        def quantize(bf, tag, bufs=1):
+        def quantize(bf, tag, bufs):
             width = bf.shape[1] // W
             codes = flow.tile([P, width], U32, name=tag + "_codes", tag=tag + "_codes", bufs=bufs, align_bytes=64)
             scales = flow.tile([P, width], U8, name=tag + "_scales", tag=tag + "_scales", bufs=bufs, align_bytes=64)
-            nc.vector.quantize_mx(out=codes[:].bitcast(E5M2X4), scales=scales[:], in_=bf[:])
+            nc.vector.quantize_mx(out=codes[:].bitcast(E5M2X4), scales=scales[:], in_=bf)
             return codes, scales
 
-        th, z = {}, {}
+        def half_of(tile3, h):
+            return tile3[:, :, h % 2 * HALF : (h % 2 + 1) * HALF].rearrange("q j (b c) -> q b j c", b=2)
 
-        def acts(e):
-            z[e] = flow.tile([P, W, C], F32, name="z", tag="z")
-            nc.scalar.activation(z[e][:], a1_t[e][:], ACT.Silu, scale=-1.0)
-            nc.scalar.activation(z[e][:], z[e][:], ACT.Identity, bias=1.0, scale=-1.0)
-            th[e] = flow.tile([P, W, C], F32, name="th", tag="th")
-            nc.scalar.activation(th[e][:], a1_t[e][:], ACT.Tanh, scale=0.5)
+        z, x, a1_ps, x_ps, dh, th, dr, da, dq, d_q = {}, {}, {}, {}, {}, {}, {}, {}, {}, {}
 
-        x = {}
+        def make_z(h):
+            z[h] = flow.tile([P, 2, W, P], F32, name="z", tag="z", bufs=5)
+            nc.scalar.activation(z[h][:], half_of(a1_t[h // 2], h), ACT.Silu, scale=-1.0)
+            nc.scalar.activation(z[h][:], z[h][:], ACT.Identity, bias=1.0, scale=-1.0)
 
-        share = 240
+        def new_x(h):
+            x[h] = flow.tile([P, 2, W, P], F32, name="x", tag="x")
 
-        def factors_gpsimd(e):
-            x[e] = flow.tile([P, W, C], F32, name="x", tag="x", bufs=1, align_bytes=64)
-            nc.gpsimd.tensor_tensor(x[e][:, :, :share], z[e][:, :, :share], a3_t[e][:, :, :share], MULT)
+        def make_x(h, engine):
+            engine.tensor_tensor(x[h][:], z[h][:], half_of(a3_t[h // 2], h), MULT)
 
-        def factors_vector(e):
-            nc.vector.tensor_tensor(x[e][:, :, share:], z[e][:, :, share:], a3_t[e][:, :, share:], MULT)
+        def turn(src, tag):
+            bank = psum.tile([P, H], F32, name=tag, tag=tag)
+            for j in range(W):
+                nc.tensor.transpose(bank[:, j * P : (j + 1) * P], src[:, j, :], ident[:])
+            return bank
 
-        dh, dr, da1, da3 = {}, {}, {}, {}
+        def turn_a1(h, b):
+            a1_ps[h, b] = turn(half_of(a1_t[h // 2], h)[:, b], "a1_ps")
 
-        def first(e):
-            dh[e] = []
-            half = slice(e % 2 * C, (e % 2 + 1) * C)
-            for t in range(W):
-                dh_t = psum.tile([P, C], F32, name="dh", tag="dh", bufs=4)
-                dh[e].append(dh_t)
-                nc.tensor.matmul_mx(
-                    out=dh_t[:],
-                    lhsT=w2_sb[:, e, 2 * P * t : 2 * P * (t + 1)].bitcast(E2M1X4),
-                    lhsT_scale=w2_sc[:, e, P * t : P * (t + 1)],
-                    rhs=g_q[e // 2][0][:, half].bitcast(E5M2X4),
-                    rhs_scale=g_q[e // 2][1][:, half],
-                    start=True,
-                    stop=True,
+        def turn_x(h, b):
+            x_ps[h, b] = turn(x[h][:, b], "x_ps")
+
+        def make_th(h, b):
+            if b == 0 and h + 1 < HALVES:
+                new_x(h + 1)
+                th[h, b] = x[h + 1][:, 0].rearrange("q j c -> q (j c)")
+            else:
+                th[h, b] = flow.tile([P, H], F32, name="th", tag="th", bufs=1)[:]
+            nc.scalar.activation(th[h, b], a1_ps[h, b][:], ACT.Tanh, scale=0.5)
+
+        def first(h, b):
+            e = h // 2
+            cols = slice((h % 2 * 2 + b) * P, (h % 2 * 2 + b + 1) * P)
+            dh[h, b] = psum.tile([P, H], F32, name="dh", tag="dh")
+            nc.tensor.matmul_mx(
+                out=dh[h, b][:],
+                lhsT=g_q[e][0][:, cols].bitcast(E5M2X4),
+                lhsT_scale=g_q[e][1][:, cols],
+                rhs=w2_sb[:, e].bitcast(E2M1X4),
+                rhs_scale=w2_sc[:, e],
+                start=True,
+                stop=True,
+            )
+
+        def by_pairs(ap):
+            return ap.rearrange("s (m u r) -> s u m r", u=2, r=2)
+
+        def gated(h, b, dst):
+            dr[h, b] = dst
+            nc.vector.scalar_tensor_tensor(dst, th[h, b], 1.0, dh[h, b][:], ADD, MULT)
+
+        def deltas(h, b):
+            da[h, b] = flow.tile([P, 2, H], BF16, name="da", tag="da", bufs=4)
+            for i, bank in ((1, a1_ps[h, b]), (0, x_ps[h, b])):
+                nc.vector.tensor_tensor(
+                    da[h, b][:, i].rearrange("s (u m r) -> s u m r", u=2, r=2),
+                    by_pairs(dr[h, b]),
+                    by_pairs(bank[:]),
+                    MULT,
                 )
 
-        def gated(e):
-            dr[e] = flow.tile([P, W, C], F32, name="dr", tag="dr", bufs=1, align_bytes=64)
-            for t in range(W):
-                nc.vector.scalar_tensor_tensor(dr[e][:, t, :], th[e][:, t, :], 1.0, dh[e][t][:], ADD, MULT)
+        def turn_back(h, b):
+            e = h // 2
+            if h % 2 == 0 and b == 0:
+                dq[e] = flow.tile([P, 2, C, 2], F32, name="dq", tag="dq", align_bytes=64)
+            words = da[h, b][:].rearrange("s i k -> s (i k)").bitcast(F32)
+            bank = psum.tile([P, W * P], F32, name="back", tag="drain")
+            for j in range(W):
+                nc.tensor.transpose(bank[:, j * P : (j + 1) * P], words[:, j * P : (j + 1) * P], ident[:])
+            c0 = (h % 2 * 2 + b) * P
+            nc.scalar.copy(dq[e][:, :, c0 : c0 + P, :], bank[:].rearrange("p (i u s) -> p i s u", i=2, u=2))
 
-        def deltas(e):
-            da1[e] = flow.tile([P, W * C], BF16, name="da1", tag="da1", bufs=1, align_bytes=64)
-            nc.vector.tensor_tensor(into_quads(da1[e][:]), by_quads(dr[e][:]), by_quads(x[e][:]), MULT)
-            da3[e] = flow.tile([P, W * C], BF16, name="da3", tag="da3", bufs=1, align_bytes=64)
-            nc.vector.tensor_tensor(into_quads(da3[e][:]), by_quads(dr[e][:]), by_quads(a1_t[e][:]), MULT)
+        def quantize_d(e):
+            d_q[e] = quantize(dq[e][:].rearrange("p i c u -> p (i c u)").bitcast(BF16), "d", E)
 
-        def second(e):
-            acc = []
-            for kt in range(KT):
-                acc_k = psum.tile([P, C], F32, name="acc", tag="acc", bufs=4)
-                acc.append(acc_k)
-            for i, (w, sc, q) in enumerate(((w1_sb, w1_sc, d1_q[e]), (w3_sb, w3_sc, d3_q[e]))):
-                for kt in range(KT):
-                    nc.tensor.matmul_mx(
-                        out=acc[kt][:],
-                        lhsT=w[:, e, 2 * P * kt : 2 * P * (kt + 1)].bitcast(E2M1X4),
-                        lhsT_scale=sc[:, e, P * kt : P * (kt + 1)],
-                        rhs=q[0][:].bitcast(E5M2X4),
-                        rhs_scale=q[1][:],
-                        start=i == 0,
-                        stop=i == 1,
-                    )
-            for kt in range(KT):
-                nc.scalar.activation(dx[kt][:, e * C : (e + 1) * C], acc[kt][:], ACT.Copy, scale=0.5)
+        def second(e, kt):
+            acc = psum.tile([P, C], F32, name="acc", tag="drain")
+            for i, (w, sc) in enumerate(((w1_sb, w1_sc), (w3_sb, w3_sc))):
+                nc.tensor.matmul_mx(
+                    out=acc[:],
+                    lhsT=w[:, e, 2 * P * kt : 2 * P * (kt + 1)].bitcast(E2M1X4),
+                    lhsT_scale=sc[:, e, P * kt : P * (kt + 1)],
+                    rhs=d_q[e][0][:, i * C : (i + 1) * C].bitcast(E5M2X4),
+                    rhs_scale=d_q[e][1][:, i * C : (i + 1) * C],
+                    start=i == 0,
+                    stop=i == 1,
+                )
+            nc.scalar.activation(dx[kt][:, e * C : (e + 1) * C], acc[:], ACT.Copy, scale=0.5)
 
-        g_q, d1_q, d3_q = {}, {}, {}
+        def prepare(h):
+            for b in range(2):
+                turn_a1(h, b)
+                make_th(h, b)
+            for b in range(2):
+                first(h, b)
+            for b in range(2):
+                turn_x(h, b)
 
-        for e in range(0, E, 2):
-            nc.vector.tensor_copy(
-                w2_sb[:, e : e + 2].bitcast(U16).rearrange("p e (t m) -> p e t m", t=W),
-                w2_raw[:, e : e + 2].bitcast(U16).rearrange("p e (m t) -> p e t m", t=W),
-            )
-        acts(0)
-        gather(0)
+        g_pair = flow.tile([P, W, 2 * C], F32, name="g_pair", tag="dx0", bufs=1)
+        g_val[0], g_val[1] = g_pair[:, :, :C], g_pair[:, :, C:]
+        for t in range(W - 1):
+            gather(g_pair[:, t, :], t, 0, 2 * C)
+        make_z(0)
+        for b in range(2):
+            turn_a1(0, b)
+            make_th(0, b)
+        make_z(1)
+        gather(g_pair[:, W - 1, :C], W - 1, 0, C)
         round_g(0)
-        nc.vector.tensor_copy(
-            w2_sc[:].rearrange("p e (t m) -> p e t m", t=W),
-            w2_rawsc[:].rearrange("p e (m t) -> p e t m", t=W),
-        )
-        acts(1)
-        gather(1)
-        g_q[0] = quantize(g_bf[0], "g", 2)
-        first(0)
+        gather(g_pair[:, W - 1, C:], W - 1, C, 2 * C)
+        new_x(0)
+        make_x(0, nc.vector)
+        g_q[0] = quantize(g_bf[0][:], "g", 2)
+        for b in range(2):
+            first(0, b)
+        for b in range(2):
+            turn_x(0, b)
         round_g(1)
-        factors_gpsimd(0)
-        factors_vector(0)
-        gated(0)
-        first(1)
-        dx = []
-        for kt in range(KT):
-            dx_t = flow.tile([P, S], F32, name=f"dx{kt}", tag=f"dx{kt}", bufs=1)
-            dx.append(dx_t)
-        for e in range(E):
+        for h in range(2, 4):
+            make_z(h)
+        dx = [flow.tile([P, S], F32, name=f"dx{kt}", tag=f"dx{kt}", bufs=1) for kt in range(KT)]
+
+        for h in range(HALVES):
+            e = h // 2
+            ahead = h + 1 < HALVES
+            if h % 2 == 0:
+                g_next = flow.tile([P, W, C], F32, name="g_val", tag="g_val")
+                g_val[e + 2] = g_next[:]
+                if e + 2 < E:
+                    load_a3(e + 2)
+                if e + 3 < E:
+                    load_a1(e + 3)
+            t0 = h % 2 * 2
+            gated(h, 0, g_next[:, t0 + 1, :])
+            gated(h, 1, g_next[:, t0, :])
+            if ahead:
+                make_x(h + 1, nc.gpsimd)
+                for b in range(2):
+                    first(h + 1, b)
+            if h % 2 and e:
+                second(e - 1, 0)
+            if h + 4 < HALVES:
+                make_z(h + 4)
+            for b in range(2):
+                deltas(h, b)
+            for b in range(2):
+                if ahead:
+                    turn_a1(h + 1, b)
+                    make_th(h + 1, b)
+                turn_back(h, b)
+            if ahead:
+                for b in range(2):
+                    turn_x(h + 1, b)
             if e + 2 < E:
-                load_a3(e + 2)
-                acts(e + 2)
-            if e + 3 < E:
-                load_a1(e + 3)
-            deltas(e)
-            if e + 1 < E:
-                factors_gpsimd(e + 1)
-                gated(e + 1)
-                factors_vector(e + 1)
-            if e == 0 or e == 2:
-                g_q[e // 2 + 1] = quantize(g_bf[e // 2 + 1], "g", 2)
-            if e + 2 < E:
-                first(e + 2)
-            d1_q[e] = quantize(da1[e], "d1")
-            d3_q[e] = quantize(da3[e], "d3")
-            second(e)
-            if e == 0:
-                gather(2)
-                round_g(2)
+                for t in (t0, t0 + 1):
+                    gather(g_next[:, t, :], t, (e + 2) * C, (e + 3) * C)
+                if h % 2:
+                    round_g(e + 2)
+            if h % 2 == 0:
+                if e + 1 < E:
+                    g_q[e + 1] = quantize(g_bf[e + 1][:], "g", 2)
+                if e:
+                    quantize_d(e - 1)
+        quantize_d(E - 1)
+        second(E - 1, 0)
+        for kt in range(1, KT):
+            for e in range(E):
+                second(e, kt)
 
         pieces = [(0, 0, T), (1, 0, T), (2, 0, 1024), (2, 1024, T)]
-        y = {}
-
-        def add(kt, c0, c1):
-            y1, y2 = y[kt]
-            adder = nc.vector if (kt, c0, c1) == pieces[-1] else nc.gpsimd
-            adder.tensor_tensor(y1[:, c0:c1], y1[:, c0:c1], y2[:, c0:c1], ADD)
-            nc.sync.dma_start(out=out[kt * P : (kt + 1) * P, c0:c1], in_=y1[:, c0:c1])
-
-        for i, (kt, c0, c1) in enumerate(pieces):
+        for kt, c0, c1 in pieces:
             if c0 == 0:
-                y1 = flow.tile([P, T], F32, name="y1", tag="z")
-                y2 = flow.tile([P, T], F32, name="y2", tag="th")
-                y[kt] = y1, y2
-            nc.vector.tensor_copy(y1[:, c0:c1], dx[kt][:].indirect(pos1_sb[:, c0 // 16 : c1 // 16]))
-            if i:
-                add(*pieces[i - 1])
-            nc.vector.tensor_copy(y2[:, c0:c1], dx[kt][:].indirect(pos2_sb[:, c0 // 16 : c1 // 16]))
-        add(*pieces[-1])
+                y1 = flow.tile([P, T], F32, name="y1", tag="a3")
+                y2 = flow.tile([P, T], F32, name="y2", tag="a1", bufs=3)
+                nc.vector.tensor_copy(y1[:], dx[kt][:].indirect(pos1_sb[:]))
+            nc.vector.tensor_tensor(
+                y2[:, c0:c1], dx[kt][:].indirect(pos2_sb[:, c0 // 16 : c1 // 16]), y1[:, c0:c1], ADD
+            )
+            nc.sync.dma_start(out=out[kt * P : (kt + 1) * P, c0:c1], in_=y2[:, c0:c1])

@@ -42,7 +42,12 @@ def tile_moe_bdx_glu_silu_kernel(
         pos1_sb = keep.tile([P, T // 16], U16, name="pos1_sb")
         pos2_sb = keep.tile([P, T // 16], U16, name="pos2_sb")
         dy = [flow.tile([P, T], F32, name=f"dy{t}", tag=f"dy{t}" if t else "dx2", bufs=1) for t in range(W)]
-        gate_sb = flow.tile([P, S], F32, name="gate_sb", tag="dx1", bufs=1)
+        gate_sb = flow.tile([P, S - C], F32, name="gate_sb", tag="dx1", bufs=1)
+        g_first = [
+            flow.tile([P, W * HALF], BF16, name="g_first", tag=tag, bufs=bufs, align_bytes=64)
+            for tag, bufs in (("g1_codes", 1), ("dq", 2))
+        ]
+        gate_2 = flow.tile([P, C], F32, name="gate_2", tag="dq", bufs=2, align_bytes=64)
         w2_sb = keep.tile([P, E, 2 * H], U8, name="w2_sb", align_bytes=64)
         w1_sb = keep.tile([P, E, 2 * K], U8, name="w1_sb", align_bytes=64)
         w3_sb = keep.tile([P, E, 2 * K], U8, name="w3_sb", align_bytes=64)
@@ -81,8 +86,13 @@ def tile_moe_bdx_glu_silu_kernel(
                 a3_t[e] = flow.tile([P, W, C], F32, name="a3_sb", tag="a3")
             nc.sync.dma_start(out=a3_t[e][:, :, c0:c1], in_=a3_rows[:, :, e * C + c0 : e * C + c1])
 
+        def gate_cols(c0, c1):
+            if c0 < 2 * C:
+                return gate_sb[:, c0:c1]
+            return gate_2[:] if c0 == 2 * C else gate_sb[:, c0 - C : c1 - C]
+
         def load_gate(c0, c1):
-            nc.sync.dma_start(out=gate_sb[:, c0:c1], in_=gate[:P, c0:c1])
+            nc.sync.dma_start(out=gate_cols(c0, c1), in_=gate[:P, c0:c1])
 
         nc.sync.dma_start(offs_sb[:], offs)
         load_gate(0, 2 * C)
@@ -95,9 +105,10 @@ def tile_moe_bdx_glu_silu_kernel(
         load_scales(w2_sc, w2_scales)
         load_a1(1)
         load_a3(0, HALF, C)
-        load_gate(2 * C, S)
+        load_gate(2 * C, 3 * C)
         load_a3(1)
         load_a1(2)
+        load_gate(3 * C, S)
         load_words(w2_sb, w2_words, 2, E)
         load_words(w1_sb, w1_words)
         load_words(w3_sb, w3_words)
@@ -115,18 +126,26 @@ def tile_moe_bdx_glu_silu_kernel(
         g_val, g_bf, g_q = {}, {}, {}
 
         def gather(dst, t, c0, c1):
-            nc.vector.tensor_tensor(dst, dy[t][:].indirect(offs_sb[:, c0 // 16 : c1 // 16]), gate_sb[:, c0:c1], MULT)
+            nc.vector.tensor_tensor(dst, dy[t][:].indirect(offs_sb[:, c0 // 16 : c1 // 16]), gate_cols(c0, c1), MULT)
+
+        def round_into(dst, src):
+            nc.scalar.copy(into_quads(dst), by_quads(src))
 
         def round_g(e):
-            g_bf[e] = flow.tile([P, W * C], BF16, name="g_bf", tag="g_bf", align_bytes=64)
-            nc.scalar.copy(into_quads(g_bf[e][:]), by_quads(g_val[e]))
+            g_bf[e] = flow.tile([P, W * C], BF16, name="g_bf", tag="g_bf", bufs=1, align_bytes=64)
+            round_into(g_bf[e][:], g_val[e])
 
-        def quantize(bf, tag, bufs):
-            width = bf.shape[1] // W
-            codes = flow.tile([P, width], U32, name=tag + "_codes", tag=tag + "_codes", bufs=bufs, align_bytes=64)
-            scales = flow.tile([P, width], U8, name=tag + "_scales", tag=tag + "_scales", bufs=bufs, align_bytes=64)
-            nc.vector.quantize_mx(out=codes[:].bitcast(E5M2X4), scales=scales[:], in_=bf)
+        def new_codes(width, tag):
+            codes = flow.tile([P, width], U32, name=tag + "_codes", tag=tag + "_codes", bufs=1, align_bytes=64)
+            scales = flow.tile([P, width], U8, name=tag + "_scales", tag=tag + "_scales", bufs=1, align_bytes=64)
             return codes, scales
+
+        def quantize(q, bf, c0, c1):
+            nc.vector.quantize_mx(out=q[0][:, c0:c1].bitcast(E5M2X4), scales=q[1][:, c0:c1], in_=bf)
+
+        def quantize_g(e):
+            g_q[e] = new_codes(C, f"g{e % 2}")
+            quantize(g_q[e], g_bf[e][:], 0, C)
 
         def half_of(tile3, h):
             return tile3[:, :, h % 2 * HALF : (h % 2 + 1) * HALF].rearrange("q j (b c) -> q b j c", b=2)
@@ -134,15 +153,23 @@ def tile_moe_bdx_glu_silu_kernel(
         z, x, a1_ps, x_ps, dh, th, dr, da, dq, d_q = {}, {}, {}, {}, {}, {}, {}, {}, {}, {}
 
         def make_z(h):
-            z[h] = flow.tile([P, 2, W, P], F32, name="z", tag="z", bufs=5)
+            z[h] = flow.tile([P, 2, W, P], F32, name="z", tag="z", bufs=2)
             nc.scalar.activation(z[h][:], half_of(a1_t[h // 2], h), ACT.Silu, scale=-1.0)
+
+        def end_z(h):
             nc.scalar.activation(z[h][:], z[h][:], ACT.Identity, bias=1.0, scale=-1.0)
 
-        def new_x(h):
-            x[h] = flow.tile([P, 2, W, P], F32, name="x", tag="x")
+        def new_dq(e):
+            dq[e] = flow.tile([P, 2, C, 2], F32, name="dq", tag="dq", bufs=2, align_bytes=64)
 
         def make_x(h, engine):
-            engine.tensor_tensor(x[h][:], z[h][:], half_of(a3_t[h // 2], h), MULT)
+            if h % 2:
+                new_dq(h // 2)
+                x[h] = dq[h // 2][:, :, HALF:, :].rearrange("q b (j c) u -> q b j (c u)", j=W)
+            else:
+                tag = "g_bf" if h else "g1_codes"
+                x[h] = flow.tile([P, 2, W, P], F32, name="x", tag=tag, bufs=1, align_bytes=64)[:]
+            engine.tensor_tensor(x[h], z[h][:], half_of(a3_t[h // 2], h), MULT)
 
         def turn(src, tag):
             bank = psum.tile([P, H], F32, name=tag, tag=tag)
@@ -157,11 +184,7 @@ def tile_moe_bdx_glu_silu_kernel(
             x_ps[h, b] = turn(x[h][:, b], "x_ps")
 
         def make_th(h, b):
-            if b == 0 and h + 1 < HALVES:
-                new_x(h + 1)
-                th[h, b] = x[h + 1][:, 0].rearrange("q j c -> q (j c)")
-            else:
-                th[h, b] = flow.tile([P, H], F32, name="th", tag="th", bufs=1)[:]
+            th[h, b] = flow.tile([P, H], F32, name="th", tag=f"th{b}", bufs=1 + b)[:]
             nc.scalar.activation(th[h, b], a1_ps[h, b][:], ACT.Tanh, scale=0.5)
 
         def first(h, b):
@@ -185,52 +208,47 @@ def tile_moe_bdx_glu_silu_kernel(
             dr[h, b] = dst
             nc.vector.scalar_tensor_tensor(dst, th[h, b], 1.0, dh[h, b][:], ADD, MULT)
 
-        def deltas(h, b):
-            da[h, b] = flow.tile([P, 2, H], BF16, name="da", tag="da", bufs=4)
-            for i, bank in ((1, a1_ps[h, b]), (0, x_ps[h, b])):
-                nc.vector.tensor_tensor(
-                    da[h, b][:, i].rearrange("s (u m r) -> s u m r", u=2, r=2),
-                    by_pairs(dr[h, b]),
-                    by_pairs(bank[:]),
-                    MULT,
-                )
+        def new_da(h, b, tag="da", bufs=3):
+            both = flow.tile([P, 2, H], BF16, name="da", tag=tag, bufs=bufs, align_bytes=64)
+            da[h, b] = [both[:, 0] if b else th[h, 1].bitcast(BF16)[:, :H], both[:, 1]]
 
-        def turn_back(h, b):
+        def delta(h, b, i):
+            nc.vector.tensor_tensor(
+                da[h, b][i].rearrange("s (u m r) -> s u m r", u=2, r=2),
+                by_pairs(dr[h, b]),
+                by_pairs((x_ps, a1_ps)[i][h, b][:]),
+                MULT,
+            )
+
+        def turn_back(h, b, i0=0, i1=2, tag="drain"):
             e = h // 2
-            if h % 2 == 0 and b == 0:
-                dq[e] = flow.tile([P, 2, C, 2], F32, name="dq", tag="dq", align_bytes=64)
-            words = da[h, b][:].rearrange("s i k -> s (i k)").bitcast(F32)
-            bank = psum.tile([P, W * P], F32, name="back", tag="drain")
-            for j in range(W):
-                nc.tensor.transpose(bank[:, j * P : (j + 1) * P], words[:, j * P : (j + 1) * P], ident[:])
+            bank = psum.tile([P, W * P], F32, name="back", tag=tag)
+            for j in range(2 * i0, 2 * i1):
+                words = da[h, b][j // 2].bitcast(F32)
+                nc.tensor.transpose(bank[:, j * P : (j + 1) * P], words[:, j % 2 * P : (j % 2 + 1) * P], ident[:])
             c0 = (h % 2 * 2 + b) * P
-            nc.scalar.copy(dq[e][:, :, c0 : c0 + P, :], bank[:].rearrange("p (i u s) -> p i s u", i=2, u=2))
+            nc.scalar.copy(
+                dq[e][:, i0:i1, c0 : c0 + P, :], bank[:].rearrange("p (i u s) -> p i s u", i=2, u=2)[:, i0:i1]
+            )
 
-        def quantize_d(e):
-            d_q[e] = quantize(dq[e][:].rearrange("p i c u -> p (i c u)").bitcast(BF16), "d", E)
+        def quantize_d(e, c0=0, c1=2 * C):
+            if e not in d_q:
+                d_q[e] = new_codes(2 * C, f"d{e}")
+            quantize(d_q[e], dq[e][:].rearrange("p i c u -> p (i c u)").bitcast(BF16)[:, W * c0 : W * c1], c0, c1)
 
-        def second(e, kt):
-            acc = psum.tile([P, C], F32, name="acc", tag="drain")
-            for i, (w, sc) in enumerate(((w1_sb, w1_sc), (w3_sb, w3_sc))):
+        def second(e, kt, tag="drain"):
+            acc = psum.tile([P, C], F32, name="acc", tag=tag)
+            for i, w, sc in ((1, w3_sb, w3_sc), (0, w1_sb, w1_sc)):
                 nc.tensor.matmul_mx(
                     out=acc[:],
                     lhsT=w[:, e, 2 * P * kt : 2 * P * (kt + 1)].bitcast(E2M1X4),
                     lhsT_scale=sc[:, e, P * kt : P * (kt + 1)],
                     rhs=d_q[e][0][:, i * C : (i + 1) * C].bitcast(E5M2X4),
                     rhs_scale=d_q[e][1][:, i * C : (i + 1) * C],
-                    start=i == 0,
-                    stop=i == 1,
+                    start=i == 1,
+                    stop=i == 0,
                 )
             nc.scalar.activation(dx[kt][:, e * C : (e + 1) * C], acc[:], ACT.Copy, scale=0.5)
-
-        def prepare(h):
-            for b in range(2):
-                turn_a1(h, b)
-                make_th(h, b)
-            for b in range(2):
-                first(h, b)
-            for b in range(2):
-                turn_x(h, b)
 
         g_pair = flow.tile([P, W, 2 * C], F32, name="g_pair", tag="dx0", bufs=1)
         g_val[0], g_val[1] = g_pair[:, :, :C], g_pair[:, :, C:]
@@ -240,67 +258,96 @@ def tile_moe_bdx_glu_silu_kernel(
         for b in range(2):
             turn_a1(0, b)
             make_th(0, b)
+        end_z(0)
         make_z(1)
         gather(g_pair[:, W - 1, :C], W - 1, 0, C)
-        round_g(0)
+        round_into(g_first[0][:], g_val[0][:, :, :HALF])
+        end_z(1)
+        round_into(g_first[1][:], g_val[0][:, :, HALF:])
         gather(g_pair[:, W - 1, C:], W - 1, C, 2 * C)
-        new_x(0)
+        g_q[0] = new_codes(C, "g0")
+        quantize(g_q[0], g_first[0][:], 0, HALF)
         make_x(0, nc.vector)
-        g_q[0] = quantize(g_bf[0][:], "g", 2)
         for b in range(2):
             first(0, b)
+        quantize(g_q[0], g_first[1][:], HALF, C)
         for b in range(2):
             turn_x(0, b)
         round_g(1)
-        for h in range(2, 4):
+        for h in range(3, 2):
             make_z(h)
+            end_z(h)
         dx = [flow.tile([P, S], F32, name=f"dx{kt}", tag=f"dx{kt}", bufs=1) for kt in range(KT)]
 
         for h in range(HALVES):
             e = h // 2
             ahead = h + 1 < HALVES
-            if h % 2 == 0:
+            gathers = e + 2 < E
+            held = f"g{(e + 1) % 2}_codes" if h % 2 == 0 and e + 1 < E else f"d{max(e - 1, 0)}_codes"
+            if h % 2 == 0 and gathers:
                 g_next = flow.tile([P, W, C], F32, name="g_val", tag="g_val")
                 g_val[e + 2] = g_next[:]
-                if e + 2 < E:
-                    load_a3(e + 2)
+                load_a3(e + 2)
                 if e + 3 < E:
                     load_a1(e + 3)
             t0 = h % 2 * 2
-            gated(h, 0, g_next[:, t0 + 1, :])
-            gated(h, 1, g_next[:, t0, :])
             if ahead:
                 make_x(h + 1, nc.gpsimd)
+            if gathers:
+                gated(h, 0, g_next[:].rearrange("p t c -> p (t c)")[:, t0 * C + HALF : (t0 + 1) * C + HALF])
+            elif ahead:
+                gated(h, 0, flow.tile([P, H], F32, name="dr_a", tag=held, bufs=1, align_bytes=64)[:])
+            else:
+                gated(h, 0, flow.tile([P, H], F32, name="dr_a", tag="z", bufs=2)[:])
+            gated(h, 1, flow.tile([P, H], F32, name="dr_b", tag="dr_b", bufs=1)[:])
+            if ahead:
                 for b in range(2):
                     first(h + 1, b)
-            if h % 2 and e:
+            if h % 2 == 0 and e > 1:
+                second(e - 2, 0)
+            if h + 1 == HALVES:
                 second(e - 1, 0)
-            if h + 4 < HALVES:
-                make_z(h + 4)
-            for b in range(2):
-                deltas(h, b)
-            for b in range(2):
-                if ahead:
+            if h + 2 < HALVES:
+                make_z(h + 2)
+                end_z(h + 2)
+            new_da(h, 0)
+            if gathers and h != 1:
+                new_da(h, 1, held, 1)
+            else:
+                new_da(h, 1)
+            for i in (1, 0):
+                for b in range(2):
+                    delta(h, b, i)
+            if ahead:
+                for b in range(2):
                     turn_a1(h + 1, b)
                     make_th(h + 1, b)
-                turn_back(h, b)
+            if ahead:
+                for b in range(2):
+                    turn_back(h, b)
+            else:
+                for i in (1, 0):
+                    for b in range(2):
+                        turn_back(h, b, i, i + 1, ("drain", "dh")[i])
             if ahead:
                 for b in range(2):
                     turn_x(h + 1, b)
-            if e + 2 < E:
+            if gathers:
                 for t in (t0, t0 + 1):
                     gather(g_next[:, t, :], t, (e + 2) * C, (e + 3) * C)
                 if h % 2:
                     round_g(e + 2)
-            if h % 2 == 0:
-                if e + 1 < E:
-                    g_q[e + 1] = quantize(g_bf[e + 1][:], "g", 2)
-                if e:
-                    quantize_d(e - 1)
-        quantize_d(E - 1)
-        second(E - 1, 0)
+            if h % 2 == 0 and e + 1 < E:
+                quantize_g(e + 1)
+            elif e and ahead:
+                quantize_d(e - 1)
+        for c0, c1 in ((C, 2 * C), (0, HALF), (HALF, HALF + P), (HALF + P, C)):
+            quantize_d(E - 1, c0, c1)
+        second(E - 1, 0, "a1_ps")
         for kt in range(1, KT):
-            for e in range(E):
+            second(E - 1, kt)
+        for kt in range(1, KT):
+            for e in range(E - 1):
                 second(e, kt)
 
         pieces = [(0, 0, T), (1, 0, T), (2, 0, 1024), (2, 1024, T)]

@@ -35,19 +35,16 @@ def tile_moe_bdx_glu_silu_kernel(
     nc = tc.nc
     with ExitStack() as ctx:
         keep = ctx.enter_context(tc.tile_pool(name="keep", bufs=1))
-        flow = ctx.enter_context(tc.tile_pool(name="flow", bufs=2))
+        flow = ctx.enter_context(tc.tile_pool(name="flow", bufs=1))
         psum = ctx.enter_context(tc.psum_pool(name="psum", bufs=2))
+
+        def sbuf(shape, dtype, tag, bufs=1):
+            return flow.tile(shape, dtype, name=tag, tag=tag, bufs=bufs, align_bytes=64)[:]
 
         offs_sb = keep.tile([P, S // 16], U16, name="offs_sb")
         pos1_sb = keep.tile([P, T // 16], U16, name="pos1_sb")
         pos2_sb = keep.tile([P, T // 16], U16, name="pos2_sb")
-        dy = [flow.tile([P, T], F32, name=f"dy{t}", tag=f"dy{t}" if t else "dx2", bufs=1) for t in range(W)]
-        gate_sb = flow.tile([P, S - C], F32, name="gate_sb", tag="dx1", bufs=1)
-        g_first = [
-            flow.tile([P, W * HALF], BF16, name="g_first", tag=tag, bufs=bufs, align_bytes=64)
-            for tag, bufs in (("g1_codes", 1), ("dq", 2))
-        ]
-        gate_2 = flow.tile([P, C], F32, name="gate_2", tag="dq", bufs=2, align_bytes=64)
+        dy = [keep.tile([P, T], F32, name=f"dy{t}") for t in range(W)]
         w2_sb = keep.tile([P, E, 2 * H], U8, name="w2_sb", align_bytes=64)
         w1_sb = keep.tile([P, E, 2 * K], U8, name="w1_sb", align_bytes=64)
         w3_sb = keep.tile([P, E, 2 * K], U8, name="w3_sb", align_bytes=64)
@@ -61,8 +58,8 @@ def tile_moe_bdx_glu_silu_kernel(
         make_identity(nc, ident[:])
 
         dy_rows = dyT.rearrange("(p t) c -> t p c", t=W)
-        a1_rows = a1.rearrange("(j q) c -> q j c", q=P)
-        a3_rows = a3.rearrange("(j q) c -> q j c", q=P)
+        a1_rows = a1.rearrange("(p t) c -> p t c", t=W)
+        a3_rows = a3.rearrange("(p t) c -> p t c", t=W)
 
         def load_words(dst, words, e0=0, e1=E):
             nc.sync.dma_start(
@@ -74,288 +71,242 @@ def tile_moe_bdx_glu_silu_kernel(
             for q in range(4):
                 nc.sync.dma_start(out=dst[32 * q : 32 * q + 4].bitcast(I32), in_=rows[4 * q : 4 * q + 4])
 
-        a1_t, a3_t = {}, {}
+        a1_sb, a3_sb, gate_sb = {}, {}, {}
 
         def load_a1(e, c0=0, c1=C):
             if c0 == 0:
-                a1_t[e] = flow.tile([P, W, C], F32, name="a1_sb", tag="a1", bufs=3)
-            nc.sync.dma_start(out=a1_t[e][:, :, c0:c1], in_=a1_rows[:, :, e * C + c0 : e * C + c1])
+                a1_sb[e] = sbuf([P, W, C], F32, "a1", 3)
+            nc.sync.dma_start(out=a1_sb[e][:, :, c0:c1], in_=a1_rows[:, :, e * C + c0 : e * C + c1])
 
         def load_a3(e, c0=0, c1=C):
             if c0 == 0:
-                a3_t[e] = flow.tile([P, W, C], F32, name="a3_sb", tag="a3")
-            nc.sync.dma_start(out=a3_t[e][:, :, c0:c1], in_=a3_rows[:, :, e * C + c0 : e * C + c1])
+                a3_sb[e] = sbuf([P, W, C], F32, "a3", 2)
+            nc.sync.dma_start(out=a3_sb[e][:, :, c0:c1], in_=a3_rows[:, :, e * C + c0 : e * C + c1])
 
-        def gate_cols(c0, c1):
-            if c0 < 2 * C:
-                return gate_sb[:, c0:c1]
-            return gate_2[:] if c0 == 2 * C else gate_sb[:, c0 - C : c1 - C]
+        def load_gate(e):
+            gate_sb[e] = sbuf([P, C], F32, f"gate{e % 2}")
+            nc.sync.dma_start(out=gate_sb[e], in_=gate[:P, e * C : (e + 1) * C])
 
-        def load_gate(c0, c1):
-            nc.sync.dma_start(out=gate_cols(c0, c1), in_=gate[:P, c0:c1])
-
+        gate_pair = sbuf([P, 2 * C], F32, "gate_pair")
         nc.sync.dma_start(offs_sb[:], offs)
-        load_gate(0, 2 * C)
+        nc.sync.dma_start(out=gate_pair, in_=gate[:P, : 2 * C])
         for t in range(W):
             nc.sync.dma_start(out=dy[t][:], in_=dy_rows[t])
             if t in (1, 2):
                 load_a1(0, (t - 1) * HALF, t * HALF)
-        load_a3(0, 0, HALF)
         load_words(w2_sb, w2_words, 0, 2)
         load_scales(w2_sc, w2_scales)
+        load_a3(0)
         load_a1(1)
-        load_a3(0, HALF, C)
-        load_gate(2 * C, 3 * C)
+        load_gate(2)
         load_a3(1)
-        load_a1(2)
-        load_gate(3 * C, S)
-        load_words(w2_sb, w2_words, 2, E)
         load_words(w1_sb, w1_words)
         load_words(w3_sb, w3_words)
         load_scales(w1_sc, w1_scales)
         load_scales(w3_sc, w3_scales)
+        load_a1(2)
+        load_gate(3)
+        load_words(w2_sb, w2_words, 2, E)
         nc.sync.dma_start(pos1_sb[:], pos1)
         nc.sync.dma_start(pos2_sb[:], pos2)
 
-        def by_quads(tile3):
-            return tile3.rearrange("p t (c i) -> p c t i", i=4)
+        def by_quads(ap):
+            return ap.rearrange("p t (c i) -> p c t i", i=4)
 
-        def into_quads(tile2):
-            return tile2.rearrange("p (c i t) -> p c t i", i=4, t=W)
+        def into_quads(ap):
+            return ap.rearrange("p (c i t) -> p c t i", i=4, t=W)
 
-        g_val, g_bf, g_q = {}, {}, {}
-
-        def gather(dst, t, c0, c1):
-            nc.vector.tensor_tensor(dst, dy[t][:].indirect(offs_sb[:, c0 // 16 : c1 // 16]), gate_cols(c0, c1), MULT)
+        def gather(dst, t, c0, c1, gates):
+            nc.vector.tensor_tensor(dst, dy[t][:].indirect(offs_sb[:, c0 // 16 : c1 // 16]), gates, MULT)
 
         def round_into(dst, src):
             nc.scalar.copy(into_quads(dst), by_quads(src))
 
-        def round_g(e):
-            g_bf[e] = flow.tile([P, W * C], BF16, name="g_bf", tag="g_bf", bufs=1, align_bytes=64)
-            round_into(g_bf[e][:], g_val[e])
+        def new_codes(width, tag, bufs):
+            return sbuf([P, width], U32, tag + "_codes", bufs), sbuf([P, width], U8, tag + "_scales", bufs)
 
-        def new_codes(width, tag):
-            codes = flow.tile([P, width], U32, name=tag + "_codes", tag=tag + "_codes", bufs=1, align_bytes=64)
-            scales = flow.tile([P, width], U8, name=tag + "_scales", tag=tag + "_scales", bufs=1, align_bytes=64)
-            return codes, scales
+        def quantize(q, c0, bf):
+            cols = slice(c0, c0 + bf.shape[1] // W)
+            nc.vector.quantize_mx(out=q[0][:, cols].bitcast(E5M2X4), scales=q[1][:, cols], in_=bf)
 
-        def quantize(q, bf, c0, c1):
-            nc.vector.quantize_mx(out=q[0][:, c0:c1].bitcast(E5M2X4), scales=q[1][:, c0:c1], in_=bf)
+        def half_of(ap, h):
+            return ap[:, :, h % 2 * HALF : (h % 2 + 1) * HALF]
 
-        def quantize_g(e):
-            g_q[e] = new_codes(C, f"g{e % 2}")
-            quantize(g_q[e], g_bf[e][:], 0, C)
+        def block_of(ap, b):
+            return ap[:, :, b * P : (b + 1) * P]
 
-        def half_of(tile3, h):
-            return tile3[:, :, h % 2 * HALF : (h % 2 + 1) * HALF].rearrange("q j (b c) -> q b j c", b=2)
+        g_val, g_bf, g_q, d_q = {}, {}, {}, {}
+        z, x, th, dh, dr, dr_ps, da = {}, {}, {}, {}, {}, {}, {}
 
-        z, x, a1_ps, x_ps, dh, th, dr, da, dq, d_q = {}, {}, {}, {}, {}, {}, {}, {}, {}, {}
+        def make_u(h, tag="z", bufs=2):
+            u = sbuf([P, W, HALF], F32, tag, bufs)
+            nc.scalar.activation(u, half_of(a1_sb[h // 2], h), ACT.Silu, scale=-1.0)
+            return u
 
-        def make_z(h):
-            z[h] = flow.tile([P, 2, W, P], F32, name="z", tag="z", bufs=2)
-            nc.scalar.activation(z[h][:], half_of(a1_t[h // 2], h), ACT.Silu, scale=-1.0)
+        def make_z(h, u, dst):
+            z[h] = dst
+            nc.scalar.activation(dst, u, ACT.Identity, bias=1.0, scale=-1.0)
 
-        def end_z(h):
-            nc.scalar.activation(z[h][:], z[h][:], ACT.Identity, bias=1.0, scale=-1.0)
+        def make_x(h, tag, engine=nc.gpsimd):
+            x[h] = sbuf([P, W, HALF], F32, tag)
+            engine.tensor_tensor(x[h], z[h], half_of(a3_sb[h // 2], h), MULT)
 
-        def new_dq(e):
-            dq[e] = flow.tile([P, 2, C, 2], F32, name="dq", tag="dq", bufs=2, align_bytes=64)
+        def turn(src, tag, bufs):
+            bank = psum.tile([P, W, P], F32, name=tag, tag=tag, bufs=bufs)
+            for t in range(W):
+                nc.tensor.transpose(bank[:, t, :], src[:, t, :], ident[:])
+            return bank[:]
 
-        def make_x(h, engine):
-            if h % 2:
-                new_dq(h // 2)
-                x[h] = dq[h // 2][:, :, HALF:, :].rearrange("q b (j c) u -> q b j (c u)", j=W)
-            else:
-                tag = "g_bf" if h else "g1_codes"
-                x[h] = flow.tile([P, 2, W, P], F32, name="x", tag=tag, bufs=1, align_bytes=64)[:]
-            engine.tensor_tensor(x[h], z[h][:], half_of(a3_t[h // 2], h), MULT)
-
-        def turn(src, tag):
-            bank = psum.tile([P, H], F32, name=tag, tag=tag)
-            for j in range(W):
-                nc.tensor.transpose(bank[:, j * P : (j + 1) * P], src[:, j, :], ident[:])
-            return bank
-
-        def turn_a1(h, b):
-            a1_ps[h, b] = turn(half_of(a1_t[h // 2], h)[:, b], "a1_ps")
-
-        def turn_x(h, b):
-            x_ps[h, b] = turn(x[h][:, b], "x_ps")
-
-        def make_th(h, b):
-            th[h, b] = flow.tile([P, H], F32, name="th", tag=f"th{b}", bufs=1 + b)[:]
-            nc.scalar.activation(th[h, b], a1_ps[h, b][:], ACT.Tanh, scale=0.5)
+        def make_th(h, b, tag="th", bufs=2):
+            a1_ps = turn(block_of(half_of(a1_sb[h // 2], h), b), "a1_ps", 1)
+            th[h, b] = sbuf([P, W, P], F32, tag, bufs)
+            nc.scalar.activation(th[h, b], a1_ps, ACT.Tanh, scale=0.5)
 
         def first(h, b):
-            e = h // 2
+            codes, scales = g_q[h // 2]
             cols = slice((h % 2 * 2 + b) * P, (h % 2 * 2 + b + 1) * P)
             dh[h, b] = psum.tile([P, H], F32, name="dh", tag="dh")
             nc.tensor.matmul_mx(
                 out=dh[h, b][:],
-                lhsT=g_q[e][0][:, cols].bitcast(E5M2X4),
-                lhsT_scale=g_q[e][1][:, cols],
-                rhs=w2_sb[:, e].bitcast(E2M1X4),
-                rhs_scale=w2_sc[:, e],
+                lhsT=codes[:, cols].bitcast(E5M2X4),
+                lhsT_scale=scales[:, cols],
+                rhs=w2_sb[:, h // 2].bitcast(E2M1X4),
+                rhs_scale=w2_sc[:, h // 2],
                 start=True,
                 stop=True,
             )
 
-        def by_pairs(ap):
-            return ap.rearrange("s (m u r) -> s u m r", u=2, r=2)
-
-        def gated(h, b, dst):
-            dr[h, b] = dst
-            nc.vector.scalar_tensor_tensor(dst, th[h, b], 1.0, dh[h, b][:], ADD, MULT)
-
-        def new_da(h, b, tag="da", bufs=3):
-            both = flow.tile([P, 2, H], BF16, name="da", tag=tag, bufs=bufs, align_bytes=64)
-            da[h, b] = [both[:, 0] if b else th[h, 1].bitcast(BF16)[:, :H], both[:, 1]]
+        def gated(h, b):
+            dr[h, b] = sbuf([P, W, P], F32, "dr", 2)
+            dh_tm = dh[h, b][:].rearrange("s (m t) -> s t m", t=W)
+            nc.vector.scalar_tensor_tensor(dr[h, b], th[h, b], 1.0, dh_tm, ADD, MULT)
+            dr_ps[h, b] = turn(dr[h, b], "dr_ps", 3)
 
         def delta(h, b, i):
+            factor = half_of(a1_sb[h // 2], h) if i else x[h]
             nc.vector.tensor_tensor(
-                da[h, b][i].rearrange("s (u m r) -> s u m r", u=2, r=2),
-                by_pairs(dr[h, b]),
-                by_pairs((x_ps, a1_ps)[i][h, b][:]),
+                into_quads(da[h][:, 1 - i, b * W * P : (b + 1) * W * P]),
+                by_quads(block_of(factor, b)),
+                by_quads(dr_ps[h, b]),
                 MULT,
             )
 
-        def turn_back(h, b, i0=0, i1=2, tag="drain"):
-            e = h // 2
-            bank = psum.tile([P, W * P], F32, name="back", tag=tag)
-            for j in range(2 * i0, 2 * i1):
-                words = da[h, b][j // 2].bitcast(F32)
-                nc.tensor.transpose(bank[:, j * P : (j + 1) * P], words[:, j % 2 * P : (j % 2 + 1) * P], ident[:])
-            c0 = (h % 2 * 2 + b) * P
-            nc.scalar.copy(
-                dq[e][:, i0:i1, c0 : c0 + P, :], bank[:].rearrange("p (i u s) -> p i s u", i=2, u=2)[:, i0:i1]
-            )
+        def quantize_d(h):
+            if h % 2 == 0:
+                d_q[h // 2] = new_codes(2 * C, "d", 2)
+            for i in (1, 0):
+                quantize(d_q[h // 2], i * C + h % 2 * HALF, da[h][:, 1 - i])
 
-        def quantize_d(e, c0=0, c1=2 * C):
-            if e not in d_q:
-                d_q[e] = new_codes(2 * C, f"d{e}")
-            quantize(d_q[e], dq[e][:].rearrange("p i c u -> p (i c u)").bitcast(BF16)[:, W * c0 : W * c1], c0, c1)
-
-        def second(e, kt, tag="drain"):
-            acc = psum.tile([P, C], F32, name="acc", tag=tag)
+        def second(e, kt):
+            codes, scales = d_q[e]
+            acc = psum.tile([P, C], F32, name="acc", tag="acc", bufs=2)
             for i, w, sc in ((1, w3_sb, w3_sc), (0, w1_sb, w1_sc)):
                 nc.tensor.matmul_mx(
                     out=acc[:],
                     lhsT=w[:, e, 2 * P * kt : 2 * P * (kt + 1)].bitcast(E2M1X4),
                     lhsT_scale=sc[:, e, P * kt : P * (kt + 1)],
-                    rhs=d_q[e][0][:, i * C : (i + 1) * C].bitcast(E5M2X4),
-                    rhs_scale=d_q[e][1][:, i * C : (i + 1) * C],
+                    rhs=codes[:, i * C : (i + 1) * C].bitcast(E5M2X4),
+                    rhs_scale=scales[:, i * C : (i + 1) * C],
                     start=i == 1,
                     stop=i == 0,
                 )
             nc.scalar.activation(dx[kt][:, e * C : (e + 1) * C], acc[:], ACT.Copy, scale=0.5)
 
-        g_pair = flow.tile([P, W, 2 * C], F32, name="g_pair", tag="dx0", bufs=1)
-        g_val[0], g_val[1] = g_pair[:, :, :C], g_pair[:, :, C:]
+        g_pair = sbuf([P, W, 2 * C], F32, "dx0")
+        g_val[1] = g_pair[:, :, C:]
         for t in range(W - 1):
-            gather(g_pair[:, t, :], t, 0, 2 * C)
-        make_z(0)
+            gather(g_pair[:, t, :], t, 0, 2 * C, gate_pair)
+        make_th(0, 0, "z", 2)
+        make_th(0, 1, "th_first", 1)
+        u_first = make_u(0, "g_bf1", 1)
+        make_z(0, u_first, u_first)
         for b in range(2):
-            turn_a1(0, b)
-            make_th(0, b)
-        end_z(0)
-        make_z(1)
-        gather(g_pair[:, W - 1, :C], W - 1, 0, C)
-        round_into(g_first[0][:], g_val[0][:, :, :HALF])
-        end_z(1)
-        round_into(g_first[1][:], g_val[0][:, :, HALF:])
-        gather(g_pair[:, W - 1, C:], W - 1, C, 2 * C)
-        g_q[0] = new_codes(C, "g0")
-        quantize(g_q[0], g_first[0][:], 0, HALF)
-        make_x(0, nc.vector)
+            make_th(1, b)
+        u_second = make_u(1)
+        gather(g_pair[:, W - 1, :C], W - 1, 0, C, gate_pair[:, :C])
+        g_first = [sbuf([P, W * HALF], BF16, tag) for tag in ("g1_codes", "x_second")]
+        for h in range(2):
+            round_into(g_first[h], half_of(g_pair[:, :, :C], h))
+        gather(g_pair[:, W - 1, C:], W - 1, C, 2 * C, gate_pair[:, C:])
+        make_z(1, u_second, sbuf([P, W, HALF], F32, "gate_pair"))
+        g_q[0] = new_codes(C, "g0", 1)
+        quantize(g_q[0], 0, g_first[0])
+        make_x(0, "g1_codes", nc.vector)
+        quantize(g_q[0], HALF, g_first[1])
         for b in range(2):
             first(0, b)
-        quantize(g_q[0], g_first[1][:], HALF, C)
-        for b in range(2):
-            turn_x(0, b)
-        round_g(1)
-        for h in range(3, 2):
-            make_z(h)
-            end_z(h)
-        dx = [flow.tile([P, S], F32, name=f"dx{kt}", tag=f"dx{kt}", bufs=1) for kt in range(KT)]
+            gated(0, b)
+        dx = [flow.tile([P, S], F32, name=f"dx{kt}", tag=f"dx{kt}", align_bytes=64) for kt in range(KT)]
 
         for h in range(HALVES):
-            e = h // 2
+            e, odd = divmod(h, 2)
             ahead = h + 1 < HALVES
             gathers = e + 2 < E
-            held = f"g{(e + 1) % 2}_codes" if h % 2 == 0 and e + 1 < E else f"d{max(e - 1, 0)}_codes"
-            if h % 2 == 0 and gathers:
-                g_next = flow.tile([P, W, C], F32, name="g_val", tag="g_val")
-                g_val[e + 2] = g_next[:]
-                load_a3(e + 2)
+            if not odd:
+                g_next = sbuf([P, W, C], F32, "g_val", 2)
+                g_val[e + 2] = g_next
+                if gathers:
+                    load_a3(e + 2)
                 if e + 3 < E:
                     load_a1(e + 3)
-            t0 = h % 2 * 2
+            planes = g_next[:, 2 * odd : 2 * odd + 2, :]
+            da[h] = planes.bitcast(BF16)
             if ahead:
-                make_x(h + 1, nc.gpsimd)
-            if gathers:
-                gated(h, 0, g_next[:].rearrange("p t c -> p (t c)")[:, t0 * C + HALF : (t0 + 1) * C + HALF])
-            elif ahead:
-                gated(h, 0, flow.tile([P, H], F32, name="dr_a", tag=held, bufs=1, align_bytes=64)[:])
-            else:
-                gated(h, 0, flow.tile([P, H], F32, name="dr_a", tag="z", bufs=2)[:])
-            gated(h, 1, flow.tile([P, H], F32, name="dr_b", tag="dr_b", bufs=1)[:])
-            if ahead:
+                if h == 0:
+                    make_x(1, "x_second")
+                elif odd:
+                    make_x(h + 1, f"g_bf{(e + 1) % 2}")
+                elif e + 1 < E:
+                    make_x(h + 1, f"gate{(e + 1) % 2}")
+                else:
+                    x[h + 1] = g_val[e + 1][:, 2:, :].rearrange("p u (v c) -> p (u v) c", v=2)
+                    nc.gpsimd.tensor_tensor(x[h + 1], z[h + 1], half_of(a3_sb[e], h + 1), MULT)
                 for b in range(2):
                     first(h + 1, b)
-            if h % 2 == 0 and e > 1:
-                second(e - 2, 0)
-            if h + 1 == HALVES:
-                second(e - 1, 0)
+            if h == 0:
+                for b in range(2):
+                    gated(1, b)
+                g_bf[1] = sbuf([P, W * C], BF16, "g_bf1")
+                round_into(g_bf[1], g_val[1])
+            if e:
+                for kt in range(odd * 2, 2 + odd):
+                    second(e - 1, kt)
+            for b in range(2):
+                delta(h, b, 1)
+                if ahead and h and b:
+                    gated(h + 1, 1)
+                delta(h, b, 0)
+                if ahead and h and not b:
+                    gated(h + 1, 0)
+            if odd and 0 < e < E - 3:
+                load_gate(e + 3)
             if h + 2 < HALVES:
-                make_z(h + 2)
-                end_z(h + 2)
-            new_da(h, 0)
-            if gathers and h != 1:
-                new_da(h, 1, held, 1)
-            else:
-                new_da(h, 1)
-            for i in (1, 0):
-                for b in range(2):
-                    delta(h, b, i)
-            if ahead:
-                for b in range(2):
-                    turn_a1(h + 1, b)
-                    make_th(h + 1, b)
-            if ahead:
-                for b in range(2):
-                    turn_back(h, b)
-            else:
-                for i in (1, 0):
-                    for b in range(2):
-                        turn_back(h, b, i, i + 1, ("drain", "dh")[i])
-            if ahead:
-                for b in range(2):
-                    turn_x(h + 1, b)
+                make_th(h + 2, 0)
+                if odd and e + 2 < E:
+                    make_th(h + 2, 1, f"g{e % 2}_codes", 1)
+                else:
+                    make_th(h + 2, 1)
+                u = make_u(h + 2)
+                make_z(h + 2, u, u)
+            quantize_d(h)
             if gathers:
-                for t in (t0, t0 + 1):
-                    gather(g_next[:, t, :], t, (e + 2) * C, (e + 3) * C)
-                if h % 2:
-                    round_g(e + 2)
-            if h % 2 == 0 and e + 1 < E:
-                quantize_g(e + 1)
-            elif e and ahead:
-                quantize_d(e - 1)
-        for c0, c1 in ((C, 2 * C), (0, HALF), (HALF, HALF + P), (HALF + P, C)):
-            quantize_d(E - 1, c0, c1)
-        second(E - 1, 0, "a1_ps")
-        for kt in range(1, KT):
+                for t in range(2):
+                    gather(planes[:, t, :], 2 * odd + t, (e + 2) * C, (e + 3) * C, gate_sb[e + 2])
+                if odd:
+                    g_bf[e + 2] = sbuf([P, W * C], BF16, f"g_bf{e % 2}")
+                    round_into(g_bf[e + 2], g_next)
+            if not odd and e + 1 < E:
+                g_q[e + 1] = new_codes(C, f"g{(e + 1) % 2}", 1)
+                quantize(g_q[e + 1], 0, g_bf[e + 1])
+        for kt in range(KT):
             second(E - 1, kt)
-        for kt in range(1, KT):
-            for e in range(E - 1):
-                second(e, kt)
 
         pieces = [(0, 0, T), (1, 0, T), (2, 0, 1024), (2, 1024, T)]
         for kt, c0, c1 in pieces:
             if c0 == 0:
-                y1 = flow.tile([P, T], F32, name="y1", tag="a3")
-                y2 = flow.tile([P, T], F32, name="y2", tag="a1", bufs=3)
-                nc.vector.tensor_copy(y1[:], dx[kt][:].indirect(pos1_sb[:]))
+                y1 = sbuf([P, T], F32, "a3", 2)
+                y2 = sbuf([P, T], F32, "a1", 3)
+                nc.vector.tensor_copy(y1, dx[kt][:].indirect(pos1_sb[:]))
             nc.vector.tensor_tensor(
                 y2[:, c0:c1], dx[kt][:].indirect(pos2_sb[:, c0 // 16 : c1 // 16]), y1[:, c0:c1], ADD
             )

@@ -147,8 +147,8 @@ def tile_moe_bdx_glu_silu_kernel(
             z[h] = dst
             nc.scalar.activation(dst, u, ACT.Identity, bias=1.0, scale=-1.0)
 
-        def make_x(h, tag, engine=nc.gpsimd):
-            x[h] = sbuf([P, W, HALF], F32, tag)
+        def make_x(h, dst, engine=nc.gpsimd):
+            x[h] = dst
             engine.tensor_tensor(x[h], z[h], half_of(a3_sb[h // 2], h), MULT)
 
         def turn(src, tag, bufs):
@@ -157,9 +157,18 @@ def tile_moe_bdx_glu_silu_kernel(
                 nc.tensor.transpose(bank[:, t, :], src[:, t, :], ident[:])
             return bank[:]
 
-        def make_th(h, b, tag="th", bufs=2):
+        def planes_of(h):
+            return g_val[h // 2 + 2][:, h % 2 * 2 : h % 2 * 2 + 2, :]
+
+        def across(h):
+            if h % 2 == 0:
+                g_val[h // 2 + 2] = sbuf([P, W, C], F32, "g_val", 2)
+            middle = planes_of(h).rearrange("p u c -> p (u c)")[:, HALF : HALF + C]
+            return middle.rearrange("p (t m) -> p t m", t=W)
+
+        def make_th(h, b, dst):
             a1_ps = turn(block_of(half_of(a1_sb[h // 2], h), b), "a1_ps", 1)
-            th[h, b] = sbuf([P, W, P], F32, tag, bufs)
+            th[h, b] = dst
             nc.scalar.activation(th[h, b], a1_ps, ACT.Tanh, scale=0.5)
 
         def first(h, b):
@@ -176,8 +185,8 @@ def tile_moe_bdx_glu_silu_kernel(
                 stop=True,
             )
 
-        def gated(h, b):
-            dr[h, b] = sbuf([P, W, P], F32, "dr", 2)
+        def gated(h, b, tag="dr", bufs=2):
+            dr[h, b] = sbuf([P, W, P], F32, tag, bufs)
             dh_tm = dh[h, b][:].rearrange("s (m t) -> s t m", t=W)
             nc.vector.scalar_tensor_tensor(dr[h, b], th[h, b], 1.0, dh_tm, ADD, MULT)
             dr_ps[h, b] = turn(dr[h, b], "dr_ps", 3)
@@ -216,22 +225,23 @@ def tile_moe_bdx_glu_silu_kernel(
         g_val[1] = g_pair[:, :, C:]
         for t in range(W - 1):
             gather(g_pair[:, t, :], t, 0, 2 * C, gate_pair)
-        make_th(0, 0, "z", 2)
-        make_th(0, 1, "th_first", 1)
-        u_first = make_u(0, "g_bf1", 1)
+        g_first = [sbuf([P, W * HALF], BF16, "g_val", 2), sbuf([P, W * HALF], BF16, "dax2")]
+        make_th(0, 0, sbuf([P, W, P], F32, "z", 2))
+        make_th(0, 1, sbuf([P, W, P], F32, "g_val", 2))
+        u_first = make_u(0, "g_bf", 1)
         make_z(0, u_first, u_first)
         for b in range(2):
-            make_th(1, b)
+            make_th(1, b, sbuf([P, W, P], F32, "th", 2))
         u_second = make_u(1)
         gather(g_pair[:, W - 1, :C], W - 1, 0, C, gate_pair[:, :C])
-        g_first = [sbuf([P, W * HALF], BF16, tag) for tag in ("g1_codes", "x_second")]
         for h in range(2):
             round_into(g_first[h], half_of(g_pair[:, :, :C], h))
         gather(g_pair[:, W - 1, C:], W - 1, C, 2 * C, gate_pair[:, C:])
         make_z(1, u_second, sbuf([P, W, HALF], F32, "gate_pair"))
         g_q[0] = new_codes(C, "g0", 1)
         quantize(g_q[0], 0, g_first[0])
-        make_x(0, "g1_codes", nc.vector)
+        g_val[2] = sbuf([P, W, C], F32, "g_val", 2)
+        make_x(0, planes_of(0).rearrange("p u (v c) -> p (u v) c", v=2), nc.vector)
         quantize(g_q[0], HALF, g_first[1])
         for b in range(2):
             first(0, b)
@@ -243,61 +253,59 @@ def tile_moe_bdx_glu_silu_kernel(
             ahead = h + 1 < HALVES
             gathers = e + 2 < E
             if not odd:
-                g_next = sbuf([P, W, C], F32, "g_val", 2)
-                g_val[e + 2] = g_next
                 if gathers:
                     load_a3(e + 2)
                 if e + 3 < E:
                     load_a1(e + 3)
-            planes = g_next[:, 2 * odd : 2 * odd + 2, :]
-            da[h] = planes.bitcast(BF16)
+            da[h] = sbuf([P, 2, W * HALF], BF16, f"dax{h % 3}")
             if ahead:
-                if h == 0:
-                    make_x(1, "x_second")
-                elif odd:
-                    make_x(h + 1, f"g_bf{(e + 1) % 2}")
-                elif e + 1 < E:
-                    make_x(h + 1, f"gate{(e + 1) % 2}")
-                else:
-                    x[h + 1] = g_val[e + 1][:, 2:, :].rearrange("p u (v c) -> p (u v) c", v=2)
-                    nc.gpsimd.tensor_tensor(x[h + 1], z[h + 1], half_of(a3_sb[e], h + 1), MULT)
+                make_x(h + 1, sbuf([P, W, HALF], F32, f"dax{(h - 1) % 3}"))
                 for b in range(2):
                     first(h + 1, b)
             if h == 0:
-                for b in range(2):
-                    gated(1, b)
-                g_bf[1] = sbuf([P, W * C], BF16, "g_bf1")
+                gated(1, 0)
+                gated(1, 1, "g1_codes", 1)
+                g_bf[1] = sbuf([P, W * C], BF16, "g_bf")
                 round_into(g_bf[1], g_val[1])
             if e:
                 for kt in range(odd * 2, 2 + odd):
                     second(e - 1, kt)
-            for b in range(2):
-                delta(h, b, 1)
-                if ahead and h and b:
-                    gated(h + 1, 1)
-                delta(h, b, 0)
-                if ahead and h and not b:
+            delta(h, 0, 1)
+            delta(h, 0, 0)
+            if h == 0:
+                delta(h, 1, 0)
+                delta(h, 1, 1)
+            else:
+                if ahead:
                     gated(h + 1, 0)
+                delta(h, 1, 1)
+                if ahead:
+                    gated(h + 1, 1)
+                delta(h, 1, 0)
             if odd and 0 < e < E - 3:
                 load_gate(e + 3)
             if h + 2 < HALVES:
-                make_th(h + 2, 0)
                 if odd and e + 2 < E:
-                    make_th(h + 2, 1, f"g{e % 2}_codes", 1)
+                    make_th(h + 2, 0, sbuf([P, W, P], F32, f"g{e % 2}_codes"))
                 else:
-                    make_th(h + 2, 1)
+                    make_th(h + 2, 0, sbuf([P, W, P], F32, "th", 2))
+                if (h + 1) // 2 + 2 < E:
+                    make_th(h + 2, 1, across(h + 1))
+                else:
+                    make_th(h + 2, 1, sbuf([P, W, P], F32, "th", 2))
                 u = make_u(h + 2)
                 make_z(h + 2, u, u)
-            quantize_d(h)
-            if gathers:
-                for t in range(2):
-                    gather(planes[:, t, :], 2 * odd + t, (e + 2) * C, (e + 3) * C, gate_sb[e + 2])
-                if odd:
-                    g_bf[e + 2] = sbuf([P, W * C], BF16, f"g_bf{e % 2}")
-                    round_into(g_bf[e + 2], g_next)
-            if not odd and e + 1 < E:
-                g_q[e + 1] = new_codes(C, f"g{(e + 1) % 2}", 1)
-                quantize(g_q[e + 1], 0, g_bf[e + 1])
+            for t in range(2):
+                if gathers:
+                    gather(planes_of(h)[:, t, :], 2 * odd + t, (e + 2) * C, (e + 3) * C, gate_sb[e + 2])
+                if t == 0:
+                    if not odd and e + 1 < E:
+                        g_q[e + 1] = new_codes(C, f"g{(e + 1) % 2}", 1)
+                        quantize(g_q[e + 1], 0, g_bf[e + 1])
+                    quantize_d(h)
+            if gathers and odd:
+                g_bf[e + 2] = sbuf([P, W * C], BF16, "g_bf")
+                round_into(g_bf[e + 2], g_val[e + 2])
         for kt in range(KT):
             second(E - 1, kt)
 

@@ -89,14 +89,17 @@ def tile_moe_bdx_glu_silu_kernel(
 
         gate_pair = sbuf([P, 2 * C], F32, "gate_pair")
         nc.sync.dma_start(offs_sb[:], offs)
-        nc.sync.dma_start(out=gate_pair, in_=gate[:P, : 2 * C])
         for t in range(W):
             nc.sync.dma_start(out=dy[t][:], in_=dy_rows[t])
+            if t == 0:
+                for c0 in (0, C):
+                    nc.sync.dma_start(out=gate_pair[:, c0 : c0 + C], in_=gate[:P, c0 : c0 + C])
             if t in (1, 2):
                 load_a1(0, (t - 1) * HALF, t * HALF)
+        load_a3(0, 0, HALF)
         load_words(w2_sb, w2_words, 0, 2)
         load_scales(w2_sc, w2_scales)
-        load_a3(0)
+        load_a3(0, HALF, C)
         load_a1(1)
         load_gate(2)
         load_a3(1)
@@ -110,17 +113,17 @@ def tile_moe_bdx_glu_silu_kernel(
         nc.sync.dma_start(pos1_sb[:], pos1)
         nc.sync.dma_start(pos2_sb[:], pos2)
 
-        def by_quads(ap):
-            return ap.rearrange("p t (c i) -> p c t i", i=4)
+        def by_runs(ap, run):
+            return ap.rearrange("p t (c i) -> p c t i", i=run)
 
-        def into_quads(ap):
-            return ap.rearrange("p (c i t) -> p c t i", i=4, t=W)
+        def into_runs(ap, run):
+            return ap.rearrange("p (c i t) -> p c t i", i=run, t=W)
 
         def gather(dst, t, c0, c1, gates):
             nc.vector.tensor_tensor(dst, dy[t][:].indirect(offs_sb[:, c0 // 16 : c1 // 16]), gates, MULT)
 
         def round_into(dst, src):
-            nc.scalar.copy(into_quads(dst), by_quads(src))
+            nc.scalar.copy(into_runs(dst, 4), by_runs(src, 4))
 
         def new_codes(width, tag, bufs):
             return sbuf([P, width], U32, tag + "_codes", bufs), sbuf([P, width], U8, tag + "_scales", bufs)
@@ -194,9 +197,9 @@ def tile_moe_bdx_glu_silu_kernel(
         def delta(h, b, i):
             factor = half_of(a1_sb[h // 2], h) if i else x[h]
             nc.vector.tensor_tensor(
-                into_quads(da[h][:, 1 - i, b * W * P : (b + 1) * W * P]),
-                by_quads(block_of(factor, b)),
-                by_quads(dr_ps[h, b]),
+                into_runs(da[h][:, 1 - i, b * W * P : (b + 1) * W * P], 2),
+                by_runs(block_of(factor, b), 2),
+                by_runs(dr_ps[h, b], 2),
                 MULT,
             )
 
@@ -206,24 +209,35 @@ def tile_moe_bdx_glu_silu_kernel(
             for i in (1, 0):
                 quantize(d_q[h // 2], i * C + h % 2 * HALF, da[h][:, 1 - i])
 
-        def second(e, kt):
+        def quantize_g(e):
+            g_q[e] = new_codes(C, f"g{e % 2}", 1)
+            quantize(g_q[e], 0, g_bf[e])
+
+        def second_pass(e, kt, i, acc):
             codes, scales = d_q[e]
+            w, sc = ((w1_sb, w1_sc), (w3_sb, w3_sc))[i]
+            nc.tensor.matmul_mx(
+                out=acc[:],
+                lhsT=w[:, e, 2 * P * kt : 2 * P * (kt + 1)].bitcast(E2M1X4),
+                lhsT_scale=sc[:, e, P * kt : P * (kt + 1)],
+                rhs=codes[:, i * C : (i + 1) * C].bitcast(E5M2X4),
+                rhs_scale=scales[:, i * C : (i + 1) * C],
+                start=i == 1,
+                stop=i == 0,
+            )
+            if i == 0:
+                nc.scalar.activation(dx[kt][:, e * C : (e + 1) * C], acc[:], ACT.Copy, scale=0.5)
+
+        def second(e, kt):
             acc = psum.tile([P, C], F32, name="acc", tag="acc", bufs=2)
-            for i, w, sc in ((1, w3_sb, w3_sc), (0, w1_sb, w1_sc)):
-                nc.tensor.matmul_mx(
-                    out=acc[:],
-                    lhsT=w[:, e, 2 * P * kt : 2 * P * (kt + 1)].bitcast(E2M1X4),
-                    lhsT_scale=sc[:, e, P * kt : P * (kt + 1)],
-                    rhs=codes[:, i * C : (i + 1) * C].bitcast(E5M2X4),
-                    rhs_scale=scales[:, i * C : (i + 1) * C],
-                    start=i == 1,
-                    stop=i == 0,
-                )
-            nc.scalar.activation(dx[kt][:, e * C : (e + 1) * C], acc[:], ACT.Copy, scale=0.5)
+            for i in (1, 0):
+                second_pass(e, kt, i, acc)
 
         g_pair = sbuf([P, W, 2 * C], F32, "dx0")
         g_val[1] = g_pair[:, :, C:]
-        for t in range(W - 1):
+        for c0 in (0, C):
+            gather(g_pair[:, 0, c0 : c0 + C], 0, c0, c0 + C, gate_pair[:, c0 : c0 + C])
+        for t in range(1, W - 1):
             gather(g_pair[:, t, :], t, 0, 2 * C, gate_pair)
         g_first = [sbuf([P, W * HALF], BF16, "g_val", 2), sbuf([P, W * HALF], BF16, "dax2")]
         make_th(0, 0, sbuf([P, W, P], F32, "z", 2))
@@ -257,9 +271,16 @@ def tile_moe_bdx_glu_silu_kernel(
                     load_a3(e + 2)
                 if e + 3 < E:
                     load_a1(e + 3)
-            da[h] = sbuf([P, 2, W * HALF], BF16, f"dax{h % 3}")
-            if ahead:
+            if h == HALVES - 3:
+                wide = sbuf([P, 3, W * HALF], BF16, f"dax{h % 3}")
+                da[h] = wide[:, 1:]
+            else:
+                da[h] = sbuf([P, 2, W * HALF], BF16, f"dax{h % 3}")
+            if h == HALVES - 2:
+                make_x(h + 1, wide[:, :2].bitcast(F32).rearrange("p u (v c) -> p (u v) c", v=2))
+            elif ahead:
                 make_x(h + 1, sbuf([P, W, HALF], F32, f"dax{(h - 1) % 3}"))
+            if ahead:
                 for b in range(2):
                     first(h + 1, b)
             if h == 0:
@@ -270,17 +291,23 @@ def tile_moe_bdx_glu_silu_kernel(
             if e:
                 for kt in range(odd * 2, 2 + odd):
                     second(e - 1, kt)
+            if not ahead:
+                break
             delta(h, 0, 1)
+            if h + 2 == HALVES:
+                gated(h + 1, 0)
             delta(h, 0, 0)
             if h == 0:
                 delta(h, 1, 0)
                 delta(h, 1, 1)
-            else:
-                if ahead:
-                    gated(h + 1, 0)
+            elif h + 2 == HALVES:
+                gated(h + 1, 1)
                 delta(h, 1, 1)
-                if ahead:
-                    gated(h + 1, 1)
+                delta(h, 1, 0)
+            else:
+                gated(h + 1, 0)
+                delta(h, 1, 1)
+                gated(h + 1, 1)
                 delta(h, 1, 0)
             if odd and 0 < e < E - 3:
                 load_gate(e + 3)
@@ -299,23 +326,40 @@ def tile_moe_bdx_glu_silu_kernel(
                 if gathers:
                     gather(planes_of(h)[:, t, :], 2 * odd + t, (e + 2) * C, (e + 3) * C, gate_sb[e + 2])
                 if t == 0:
-                    if not odd and e + 1 < E:
-                        g_q[e + 1] = new_codes(C, f"g{(e + 1) % 2}", 1)
-                        quantize(g_q[e + 1], 0, g_bf[e + 1])
+                    if gathers and not odd:
+                        quantize_g(e + 1)
                     quantize_d(h)
+                elif e + 2 == E and not odd:
+                    quantize_g(e + 1)
             if gathers and odd:
                 g_bf[e + 2] = sbuf([P, W * C], BF16, "g_bf")
                 round_into(g_bf[e + 2], g_val[e + 2])
-        for kt in range(KT):
-            second(E - 1, kt)
+        last = HALVES - 1
+        delta(last, 0, 1)
+        delta(last, 1, 1)
+        delta(last, 0, 0)
+        quantize(d_q[E - 1], C + HALF, da[last][:, 0])
+        delta(last, 1, 0)
+        for b in range(2):
+            quantize(d_q[E - 1], HALF + b * P, da[last][:, 1, b * W * P : (b + 1) * W * P])
+        accs = [psum.tile([P, C], F32, name="acc_last", tag="dh") for kt in range(KT)]
+        for kt, i in ((0, 1), (1, 1), (0, 0), (1, 0), (2, 1), (2, 0)):
+            second_pass(E - 1, kt, i, accs[kt])
 
-        pieces = [(0, 0, T), (1, 0, T), (2, 0, 1024), (2, 1024, T)]
-        for kt, c0, c1 in pieces:
-            if c0 == 0:
-                y1 = sbuf([P, T], F32, "a3", 2)
-                y2 = sbuf([P, T], F32, "a1", 3)
-                nc.vector.tensor_copy(y1, dx[kt][:].indirect(pos1_sb[:]))
-            nc.vector.tensor_tensor(
-                y2[:, c0:c1], dx[kt][:].indirect(pos2_sb[:, c0 // 16 : c1 // 16]), y1[:, c0:c1], ADD
-            )
-            nc.sync.dma_start(out=out[kt * P : (kt + 1) * P, c0:c1], in_=y2[:, c0:c1])
+        y1 = [sbuf([P, T], F32, "a1", 3) for kt in range(KT)]
+        y2 = [sbuf([P, T], F32, tag, bufs) for tag, bufs in (("a3", 2), ("a3", 2), ("g_val", 2))]
+
+        def fetch_first(kt):
+            nc.vector.tensor_copy(y1[kt], dx[kt][:].indirect(pos1_sb[:]))
+
+        def add_second(kt, c0, c1):
+            lists = pos2_sb[:, c0 // 16 : c1 // 16]
+            nc.vector.tensor_tensor(y2[kt][:, c0:c1], dx[kt][:].indirect(lists), y1[kt][:, c0:c1], ADD)
+            nc.sync.dma_start(out=out[kt * P : (kt + 1) * P, c0:c1], in_=y2[kt][:, c0:c1])
+
+        fetch_first(0)
+        for kt in range(1, KT):
+            fetch_first(kt)
+            add_second(kt - 1, 0, T)
+        for c0, c1 in ((0, T // 2), (T // 2, T - HALF), (T - HALF, T)):
+            add_second(KT - 1, c0, c1)

@@ -26,7 +26,7 @@ P = 128
 W = 4
 KT = K // P
 HALF = C // 2
-HALVES = 2 * E
+BLOCKS = C // P
 
 
 def tile_moe_bdx_glu_silu_kernel(
@@ -36,7 +36,7 @@ def tile_moe_bdx_glu_silu_kernel(
     with ExitStack() as ctx:
         keep = ctx.enter_context(tc.tile_pool(name="keep", bufs=1))
         flow = ctx.enter_context(tc.tile_pool(name="flow", bufs=1))
-        psum = ctx.enter_context(tc.psum_pool(name="psum", bufs=2))
+        psum = ctx.enter_context(tc.psum_pool(name="psum", bufs=1))
 
         def sbuf(shape, dtype, tag, bufs=1):
             return flow.tile(shape, dtype, name=tag, tag=tag, bufs=bufs, align_bytes=64)[:]
@@ -71,45 +71,58 @@ def tile_moe_bdx_glu_silu_kernel(
             for q in range(4):
                 nc.sync.dma_start(out=dst[32 * q : 32 * q + 4].bitcast(I32), in_=rows[4 * q : 4 * q + 4])
 
-        a1_sb, a3_sb, gate_sb = {}, {}, {}
+        gate_sb = [keep.tile([P, C], F32, name=f"gate{e}") for e in range(E)]
+        ring = keep.tile([P, 3 * W + 4, C], F32, name="ring", align_bytes=64)
+
+        def slot(e):
+            return ring[:, W * (e % 3 + 1) : W * (e % 3 + 2), :]
+
+        turns = ctx.enter_context(tc.tile_pool(name="turns", bufs=1))
+
+        def in_turn(shape, dtype, name, side):
+            return turns.tile(shape, dtype, name=name, tag=name, align_bytes=64, offset=side % 2 * 4 * W * C)[:]
+
+        a3_sb = {}
 
         def load_a1(e, c0=0, c1=C):
-            if c0 == 0:
-                a1_sb[e] = sbuf([P, W, C], F32, "a1", 3)
-            nc.sync.dma_start(out=a1_sb[e][:, :, c0:c1], in_=a1_rows[:, :, e * C + c0 : e * C + c1])
+            nc.sync.dma_start(out=slot(e)[:, :, c0:c1], in_=a1_rows[:, :, e * C + c0 : e * C + c1])
 
         def load_a3(e, c0=0, c1=C):
             if c0 == 0:
-                a3_sb[e] = sbuf([P, W, C], F32, "a3", 2)
+                a3_sb[e] = sbuf([P, W, C], F32, f"a3_{e % 2}")
             nc.sync.dma_start(out=a3_sb[e][:, :, c0:c1], in_=a3_rows[:, :, e * C + c0 : e * C + c1])
 
         def load_gate(e):
-            gate_sb[e] = sbuf([P, C], F32, f"gate{e % 2}")
-            nc.sync.dma_start(out=gate_sb[e], in_=gate[:P, e * C : (e + 1) * C])
+            nc.sync.dma_start(out=gate_sb[e][:], in_=gate[:P, e * C : (e + 1) * C])
 
-        gate_pair = sbuf([P, 2 * C], F32, "gate_pair")
-        nc.sync.dma_start(offs_sb[:], offs)
-        for t in range(W):
+        def load_dy(t):
             nc.sync.dma_start(out=dy[t][:], in_=dy_rows[t])
-            if t == 0:
-                for c0 in (0, C):
-                    nc.sync.dma_start(out=gate_pair[:, c0 : c0 + C], in_=gate[:P, c0 : c0 + C])
-            if t in (1, 2):
-                load_a1(0, (t - 1) * HALF, t * HALF)
-        load_a3(0, 0, HALF)
+
+        nc.sync.dma_start(offs_sb[:], offs)
+        load_dy(0)
+        load_gate(0)
+        load_gate(1)
+        load_dy(1)
+        load_dy(2)
+        load_a1(0, 0, HALF)
+        load_dy(3)
+        load_a1(0, HALF, C)
+        load_gate(2)
         load_words(w2_sb, w2_words, 0, 2)
         load_scales(w2_sc, w2_scales)
+        load_a3(0, 0, HALF)
         load_a3(0, HALF, C)
         load_a1(1)
-        load_gate(2)
         load_a3(1)
+        load_a1(2)
         load_words(w1_sb, w1_words)
         load_words(w3_sb, w3_words)
         load_scales(w1_sc, w1_scales)
         load_scales(w3_sc, w3_scales)
-        load_a1(2)
         load_gate(3)
         load_words(w2_sb, w2_words, 2, E)
+        load_gate(4)
+        load_gate(5)
         nc.sync.dma_start(pos1_sb[:], pos1)
         nc.sync.dma_start(pos2_sb[:], pos2)
 
@@ -119,235 +132,211 @@ def tile_moe_bdx_glu_silu_kernel(
         def into_runs(ap, run):
             return ap.rearrange("p (c i t) -> p c t i", i=run, t=W)
 
-        def gather(dst, t, c0, c1, gates):
-            nc.vector.tensor_tensor(dst, dy[t][:].indirect(offs_sb[:, c0 // 16 : c1 // 16]), gates, MULT)
+        def half_of(ap, h):
+            return ap[:, :, h * HALF : (h + 1) * HALF]
+
+        def block_of(ap, b):
+            return ap[:, :, b * P : (b + 1) * P]
+
+        def bank(tag, shape):
+            return psum.tile(shape, F32, name=tag, tag=tag)[:]
+
+        g_val, g_bf, g_q, d_q = {}, {}, {}, {}
+        z, x, th, dh, dr_ps, da = {}, {}, {}, {}, {}, {}
+
+        def gather(e, t):
+            lists = offs_sb[:, e * C // 16 : (e + 1) * C // 16]
+            nc.vector.tensor_tensor(g_val[e][:, t, :], dy[t][:].indirect(lists), gate_sb[e][:], MULT)
 
         def round_into(dst, src):
             nc.scalar.copy(into_runs(dst, 4), by_runs(src, 4))
 
-        def new_codes(width, tag, bufs):
-            return sbuf([P, width], U32, tag + "_codes", bufs), sbuf([P, width], U8, tag + "_scales", bufs)
+        def round_g(e):
+            g_bf[e] = sbuf([P, W * C], BF16, "g_bf")
+            round_into(g_bf[e], g_val[e])
 
         def quantize(q, c0, bf):
             cols = slice(c0, c0 + bf.shape[1] // W)
             nc.vector.quantize_mx(out=q[0][:, cols].bitcast(E5M2X4), scales=q[1][:, cols], in_=bf)
 
-        def half_of(ap, h):
-            return ap[:, :, h % 2 * HALF : (h % 2 + 1) * HALF]
+        def quantize_g(e):
+            g_q[e] = in_turn([P, C], U32, f"g_codes{e}", e), sbuf([P, C], U8, f"g_scales{e % 2}")
+            quantize(g_q[e], 0, g_bf[e])
 
-        def block_of(ap, b):
-            return ap[:, :, b * P : (b + 1) * P]
+        def new_d(e):
+            d_q[e] = sbuf([P, 2 * C], U32, f"d_codes{e % 3}"), sbuf([P, 2 * C], U8, f"d_scales{e % 3}")
 
-        g_val, g_bf, g_q, d_q = {}, {}, {}, {}
-        z, x, th, dh, dr, dr_ps, da = {}, {}, {}, {}, {}, {}, {}
+        def quantize_d(e):
+            new_d(e)
+            quantize(d_q[e], 0, da[e].rearrange("p i c -> p (i c)"))
 
-        def make_u(h, tag="z", bufs=2):
-            u = sbuf([P, W, HALF], F32, tag, bufs)
-            nc.scalar.activation(u, half_of(a1_sb[h // 2], h), ACT.Silu, scale=-1.0)
-            return u
+        def make_z(e, h):
+            z[e, h] = sbuf([P, W, HALF], F32, f"z{h}{e % 2}")
+            nc.scalar.activation(z[e, h], half_of(slot(e), h), ACT.Silu, scale=-1.0)
+            nc.scalar.activation(z[e, h], z[e, h], ACT.Identity, bias=1.0, scale=-1.0)
 
-        def make_z(h, u, dst):
-            z[h] = dst
-            nc.scalar.activation(dst, u, ACT.Identity, bias=1.0, scale=-1.0)
+        def make_x(e, h):
+            if (e, h) == (0, 0):
+                x[e, 0] = ring[:, :2, :].rearrange("p a (u c) -> p (a u) c", u=2)
+            elif e == 0:
+                x[e, 1] = sbuf([P, W, HALF], F32, "th_low")
+            elif h == 0:
+                both = in_turn([P, 2, W, HALF], F32, f"x{e}", e - 1)
+                x[e, 0], x[e, 1] = both[:, 0], both[:, 1]
+            nc.gpsimd.tensor_tensor(x[e, h], z[e, h], half_of(a3_sb[e], h), MULT)
 
-        def make_x(h, dst, engine=nc.gpsimd):
-            x[h] = dst
-            engine.tensor_tensor(x[h], z[h], half_of(a3_sb[h // 2], h), MULT)
-
-        def turn(src, tag, bufs):
-            bank = psum.tile([P, W, P], F32, name=tag, tag=tag, bufs=bufs)
+        def turn(src, tag):
+            dst = bank(tag, [P, W, P])
             for t in range(W):
-                nc.tensor.transpose(bank[:, t, :], src[:, t, :], ident[:])
-            return bank[:]
+                nc.tensor.transpose(dst[:, t, :], src[:, t, :], ident[:])
+            return dst
 
-        def planes_of(h):
-            return g_val[h // 2 + 2][:, h % 2 * 2 : h % 2 * 2 + 2, :]
+        def make_th(e, b, tag):
+            if (e, b // 2) not in th:
+                th[e, b // 2] = sbuf([P, 2, W, P], F32, ("th_low", "th_high")[b // 2])
+            a1_ps = turn(block_of(slot(e), b), tag)
+            nc.scalar.activation(th[e, b // 2][:, b % 2], a1_ps, ACT.Tanh, scale=0.5)
 
-        def across(h):
-            if h % 2 == 0:
-                g_val[h // 2 + 2] = sbuf([P, W, C], F32, "g_val", 2)
-            middle = planes_of(h).rearrange("p u c -> p (u c)")[:, HALF : HALF + C]
-            return middle.rearrange("p (t m) -> p t m", t=W)
-
-        def make_th(h, b, dst):
-            a1_ps = turn(block_of(half_of(a1_sb[h // 2], h), b), "a1_ps", 1)
-            th[h, b] = dst
-            nc.scalar.activation(th[h, b], a1_ps, ACT.Tanh, scale=0.5)
-
-        def first(h, b):
-            codes, scales = g_q[h // 2]
-            cols = slice((h % 2 * 2 + b) * P, (h % 2 * 2 + b + 1) * P)
-            dh[h, b] = psum.tile([P, H], F32, name="dh", tag="dh")
+        def first(e, b):
+            codes, scales = g_q[e]
+            cols = slice(b * P, (b + 1) * P)
+            dh[e, b] = bank(f"dh{b}", [P, H])
             nc.tensor.matmul_mx(
-                out=dh[h, b][:],
+                out=dh[e, b],
                 lhsT=codes[:, cols].bitcast(E5M2X4),
                 lhsT_scale=scales[:, cols],
-                rhs=w2_sb[:, h // 2].bitcast(E2M1X4),
-                rhs_scale=w2_sc[:, h // 2],
+                rhs=w2_sb[:, e].bitcast(E2M1X4),
+                rhs_scale=w2_sc[:, e],
                 start=True,
                 stop=True,
             )
 
-        def gated(h, b, tag="dr", bufs=2):
-            dr[h, b] = sbuf([P, W, P], F32, tag, bufs)
-            dh_tm = dh[h, b][:].rearrange("s (m t) -> s t m", t=W)
-            nc.vector.scalar_tensor_tensor(dr[h, b], th[h, b], 1.0, dh_tm, ADD, MULT)
-            dr_ps[h, b] = turn(dr[h, b], "dr_ps", 3)
+        def gated(e, b):
+            dr = th[e, b // 2][:, b % 2]
+            nc.vector.scalar_tensor_tensor(dr, dr, 1.0, dh[e, b].rearrange("s (m t) -> s t m", t=W), ADD, MULT)
+            dr_ps[e, b] = turn(dr, f"dr{b}")
 
-        def delta(h, b, i):
-            factor = half_of(a1_sb[h // 2], h) if i else x[h]
+        def delta(e, b, i):
+            factor = block_of(x[e, b // 2], b % 2) if i else block_of(slot(e), b)
             nc.vector.tensor_tensor(
-                into_runs(da[h][:, 1 - i, b * W * P : (b + 1) * W * P], 2),
-                by_runs(block_of(factor, b), 2),
-                by_runs(dr_ps[h, b], 2),
+                into_runs(da[e][:, i, b * W * P : (b + 1) * W * P], 2),
+                by_runs(factor, 2),
+                by_runs(dr_ps[e, b], 2),
                 MULT,
             )
 
-        def quantize_d(h):
-            if h % 2 == 0:
-                d_q[h // 2] = new_codes(2 * C, "d", 2)
-            for i in (1, 0):
-                quantize(d_q[h // 2], i * C + h % 2 * HALF, da[h][:, 1 - i])
-
-        def quantize_g(e):
-            g_q[e] = new_codes(C, f"g{e % 2}", 1)
-            quantize(g_q[e], 0, g_bf[e])
-
         def second_pass(e, kt, i, acc):
             codes, scales = d_q[e]
-            w, sc = ((w1_sb, w1_sc), (w3_sb, w3_sc))[i]
+            w, sc = ((w3_sb, w3_sc), (w1_sb, w1_sc))[i]
             nc.tensor.matmul_mx(
-                out=acc[:],
+                out=acc,
                 lhsT=w[:, e, 2 * P * kt : 2 * P * (kt + 1)].bitcast(E2M1X4),
                 lhsT_scale=sc[:, e, P * kt : P * (kt + 1)],
                 rhs=codes[:, i * C : (i + 1) * C].bitcast(E5M2X4),
                 rhs_scale=scales[:, i * C : (i + 1) * C],
-                start=i == 1,
-                stop=i == 0,
+                start=i == 0,
+                stop=i == 1,
             )
-            if i == 0:
-                nc.scalar.activation(dx[kt][:, e * C : (e + 1) * C], acc[:], ACT.Copy, scale=0.5)
+            if i == 1:
+                nc.scalar.activation(dx[kt][:, e * C : (e + 1) * C], acc, ACT.Copy, scale=0.5)
 
-        def second(e, kt):
-            acc = psum.tile([P, C], F32, name="acc", tag="acc", bufs=2)
-            for i in (1, 0):
-                second_pass(e, kt, i, acc)
+        def seconds(jobs):
+            for n, (e, kt) in enumerate(jobs):
+                acc = bank(f"dh{2 + n % 2}", [P, C])
+                for i in range(2):
+                    second_pass(e, kt, i, acc)
 
-        g_pair = sbuf([P, W, 2 * C], F32, "dx0")
-        g_val[1] = g_pair[:, :, C:]
-        for c0 in (0, C):
-            gather(g_pair[:, 0, c0 : c0 + C], 0, c0, c0 + C, gate_pair[:, c0 : c0 + C])
-        for t in range(1, W - 1):
-            gather(g_pair[:, t, :], t, 0, 2 * C, gate_pair)
-        g_first = [sbuf([P, W * HALF], BF16, "g_val", 2), sbuf([P, W * HALF], BF16, "dax2")]
-        make_th(0, 0, sbuf([P, W, P], F32, "z", 2))
-        make_th(0, 1, sbuf([P, W, P], F32, "g_val", 2))
-        u_first = make_u(0, "g_bf", 1)
-        make_z(0, u_first, u_first)
+        g_val[0] = sbuf([P, W, C], F32, "dx0")
+        g_val[1] = sbuf([P, W, C], F32, "dx1")
+        g_val[2] = ring[:, 2 : 2 + W, :]
+        for t in range(W):
+            for e in range(2):
+                gather(e, t)
+        u_first = sbuf([P, W, HALF], F32, "z00")
+        z[0, 0] = u_first
+        nc.scalar.activation(u_first, half_of(slot(0), 0), ACT.Silu, scale=-1.0)
         for b in range(2):
-            make_th(1, b, sbuf([P, W, P], F32, "th", 2))
-        u_second = make_u(1)
-        gather(g_pair[:, W - 1, :C], W - 1, 0, C, gate_pair[:, :C])
+            make_th(0, b, f"dr{b}")
+        nc.scalar.activation(u_first, u_first, ACT.Identity, bias=1.0, scale=-1.0)
+        flat = ring[:, :W, :].rearrange("p a c -> p (a c)")
+        g_first = [flat[:, 3 * C :].bitcast(BF16), flat[:, C + HALF : 2 * C + HALF].bitcast(BF16)]
         for h in range(2):
-            round_into(g_first[h], half_of(g_pair[:, :, :C], h))
-        gather(g_pair[:, W - 1, C:], W - 1, C, 2 * C, gate_pair[:, C:])
-        make_z(1, u_second, sbuf([P, W, HALF], F32, "gate_pair"))
-        g_q[0] = new_codes(C, "g0", 1)
-        quantize(g_q[0], 0, g_first[0])
-        g_val[2] = sbuf([P, W, C], F32, "g_val", 2)
-        make_x(0, planes_of(0).rearrange("p u (v c) -> p (u v) c", v=2), nc.vector)
-        quantize(g_q[0], HALF, g_first[1])
-        for b in range(2):
-            first(0, b)
-            gated(0, b)
-        dx = [flow.tile([P, S], F32, name=f"dx{kt}", tag=f"dx{kt}", align_bytes=64) for kt in range(KT)]
+            round_into(g_first[h], half_of(g_val[0], h))
+        for b in range(2, BLOCKS):
+            make_th(0, b, f"dr{b}")
+        make_z(0, 1)
+        g_q[0] = in_turn([P, C], U32, "g_codes0", 0), sbuf([P, C], U8, "g_scales0")
+        for h in range(2):
+            quantize(g_q[0], h * HALF, g_first[h])
+            gather(2, 1 - h)
+            for b in range(2):
+                first(0, 2 * h + b)
+        dx = {}
 
-        for h in range(HALVES):
-            e, odd = divmod(h, 2)
-            ahead = h + 1 < HALVES
-            gathers = e + 2 < E
-            if not odd:
-                if gathers:
-                    load_a3(e + 2)
-                if e + 3 < E:
-                    load_a1(e + 3)
-            if h == HALVES - 3:
-                wide = sbuf([P, 3, W * HALF], BF16, f"dax{h % 3}")
-                da[h] = wide[:, 1:]
-            else:
-                da[h] = sbuf([P, 2, W * HALF], BF16, f"dax{h % 3}")
-            if h == HALVES - 2:
-                make_x(h + 1, wide[:, :2].bitcast(F32).rearrange("p u (v c) -> p (u v) c", v=2))
-            elif ahead:
-                make_x(h + 1, sbuf([P, W, HALF], F32, f"dax{(h - 1) % 3}"))
-            if ahead:
-                for b in range(2):
-                    first(h + 1, b)
-            if h == 0:
-                gated(1, 0)
-                gated(1, 1, "g1_codes", 1)
-                g_bf[1] = sbuf([P, W * C], BF16, "g_bf")
-                round_into(g_bf[1], g_val[1])
-            if e:
-                for kt in range(odd * 2, 2 + odd):
-                    second(e - 1, kt)
-            if not ahead:
+        for e in range(E):
+            last = e == E - 1
+            make_x(e, 0)
+            for b in range(BLOCKS):
+                gated(e, b)
+            make_x(e, 1)
+            if not last:
+                round_g(e + 1)
+            if e == 0:
+                dx = [flow.tile([P, S], F32, name=f"dx{kt}", tag=f"dx{kt}", align_bytes=64) for kt in range(KT)]
+            if 0 < e < E - 2:
+                load_a1(e + 2)
+            for h in range(2):
+                if not last and (e + 1, h) not in z:
+                    make_z(e + 1, h)
+            if 0 < e < E - 2:
+                seconds([(e - 1, kt) for kt in range(KT)])
+            if last:
+                seconds([(late, kt) for kt in range(KT) for late in (e - 2, e - 1)])
+            da[e] = in_turn([P, 2, W * C], BF16, f"da{e}", e)
+            for pair in range(2):
+                for i in range(2):
+                    for b in (2 * pair, 2 * pair + 1):
+                        if not (last and i == 1 and b == BLOCKS - 1):
+                            delta(e, b, i)
+            if last:
                 break
-            delta(h, 0, 1)
-            if h + 2 == HALVES:
-                gated(h + 1, 0)
-            delta(h, 0, 0)
-            if h == 0:
-                delta(h, 1, 0)
-                delta(h, 1, 1)
-            elif h + 2 == HALVES:
-                gated(h + 1, 1)
-                delta(h, 1, 1)
-                delta(h, 1, 0)
+            if e + 2 < E:
+                load_a3(e + 2)
+            for b in (1, 2, 3, 0):
+                make_th(e + 1, b, f"dr{(b - 1) % BLOCKS}")
+            if e == E - 3:
+                make_z(E - 1, 0)
+            if e + 2 < E:
+                planes = list(range(W))
+                if e == 0:
+                    planes = planes[2:]
+                else:
+                    g_val[e + 2] = slot(e)
+                gather(e + 2, planes[0])
+                quantize_g(e + 1)
+                for t in planes[1:-1]:
+                    gather(e + 2, t)
+                quantize_d(e)
+                gather(e + 2, planes[-1])
             else:
-                gated(h + 1, 0)
-                delta(h, 1, 1)
-                gated(h + 1, 1)
-                delta(h, 1, 0)
-            if odd and 0 < e < E - 3:
-                load_gate(e + 3)
-            if h + 2 < HALVES:
-                if odd and e + 2 < E:
-                    make_th(h + 2, 0, sbuf([P, W, P], F32, f"g{e % 2}_codes"))
-                else:
-                    make_th(h + 2, 0, sbuf([P, W, P], F32, "th", 2))
-                if (h + 1) // 2 + 2 < E:
-                    make_th(h + 2, 1, across(h + 1))
-                else:
-                    make_th(h + 2, 1, sbuf([P, W, P], F32, "th", 2))
-                u = make_u(h + 2)
-                make_z(h + 2, u, u)
-            for t in range(2):
-                if gathers:
-                    gather(planes_of(h)[:, t, :], 2 * odd + t, (e + 2) * C, (e + 3) * C, gate_sb[e + 2])
-                if t == 0:
-                    if gathers and not odd:
-                        quantize_g(e + 1)
-                    quantize_d(h)
-                elif e + 2 == E and not odd:
-                    quantize_g(e + 1)
-            if gathers and odd:
-                g_bf[e + 2] = sbuf([P, W * C], BF16, "g_bf")
-                round_into(g_bf[e + 2], g_val[e + 2])
-        last = HALVES - 1
-        delta(last, 0, 1)
-        delta(last, 1, 1)
-        delta(last, 0, 0)
-        quantize(d_q[E - 1], C + HALF, da[last][:, 0])
-        delta(last, 1, 0)
-        for b in range(2):
-            quantize(d_q[E - 1], HALF + b * P, da[last][:, 1, b * W * P : (b + 1) * W * P])
-        accs = [psum.tile([P, C], F32, name="acc_last", tag="dh") for kt in range(KT)]
-        for kt, i in ((0, 1), (1, 1), (0, 0), (1, 0), (2, 1), (2, 0)):
-            second_pass(E - 1, kt, i, accs[kt])
+                quantize_g(e + 1)
+                quantize_d(e)
+            for b in range(BLOCKS):
+                first(e + 1, b)
 
-        y1 = [sbuf([P, T], F32, "a1", 3) for kt in range(KT)]
-        y2 = [sbuf([P, T], F32, tag, bufs) for tag, bufs in (("a3", 2), ("a3", 2), ("g_val", 2))]
+        e = E - 1
+        new_d(e)
+        quantize(d_q[e], 0, da[e][:, 0])
+        delta(e, BLOCKS - 1, 1)
+        for b0, b1 in ((0, 2), (2, 3), (3, 4)):
+            quantize(d_q[e], C + b0 * P, da[e][:, 1, b0 * W * P : b1 * W * P])
+        accs = [bank(tag, [P, C]) for tag in ("dh0", "dh1", "dr0")]
+        for kt, i in ((0, 0), (1, 0), (0, 1), (1, 1), (2, 0), (2, 1)):
+            second_pass(e, kt, i, accs[kt])
+
+        rows = [ring[:, 3 * n : 3 * n + 3, :].rearrange("p a c -> p (a c)") for n in range(4)]
+        y1 = rows[:KT]
+        y2 = [rows[KT]] + [sbuf([P, T], F32, f"a3_{n}") for n in range(2)]
 
         def fetch_first(kt):
             nc.vector.tensor_copy(y1[kt], dx[kt][:].indirect(pos1_sb[:]))

@@ -79,8 +79,9 @@ def tile_moe_bdx_glu_silu_kernel(
 
         turns = ctx.enter_context(tc.tile_pool(name="turns", bufs=1))
 
-        def in_turn(shape, dtype, name, side):
-            return turns.tile(shape, dtype, name=name, tag=name, align_bytes=64, offset=side % 2 * 4 * W * C)[:]
+        def in_turn(shape, dtype, name, side, h=0):
+            offset = 4 * W * (side % 2 * C + h * HALF)
+            return turns.tile(shape, dtype, name=name, tag=name, align_bytes=64, offset=offset)[:]
 
         a3_sb = {}
 
@@ -98,16 +99,16 @@ def tile_moe_bdx_glu_silu_kernel(
         def load_dy(t):
             nc.sync.dma_start(out=dy[t][:], in_=dy_rows[t])
 
-        nc.sync.dma_start(offs_sb[:], offs)
         load_dy(0)
+        nc.sync.dma_start(offs_sb[:], offs)
         load_gate(0)
         load_gate(1)
         load_dy(1)
-        load_dy(2)
         load_a1(0, 0, HALF)
-        load_dy(3)
-        load_a1(0, HALF, C)
         load_gate(2)
+        load_dy(2)
+        load_a1(0, HALF, C)
+        load_dy(3)
         load_words(w2_sb, w2_words, 0, 2)
         load_scales(w2_sc, w2_scales)
         load_a3(0, 0, HALF)
@@ -138,8 +139,8 @@ def tile_moe_bdx_glu_silu_kernel(
         def block_of(ap, b):
             return ap[:, :, b * P : (b + 1) * P]
 
-        def bank(tag, shape):
-            return psum.tile(shape, F32, name=tag, tag=tag)[:]
+        def bank(name, shape, index):
+            return psum.tile(shape, F32, name=name, tag=name, offset=index * 4 * C)[:]
 
         g_val, g_bf, g_q, d_q = {}, {}, {}, {}
         z, x, th, dh, dr_ps, da = {}, {}, {}, {}, {}, {}
@@ -160,7 +161,7 @@ def tile_moe_bdx_glu_silu_kernel(
             nc.vector.quantize_mx(out=q[0][:, cols].bitcast(E5M2X4), scales=q[1][:, cols], in_=bf)
 
         def quantize_g(e):
-            g_q[e] = in_turn([P, C], U32, f"g_codes{e}", e), sbuf([P, C], U8, f"g_scales{e % 2}")
+            g_q[e] = in_turn([P, C], U32, f"g_codes{e}", e, 1), sbuf([P, C], U8, f"g_scales{e % 2}")
             quantize(g_q[e], 0, g_bf[e])
 
         def new_d(e):
@@ -168,7 +169,7 @@ def tile_moe_bdx_glu_silu_kernel(
 
         def quantize_d(e):
             new_d(e)
-            quantize(d_q[e], 0, da[e].rearrange("p i c -> p (i c)"))
+            quantize(d_q[e], 0, da[e])
 
         def make_z(e, h):
             z[e, h] = sbuf([P, W, HALF], F32, f"z{h}{e % 2}")
@@ -178,29 +179,26 @@ def tile_moe_bdx_glu_silu_kernel(
         def make_x(e, h):
             if (e, h) == (0, 0):
                 x[e, 0] = ring[:, :2, :].rearrange("p a (u c) -> p (a u) c", u=2)
-            elif e == 0:
-                x[e, 1] = sbuf([P, W, HALF], F32, "th_low")
-            elif h == 0:
-                both = in_turn([P, 2, W, HALF], F32, f"x{e}", e - 1)
-                x[e, 0], x[e, 1] = both[:, 0], both[:, 1]
+            else:
+                x[e, h] = in_turn([P, W, HALF], F32, f"x{e}{h}", e - 1, h)
             nc.gpsimd.tensor_tensor(x[e, h], z[e, h], half_of(a3_sb[e], h), MULT)
 
-        def turn(src, tag):
-            dst = bank(tag, [P, W, P])
+        def turn(src, name, index):
+            dst = bank(name, [P, W, P], index)
             for t in range(W):
                 nc.tensor.transpose(dst[:, t, :], src[:, t, :], ident[:])
             return dst
 
-        def make_th(e, b, tag):
+        def make_th(e, b, index):
             if (e, b // 2) not in th:
                 th[e, b // 2] = sbuf([P, 2, W, P], F32, ("th_low", "th_high")[b // 2])
-            a1_ps = turn(block_of(slot(e), b), tag)
+            a1_ps = turn(block_of(slot(e), b), f"a1_ps{e}{b}", index)
             nc.scalar.activation(th[e, b // 2][:, b % 2], a1_ps, ACT.Tanh, scale=0.5)
 
         def first(e, b):
             codes, scales = g_q[e]
             cols = slice(b * P, (b + 1) * P)
-            dh[e, b] = bank(f"dh{b}", [P, H])
+            dh[e, b] = bank(f"dh{e}{b}", [P, H], b)
             nc.tensor.matmul_mx(
                 out=dh[e, b],
                 lhsT=codes[:, cols].bitcast(E5M2X4),
@@ -214,14 +212,30 @@ def tile_moe_bdx_glu_silu_kernel(
         def gated(e, b):
             dr = th[e, b // 2][:, b % 2]
             nc.vector.scalar_tensor_tensor(dr, dr, 1.0, dh[e, b].rearrange("s (m t) -> s t m", t=W), ADD, MULT)
-            dr_ps[e, b] = turn(dr, f"dr{b}")
+            dr_ps[e, b] = turn(dr, f"dr_ps{e}{b}", BLOCKS + b)
+
+        def da_of(e, i, b0, b1):
+            return da[e][:, (i * BLOCKS + b0) * W * P : (i * BLOCKS + b1) * W * P]
 
         def delta(e, b, i):
             factor = block_of(x[e, b // 2], b % 2) if i else block_of(slot(e), b)
             nc.vector.tensor_tensor(
-                into_runs(da[e][:, i, b * W * P : (b + 1) * W * P], 2),
+                into_runs(da_of(e, i, b, b + 1), 2),
                 by_runs(factor, 2),
                 by_runs(dr_ps[e, b], 2),
+                MULT,
+            )
+
+        def delta_aside(e, b):
+            woven = sbuf([P, P, W], F32, "woven")
+            nc.scalar.copy(woven, dr_ps[e, b].rearrange("p t c -> p c t"))
+            return woven
+
+        def delta_woven(e, b, woven):
+            nc.gpsimd.tensor_tensor(
+                da_of(e, 0, b, b + 1).rearrange("p (c t) -> p c t", t=W),
+                woven,
+                block_of(slot(e), b).rearrange("p t c -> p c t"),
                 MULT,
             )
 
@@ -240,11 +254,13 @@ def tile_moe_bdx_glu_silu_kernel(
             if i == 1:
                 nc.scalar.activation(dx[kt][:, e * C : (e + 1) * C], acc, ACT.Copy, scale=0.5)
 
-        def seconds(jobs):
-            for n, (e, kt) in enumerate(jobs):
-                acc = bank(f"dh{2 + n % 2}", [P, C])
+        def seconds(jobs, accs):
+            for (e, kt), acc in zip(jobs, accs):
                 for i in range(2):
                     second_pass(e, kt, i, acc)
+
+        def three_banks(e):
+            return [bank(f"acc{e}{n}", [P, C], BLOCKS - 1 + n) for n in range(KT)]
 
         g_val[0] = sbuf([P, W, C], F32, "dx0")
         g_val[1] = sbuf([P, W, C], F32, "dx1")
@@ -252,23 +268,29 @@ def tile_moe_bdx_glu_silu_kernel(
         for t in range(W):
             for e in range(2):
                 gather(e, t)
+            if t == 1:
+                gather(2, 0)
         u_first = sbuf([P, W, HALF], F32, "z00")
         z[0, 0] = u_first
         nc.scalar.activation(u_first, half_of(slot(0), 0), ACT.Silu, scale=-1.0)
         for b in range(2):
-            make_th(0, b, f"dr{b}")
+            make_th(0, b, BLOCKS + b)
         nc.scalar.activation(u_first, u_first, ACT.Identity, bias=1.0, scale=-1.0)
         flat = ring[:, :W, :].rearrange("p a c -> p (a c)")
-        g_first = [flat[:, 3 * C :].bitcast(BF16), flat[:, C + HALF : 2 * C + HALF].bitcast(BF16)]
+        g_first = [flat[:, 3 * C :].bitcast(BF16), flat[:, C : 2 * C].bitcast(BF16)]
+        for b in range(2, BLOCKS):
+            make_th(0, b, BLOCKS + b)
+        u_second = sbuf([P, W, HALF], F32, "z10")
+        nc.scalar.activation(u_second, half_of(slot(0), 1), ACT.Silu, scale=-1.0)
         for h in range(2):
             round_into(g_first[h], half_of(g_val[0], h))
-        for b in range(2, BLOCKS):
-            make_th(0, b, f"dr{b}")
-        make_z(0, 1)
+        z[0, 1] = half_of(g_val[0], 0)
+        nc.scalar.activation(z[0, 1], u_second, ACT.Identity, bias=1.0, scale=-1.0)
         g_q[0] = in_turn([P, C], U32, "g_codes0", 0), sbuf([P, C], U8, "g_scales0")
         for h in range(2):
             quantize(g_q[0], h * HALF, g_first[h])
-            gather(2, 1 - h)
+            if h == 0:
+                gather(2, 1)
             for b in range(2):
                 first(0, 2 * h + b)
         dx = {}
@@ -279,8 +301,10 @@ def tile_moe_bdx_glu_silu_kernel(
             for b in range(BLOCKS):
                 gated(e, b)
             make_x(e, 1)
+            da[e] = in_turn([P, 2 * W * C], BF16, f"da{e}", e)
             if not last:
                 round_g(e + 1)
+                woven = delta_aside(e, 1)
             if e == 0:
                 dx = [flow.tile([P, S], F32, name=f"dx{kt}", tag=f"dx{kt}", align_bytes=64) for kt in range(KT)]
             if 0 < e < E - 2:
@@ -288,22 +312,25 @@ def tile_moe_bdx_glu_silu_kernel(
             for h in range(2):
                 if not last and (e + 1, h) not in z:
                     make_z(e + 1, h)
-            if 0 < e < E - 2:
-                seconds([(e - 1, kt) for kt in range(KT)])
-            if last:
-                seconds([(late, kt) for kt in range(KT) for late in (e - 2, e - 1)])
-            da[e] = in_turn([P, 2, W * C], BF16, f"da{e}", e)
             for pair in range(2):
                 for i in range(2):
                     for b in (2 * pair, 2 * pair + 1):
-                        if not (last and i == 1 and b == BLOCKS - 1):
+                        if (b, i) != ((BLOCKS - 1, 1) if last else (1, 0)):
                             delta(e, b, i)
+                        elif not last:
+                            delta_woven(e, b, woven)
+                if pair == 0 and 0 < e < E - 2:
+                    seconds([(e - 1, kt) for kt in range(KT)], three_banks(e))
+                if pair == 0 and last:
+                    seconds([(e - 1, 0), (e - 2, 1), (e - 1, 1)], three_banks(e))
+                if pair == 0 and e == E - 2:
+                    seconds([(e - 1, 0)], [bank("acc_one", [P, C], BLOCKS - 1)])
             if last:
                 break
             if e + 2 < E:
                 load_a3(e + 2)
-            for b in (1, 2, 3, 0):
-                make_th(e + 1, b, f"dr{(b - 1) % BLOCKS}")
+            for n in range(BLOCKS):
+                make_th(e + 1, n, BLOCKS + (n + 2) % BLOCKS)
             if e == E - 3:
                 make_z(E - 1, 0)
             if e + 2 < E:
@@ -326,13 +353,16 @@ def tile_moe_bdx_glu_silu_kernel(
 
         e = E - 1
         new_d(e)
-        quantize(d_q[e], 0, da[e][:, 0])
+        quantize(d_q[e], 0, da_of(e, 0, 0, BLOCKS))
         delta(e, BLOCKS - 1, 1)
         for b0, b1 in ((0, 2), (2, 3), (3, 4)):
-            quantize(d_q[e], C + b0 * P, da[e][:, 1, b0 * W * P : b1 * W * P])
-        accs = [bank(tag, [P, C]) for tag in ("dh0", "dh1", "dr0")]
-        for kt, i in ((0, 0), (1, 0), (0, 1), (1, 1), (2, 0), (2, 1)):
+            quantize(d_q[e], C + b0 * P, da_of(e, 1, b0, b1))
+        places = (0, BLOCKS + 2)
+        accs = [bank(f"acc_last{kt}", [P, C], places[kt]) for kt in range(2)]
+        for kt, i in ((0, 0), (1, 0), (0, 1), (1, 1)):
             second_pass(e, kt, i, accs[kt])
+        for n in range(3):
+            seconds([(e - 2 + n, KT - 1)], [bank(f"acc_late{n}", [P, C], places[n % 2])])
 
         rows = [ring[:, 3 * n : 3 * n + 3, :].rearrange("p a c -> p (a c)") for n in range(4)]
         y1 = rows[:KT]

@@ -53,9 +53,9 @@ def tile_moe_bdx_glu_silu_kernel(
         w3_sc = keep.tile([P, E, K], U8, name="w3_sc", align_bytes=64)
         ident = keep.tile([P, P], F32, name="ident")
 
-        for plane in (w2_sc, w1_sc, w3_sc):
-            nc.gpsimd.memset(plane[:].rearrange("p e i -> p (e i)").bitcast(U32), 0)
         make_identity(nc, ident[:])
+        for plane in (w2_sc, w1_sc, w3_sc):
+            nc.vector.memset(plane[:].rearrange("p e i -> p (e i)").bitcast(U32), 0)
 
         dy_rows = dyT.rearrange("(p t) c -> t p c", t=W)
         a1_rows = a1.rearrange("(p t) c -> p t c", t=W)
@@ -83,6 +83,7 @@ def tile_moe_bdx_glu_silu_kernel(
             offset = 4 * W * (side % 2 * C + h * HALF)
             return turns.tile(shape, dtype, name=name, tag=name, align_bytes=64, offset=offset)[:]
 
+        low = ctx.enter_context(tc.tile_pool(name="low", bufs=1))
         a3_sb = {}
 
         def load_a1(e, c0=0, c1=C):
@@ -93,19 +94,20 @@ def tile_moe_bdx_glu_silu_kernel(
                 a3_sb[e] = sbuf([P, W, C], F32, f"a3_{e % 2}")
             nc.sync.dma_start(out=a3_sb[e][:, :, c0:c1], in_=a3_rows[:, :, e * C + c0 : e * C + c1])
 
-        def load_gate(e):
-            nc.sync.dma_start(out=gate_sb[e][:], in_=gate[:P, e * C : (e + 1) * C])
+        gate_col = keep.tile([P, E, 2 * W], F32, name="gate_col")
+
+        def load_gates(e0, e1):
+            row = gate[0, e0 * C : e1 * C].rearrange("(e p t) -> p e t", p=P, t=W)
+            nc.sync.dma_start(out=gate_col[:, e0:e1, :W], in_=row)
 
         def load_dy(t):
             nc.sync.dma_start(out=dy[t][:], in_=dy_rows[t])
 
+        load_gates(0, 4)
         load_dy(0)
         nc.sync.dma_start(offs_sb[:], offs)
-        load_gate(0)
-        load_gate(1)
         load_dy(1)
         load_a1(0, 0, HALF)
-        load_gate(2)
         load_dy(2)
         load_a1(0, HALF, C)
         load_dy(3)
@@ -120,10 +122,8 @@ def tile_moe_bdx_glu_silu_kernel(
         load_words(w3_sb, w3_words)
         load_scales(w1_sc, w1_scales)
         load_scales(w3_sc, w3_scales)
-        load_gate(3)
+        load_gates(4, E)
         load_words(w2_sb, w2_words, 2, E)
-        load_gate(4)
-        load_gate(5)
         nc.sync.dma_start(pos1_sb[:], pos1)
         nc.sync.dma_start(pos2_sb[:], pos2)
 
@@ -145,6 +145,12 @@ def tile_moe_bdx_glu_silu_kernel(
         g_val, g_bf, g_q, d_q = {}, {}, {}, {}
         z, x, th, dh, dr_ps, da = {}, {}, {}, {}, {}, {}
 
+        def spread_gate(e, index, copy):
+            rows = bank(f"gate_ps{e}", [P, W, P], index)
+            for t in range(W):
+                nc.tensor.transpose(rows[:, t, :], gate_col[:, e, t : t + 1].to_broadcast([P, P]), ident[:])
+            copy(gate_sb[e][:].rearrange("p (c t) -> p c t", t=W), rows.rearrange("p t c -> p c t"))
+
         def gather(e, t):
             lists = offs_sb[:, e * C // 16 : (e + 1) * C // 16]
             nc.vector.tensor_tensor(g_val[e][:, t, :], dy[t][:].indirect(lists), gate_sb[e][:], MULT)
@@ -153,7 +159,8 @@ def tile_moe_bdx_glu_silu_kernel(
             nc.scalar.copy(into_runs(dst, 4), by_runs(src, 4))
 
         def round_g(e):
-            g_bf[e] = sbuf([P, W * C], BF16, "g_bf")
+            place = 0 if 1 < e < E - 1 else 8 * W * HALF
+            g_bf[e] = low.tile([P, W * C], BF16, name=f"g_bf{e}", tag=f"g_bf{e}", align_bytes=64, offset=place)[:]
             round_into(g_bf[e], g_val[e])
 
         def quantize(q, c0, bf):
@@ -165,7 +172,7 @@ def tile_moe_bdx_glu_silu_kernel(
             quantize(g_q[e], 0, g_bf[e])
 
         def new_d(e):
-            d_q[e] = sbuf([P, 2 * C], U32, f"d_codes{e % 3}"), sbuf([P, 2 * C], U8, f"d_scales{e % 3}")
+            d_q[e] = sbuf([P, 2 * C], U32, f"d_codes{e % 4}"), sbuf([P, 2 * C], U8, f"d_scales{e % 4}")
 
         def quantize_d(e):
             new_d(e)
@@ -191,7 +198,9 @@ def tile_moe_bdx_glu_silu_kernel(
 
         def make_th(e, b, index):
             if (e, b // 2) not in th:
-                th[e, b // 2] = sbuf([P, 2, W, P], F32, ("th_low", "th_high")[b // 2])
+                name = f"th{e}{b // 2}"
+                place = 4 * W * HALF * (b // 2)
+                th[e, b // 2] = low.tile([P, 2, W, P], F32, name=name, tag=name, align_bytes=64, offset=place)[:]
             a1_ps = turn(block_of(slot(e), b), f"a1_ps{e}{b}", index)
             nc.scalar.activation(th[e, b // 2][:, b % 2], a1_ps, ACT.Tanh, scale=0.5)
 
@@ -239,7 +248,7 @@ def tile_moe_bdx_glu_silu_kernel(
                 MULT,
             )
 
-        def second_pass(e, kt, i, acc):
+        def second_pass(e, kt, i, acc, opens=0):
             codes, scales = d_q[e]
             w, sc = ((w3_sb, w3_sc), (w1_sb, w1_sc))[i]
             nc.tensor.matmul_mx(
@@ -248,10 +257,10 @@ def tile_moe_bdx_glu_silu_kernel(
                 lhsT_scale=sc[:, e, P * kt : P * (kt + 1)],
                 rhs=codes[:, i * C : (i + 1) * C].bitcast(E5M2X4),
                 rhs_scale=scales[:, i * C : (i + 1) * C],
-                start=i == 0,
-                stop=i == 1,
+                start=i == opens,
+                stop=i != opens,
             )
-            if i == 1:
+            if i != opens:
                 nc.scalar.activation(dx[kt][:, e * C : (e + 1) * C], acc, ACT.Copy, scale=0.5)
 
         def seconds(jobs, accs):
@@ -262,6 +271,8 @@ def tile_moe_bdx_glu_silu_kernel(
         def three_banks(e):
             return [bank(f"acc{e}{n}", [P, C], BLOCKS - 1 + n) for n in range(KT)]
 
+        for e in range(4):
+            spread_gate(e, e, nc.vector.tensor_copy if e < 2 else nc.scalar.copy)
         g_val[0] = sbuf([P, W, C], F32, "dx0")
         g_val[1] = sbuf([P, W, C], F32, "dx1")
         g_val[2] = ring[:, 2 : 2 + W, :]
@@ -303,8 +314,13 @@ def tile_moe_bdx_glu_silu_kernel(
             make_x(e, 1)
             da[e] = in_turn([P, 2 * W * C], BF16, f"da{e}", e)
             if not last:
-                round_g(e + 1)
+                if e in (0, E - 2):
+                    round_g(e + 1)
                 woven = delta_aside(e, 1)
+                if e not in (0, E - 2):
+                    round_g(e + 1)
+            if 0 < e < E - 3:
+                spread_gate(e + 3, 2, nc.scalar.copy)
             if e == 0:
                 dx = [flow.tile([P, S], F32, name=f"dx{kt}", tag=f"dx{kt}", align_bytes=64) for kt in range(KT)]
             if 0 < e < E - 2:
@@ -320,11 +336,9 @@ def tile_moe_bdx_glu_silu_kernel(
                         elif not last:
                             delta_woven(e, b, woven)
                 if pair == 0 and 0 < e < E - 2:
-                    seconds([(e - 1, kt) for kt in range(KT)], three_banks(e))
+                    seconds([(e - 1, kt) for kt in range(KT if e < E - 3 else KT - 1)], three_banks(e))
                 if pair == 0 and last:
-                    seconds([(e - 1, 0), (e - 2, 1), (e - 1, 1)], three_banks(e))
-                if pair == 0 and e == E - 2:
-                    seconds([(e - 1, 0)], [bank("acc_one", [P, C], BLOCKS - 1)])
+                    seconds([(e - 2, 0), (e - 1, 0), (e - 2, 1)], three_banks(e))
             if last:
                 break
             if e + 2 < E:
@@ -352,33 +366,36 @@ def tile_moe_bdx_glu_silu_kernel(
                 first(e + 1, b)
 
         e = E - 1
+        seconds([(e - 1, 1)], [bank("acc_fourth", [P, C], BLOCKS + 2)])
         new_d(e)
         quantize(d_q[e], 0, da_of(e, 0, 0, BLOCKS))
         delta(e, BLOCKS - 1, 1)
         for b0, b1 in ((0, 2), (2, 3), (3, 4)):
             quantize(d_q[e], C + b0 * P, da_of(e, 1, b0, b1))
-        places = (0, BLOCKS + 2)
+        places = (0, BLOCKS + 3)
         accs = [bank(f"acc_last{kt}", [P, C], places[kt]) for kt in range(2)]
-        for kt, i in ((0, 0), (1, 0), (0, 1), (1, 1)):
-            second_pass(e, kt, i, accs[kt])
-        for n in range(3):
-            seconds([(e - 2 + n, KT - 1)], [bank(f"acc_late{n}", [P, C], places[n % 2])])
+        for kt, i in ((0, 0), (0, 1), (1, 1), (1, 0)):
+            second_pass(e, kt, i, accs[kt], opens=kt)
+        for n in range(4):
+            seconds([(E - 4 + n, KT - 1)], [bank(f"acc_late{n}", [P, C], places[n % 2])])
 
         rows = [ring[:, 3 * n : 3 * n + 3, :].rearrange("p a c -> p (a c)") for n in range(4)]
         y1 = rows[:KT]
         y2 = [rows[KT]] + [sbuf([P, T], F32, f"a3_{n}") for n in range(2)]
 
-        def fetch_first(kt):
-            nc.vector.tensor_copy(y1[kt], dx[kt][:].indirect(pos1_sb[:]))
+        def fetch_first(kt, c0=0, c1=T):
+            nc.vector.tensor_copy(y1[kt][:, c0:c1], dx[kt][:].indirect(pos1_sb[:, c0 // 16 : c1 // 16]))
 
         def add_second(kt, c0, c1):
             lists = pos2_sb[:, c0 // 16 : c1 // 16]
             nc.vector.tensor_tensor(y2[kt][:, c0:c1], dx[kt][:].indirect(lists), y1[kt][:, c0:c1], ADD)
             nc.sync.dma_start(out=out[kt * P : (kt + 1) * P, c0:c1], in_=y2[kt][:, c0:c1])
 
-        fetch_first(0)
-        for kt in range(1, KT):
+        for kt in range(KT - 1):
             fetch_first(kt)
-            add_second(kt - 1, 0, T)
+        for kt in range(KT - 1):
+            add_second(kt, 0, T)
+        fetch_first(KT - 1, 0, T // 2)
+        fetch_first(KT - 1, T // 2, T)
         for c0, c1 in ((0, T // 2), (T // 2, T - HALF), (T - HALF, T)):
             add_second(KT - 1, c0, c1)

@@ -27,6 +27,7 @@ W = 4
 KT = K // P
 HALF = C // 2
 BLOCKS = C // P
+ASIDE = 96
 
 
 def tile_moe_bdx_glu_silu_kernel(
@@ -94,20 +95,25 @@ def tile_moe_bdx_glu_silu_kernel(
                 a3_sb[e] = sbuf([P, W, C], F32, f"a3_{e % 2}")
             nc.sync.dma_start(out=a3_sb[e][:, :, c0:c1], in_=a3_rows[:, :, e * C + c0 : e * C + c1])
 
-        gate_col = keep.tile([P, E, 2 * W], F32, name="gate_col")
+        gate_col = {}
 
-        def load_gates(e0, e1):
+        def load_gates(e0, e1, place):
+            cols = place.rearrange("p (e t) -> p e t", t=2 * W)
             row = gate[0, e0 * C : e1 * C].rearrange("(e p t) -> p e t", p=P, t=W)
-            nc.sync.dma_start(out=gate_col[:, e0:e1, :W], in_=row)
+            nc.sync.dma_start(out=cols[:, :, :W], in_=row)
+            for e in range(e0, e1):
+                gate_col[e] = cols[:, e - e0, :]
 
         def load_dy(t):
             nc.sync.dma_start(out=dy[t][:], in_=dy_rows[t])
 
-        load_gates(0, 4)
+        u_first = sbuf([P, W, HALF], F32, "z00")
+        load_gates(0, 4, u_first[:, 1, : 4 * 2 * W])
+        nc.sync.dma_start(out=slot(0)[:, 0, :HALF], in_=a1_rows[:, 0, :HALF])
         load_dy(0)
         nc.sync.dma_start(offs_sb[:], offs)
         load_dy(1)
-        load_a1(0, 0, HALF)
+        nc.sync.dma_start(out=slot(0)[:, 1:, :HALF], in_=a1_rows[:, 1:, :HALF])
         load_dy(2)
         load_a1(0, HALF, C)
         load_dy(3)
@@ -122,7 +128,7 @@ def tile_moe_bdx_glu_silu_kernel(
         load_words(w3_sb, w3_words)
         load_scales(w1_sc, w1_scales)
         load_scales(w3_sc, w3_scales)
-        load_gates(4, E)
+        load_gates(4, E, sbuf([P, 2 * 2 * W], F32, "late_gates"))
         load_words(w2_sb, w2_words, 2, E)
         nc.sync.dma_start(pos1_sb[:], pos1)
         nc.sync.dma_start(pos2_sb[:], pos2)
@@ -148,7 +154,7 @@ def tile_moe_bdx_glu_silu_kernel(
         def spread_gate(e, index, copy):
             rows = bank(f"gate_ps{e}", [P, W, P], index)
             for t in range(W):
-                nc.tensor.transpose(rows[:, t, :], gate_col[:, e, t : t + 1].to_broadcast([P, P]), ident[:])
+                nc.tensor.transpose(rows[:, t, :], gate_col[e][:, t : t + 1].to_broadcast([P, P]), ident[:])
             copy(gate_sb[e][:].rearrange("p (c t) -> p c t", t=W), rows.rearrange("p t c -> p c t"))
 
         def gather(e, t):
@@ -178,9 +184,11 @@ def tile_moe_bdx_glu_silu_kernel(
             new_d(e)
             quantize(d_q[e], 0, da[e])
 
-        def make_z(e, h):
+        def begin_z(e, h):
             z[e, h] = sbuf([P, W, HALF], F32, f"z{h}{e % 2}")
             nc.scalar.activation(z[e, h], half_of(slot(e), h), ACT.Silu, scale=-1.0)
+
+        def finish_z(e, h):
             nc.scalar.activation(z[e, h], z[e, h], ACT.Identity, bias=1.0, scale=-1.0)
 
         def make_x(e, h):
@@ -226,25 +234,25 @@ def tile_moe_bdx_glu_silu_kernel(
         def da_of(e, i, b0, b1):
             return da[e][:, (i * BLOCKS + b0) * W * P : (i * BLOCKS + b1) * W * P]
 
-        def delta(e, b, i):
+        def delta(e, b, i, c0=0):
             factor = block_of(x[e, b // 2], b % 2) if i else block_of(slot(e), b)
             nc.vector.tensor_tensor(
-                into_runs(da_of(e, i, b, b + 1), 2),
-                by_runs(factor, 2),
-                by_runs(dr_ps[e, b], 2),
+                into_runs(da_of(e, i, b, b + 1)[:, W * c0 :], 2),
+                by_runs(factor[:, :, c0:], 2),
+                by_runs(dr_ps[e, b][:, :, c0:], 2),
                 MULT,
             )
 
         def delta_aside(e, b):
-            woven = sbuf([P, P, W], F32, "woven")
-            nc.scalar.copy(woven, dr_ps[e, b].rearrange("p t c -> p c t"))
+            woven = sbuf([P, ASIDE, W], F32, "woven")
+            nc.scalar.copy(woven, dr_ps[e, b][:, :, :ASIDE].rearrange("p t c -> p c t"))
             return woven
 
         def delta_woven(e, b, woven):
             nc.gpsimd.tensor_tensor(
-                da_of(e, 0, b, b + 1).rearrange("p (c t) -> p c t", t=W),
+                da_of(e, 0, b, b + 1)[:, : W * ASIDE].rearrange("p (c t) -> p c t", t=W),
                 woven,
-                block_of(slot(e), b).rearrange("p t c -> p c t"),
+                block_of(slot(e), b)[:, :, :ASIDE].rearrange("p t c -> p c t"),
                 MULT,
             )
 
@@ -271,8 +279,9 @@ def tile_moe_bdx_glu_silu_kernel(
         def three_banks(e):
             return [bank(f"acc{e}{n}", [P, C], BLOCKS - 1 + n) for n in range(KT)]
 
+        nc.scalar.activation(u_first[:, 0], slot(0)[:, 0, :HALF], ACT.Silu, scale=-1.0)
         for e in range(4):
-            spread_gate(e, e, nc.vector.tensor_copy if e < 2 else nc.scalar.copy)
+            spread_gate(e, e, nc.vector.tensor_copy if e == 0 else nc.scalar.copy)
         g_val[0] = sbuf([P, W, C], F32, "dx0")
         g_val[1] = sbuf([P, W, C], F32, "dx1")
         g_val[2] = ring[:, 2 : 2 + W, :]
@@ -281,9 +290,8 @@ def tile_moe_bdx_glu_silu_kernel(
                 gather(e, t)
             if t == 1:
                 gather(2, 0)
-        u_first = sbuf([P, W, HALF], F32, "z00")
         z[0, 0] = u_first
-        nc.scalar.activation(u_first, half_of(slot(0), 0), ACT.Silu, scale=-1.0)
+        nc.scalar.activation(u_first[:, 1:], slot(0)[:, 1:, :HALF], ACT.Silu, scale=-1.0)
         for b in range(2):
             make_th(0, b, BLOCKS + b)
         nc.scalar.activation(u_first, u_first, ACT.Identity, bias=1.0, scale=-1.0)
@@ -313,12 +321,11 @@ def tile_moe_bdx_glu_silu_kernel(
                 gated(e, b)
             make_x(e, 1)
             da[e] = in_turn([P, 2 * W * C], BF16, f"da{e}", e)
-            if not last:
-                if e in (0, E - 2):
-                    round_g(e + 1)
-                woven = delta_aside(e, 1)
-                if e not in (0, E - 2):
-                    round_g(e + 1)
+            if e in (0, E - 2):
+                round_g(e + 1)
+            woven = delta_aside(e, 1)
+            if 0 < e < E - 2:
+                round_g(e + 1)
             if 0 < e < E - 3:
                 spread_gate(e + 3, 2, nc.scalar.copy)
             if e == 0:
@@ -326,14 +333,17 @@ def tile_moe_bdx_glu_silu_kernel(
             if 0 < e < E - 2:
                 load_a1(e + 2)
             for h in range(2):
-                if not last and (e + 1, h) not in z:
-                    make_z(e + 1, h)
+                if not last:
+                    if (e + 1, h) not in z:
+                        begin_z(e + 1, h)
+                    finish_z(e + 1, h)
             for pair in range(2):
                 for i in range(2):
                     for b in (2 * pair, 2 * pair + 1):
-                        if (b, i) != ((BLOCKS - 1, 1) if last else (1, 0)):
+                        if (b, i) != (1, 0):
                             delta(e, b, i)
-                        elif not last:
+                        else:
+                            delta(e, b, i, ASIDE)
                             delta_woven(e, b, woven)
                 if pair == 0 and 0 < e < E - 2:
                     seconds([(e - 1, kt) for kt in range(KT if e < E - 3 else KT - 1)], three_banks(e))
@@ -346,7 +356,7 @@ def tile_moe_bdx_glu_silu_kernel(
             for n in range(BLOCKS):
                 make_th(e + 1, n, BLOCKS + (n + 2) % BLOCKS)
             if e == E - 3:
-                make_z(E - 1, 0)
+                begin_z(E - 1, 0)
             if e + 2 < E:
                 planes = list(range(W))
                 if e == 0:
@@ -368,10 +378,8 @@ def tile_moe_bdx_glu_silu_kernel(
         e = E - 1
         seconds([(e - 1, 1)], [bank("acc_fourth", [P, C], BLOCKS + 2)])
         new_d(e)
-        quantize(d_q[e], 0, da_of(e, 0, 0, BLOCKS))
-        delta(e, BLOCKS - 1, 1)
-        for b0, b1 in ((0, 2), (2, 3), (3, 4)):
-            quantize(d_q[e], C + b0 * P, da_of(e, 1, b0, b1))
+        for i in range(2):
+            quantize(d_q[e], i * C, da_of(e, i, 0, BLOCKS))
         places = (0, BLOCKS + 3)
         accs = [bank(f"acc_last{kt}", [P, C], places[kt]) for kt in range(2)]
         for kt, i in ((0, 0), (0, 1), (1, 1), (1, 0)):

@@ -27,7 +27,17 @@ W = 4
 KT = K // P
 HALF = C // 2
 BLOCKS = C // P
-ASIDE = 96
+HALVES = 2 * E
+
+WHOLE = 4 * W * C
+A1_AT = 0
+A3_AT = A1_AT + E * WHOLE
+U_AT = A3_AT + 3 * WHOLE
+TH_AT = U_AT + WHOLE
+SIDE_AT = TH_AT + WHOLE
+GV_AT = SIDE_AT + 3 * WHOLE
+GB_AT = GV_AT + WHOLE
+DX_AT = GB_AT + WHOLE // 2
 
 
 def tile_moe_bdx_glu_silu_kernel(
@@ -37,10 +47,17 @@ def tile_moe_bdx_glu_silu_kernel(
     with ExitStack() as ctx:
         keep = ctx.enter_context(tc.tile_pool(name="keep", bufs=1))
         flow = ctx.enter_context(tc.tile_pool(name="flow", bufs=1))
+        yard = ctx.enter_context(tc.tile_pool(name="yard", bufs=1))
         psum = ctx.enter_context(tc.psum_pool(name="psum", bufs=1))
 
-        def sbuf(shape, dtype, tag, bufs=1):
-            return flow.tile(shape, dtype, name=tag, tag=tag, bufs=bufs, align_bytes=64)[:]
+        def sbuf(shape, dtype, tag):
+            return flow.tile(shape, dtype, name=tag, tag=tag, bufs=1, align_bytes=64)[:]
+
+        def placed(shape, dtype, name, offset):
+            return yard.tile(shape, dtype, name=name, tag=name, align_bytes=64, offset=offset)
+
+        def bank(name, shape, index):
+            return psum.tile(shape, F32, name=name, tag=name, offset=index * 4 * C)[:]
 
         offs_sb = keep.tile([P, S // 16], U16, name="offs_sb")
         pos1_sb = keep.tile([P, T // 16], U16, name="pos1_sb")
@@ -72,131 +89,132 @@ def tile_moe_bdx_glu_silu_kernel(
             for q in range(4):
                 nc.sync.dma_start(out=dst[32 * q : 32 * q + 4].bitcast(I32), in_=rows[4 * q : 4 * q + 4])
 
-        gate_sb = [keep.tile([P, C], F32, name=f"gate{e}") for e in range(E)]
-        ring = keep.tile([P, 3 * W + 4, C], F32, name="ring", align_bytes=64)
+        a1_sb, a3_sb = {}, {}
 
-        def slot(e):
-            return ring[:, W * (e % 3 + 1) : W * (e % 3 + 2), :]
+        def load_a1(e):
+            whole = placed([P, W, C], F32, f"a1_{e}", A1_AT + e * WHOLE)[:]
+            nc.sync.dma_start(out=whole, in_=a1_rows[:, :, e * C : (e + 1) * C])
+            for h in range(2):
+                a1_sb[2 * e + h] = whole[:, :, h * HALF : (h + 1) * HALF]
 
-        turns = ctx.enter_context(tc.tile_pool(name="turns", bufs=1))
+        def load_a3(k):
+            a3_sb[k] = placed([P, W, HALF], F32, f"a3_{k}", A3_AT + k % 6 * WHOLE // 2)[:]
+            nc.sync.dma_start(out=a3_sb[k], in_=a3_rows[:, :, k * HALF : (k + 1) * HALF])
 
-        def in_turn(shape, dtype, name, side, h=0):
-            offset = 4 * W * (side % 2 * C + h * HALF)
-            return turns.tile(shape, dtype, name=name, tag=name, align_bytes=64, offset=offset)[:]
+        gate_cols = {}
 
-        low = ctx.enter_context(tc.tile_pool(name="low", bufs=1))
-        a3_sb = {}
-
-        def load_a1(e, c0=0, c1=C):
-            nc.sync.dma_start(out=slot(e)[:, :, c0:c1], in_=a1_rows[:, :, e * C + c0 : e * C + c1])
-
-        def load_a3(e, c0=0, c1=C):
-            if c0 == 0:
-                a3_sb[e] = sbuf([P, W, C], F32, f"a3_{e % 2}")
-            nc.sync.dma_start(out=a3_sb[e][:, :, c0:c1], in_=a3_rows[:, :, e * C + c0 : e * C + c1])
-
-        gate_col = {}
-
-        def load_gates(e0, e1, place):
-            cols = place.rearrange("p (e t) -> p e t", t=2 * W)
-            row = gate[0, e0 * C : e1 * C].rearrange("(e p t) -> p e t", p=P, t=W)
-            nc.sync.dma_start(out=cols[:, :, :W], in_=row)
+        def load_gates(e0, e1):
+            cols = keep.tile([P, 2 * (e1 - e0), 2], F32, name=f"gate_cols{e0}")[:]
+            nc.sync.dma_start(out=cols, in_=gate[0, e0 * C : e1 * C].rearrange("(k q i) -> q k i", q=P, i=2))
             for e in range(e0, e1):
-                gate_col[e] = cols[:, e - e0, :]
+                gate_cols[e] = cols[:, 2 * (e - e0) : 2 * (e - e0 + 1), :]
 
         def load_dy(t):
             nc.sync.dma_start(out=dy[t][:], in_=dy_rows[t])
 
-        u_first = sbuf([P, W, HALF], F32, "z00")
-        load_gates(0, 4, u_first[:, 1, : 4 * 2 * W])
-        nc.sync.dma_start(out=slot(0)[:, 0, :HALF], in_=a1_rows[:, 0, :HALF])
+        for h in range(2):
+            a1_sb[h] = placed([P, W, HALF], F32, f"a1_first{h}", A1_AT + h * WHOLE // 2)[:]
+        nc.sync.dma_start(out=a1_sb[0][:, 0], in_=a1_rows[:, 0, :HALF])
         load_dy(0)
         nc.sync.dma_start(offs_sb[:], offs)
         load_dy(1)
-        nc.sync.dma_start(out=slot(0)[:, 1:, :HALF], in_=a1_rows[:, 1:, :HALF])
         load_dy(2)
-        load_a1(0, HALF, C)
         load_dy(3)
-        load_words(w2_sb, w2_words, 0, 2)
+        load_gates(0, 1)
+        nc.sync.dma_start(out=a1_sb[0][:, 1:], in_=a1_rows[:, 1:, :HALF])
+        load_words(w2_sb, w2_words, 0, 1)
         load_scales(w2_sc, w2_scales)
-        load_a3(0, 0, HALF)
-        load_a3(0, HALF, C)
-        load_a1(1)
+        nc.sync.dma_start(out=a1_sb[1], in_=a1_rows[:, :, HALF:C])
+        load_a3(0)
         load_a3(1)
+        load_gates(1, E)
+        load_a1(1)
+        load_a3(2)
+        load_words(w2_sb, w2_words, 1, 2)
         load_a1(2)
-        load_words(w1_sb, w1_words)
-        load_words(w3_sb, w3_words)
-        load_scales(w1_sc, w1_scales)
+        load_a3(3)
+        load_a3(4)
+        load_a1(3)
+        load_words(w3_sb, w3_words, 0, 2)
+        load_words(w1_sb, w1_words, 0, 2)
         load_scales(w3_sc, w3_scales)
-        load_gates(4, E, sbuf([P, 2 * 2 * W], F32, "late_gates"))
+        load_scales(w1_sc, w1_scales)
         load_words(w2_sb, w2_words, 2, E)
-        nc.sync.dma_start(pos1_sb[:], pos1)
-        nc.sync.dma_start(pos2_sb[:], pos2)
+        load_a3(5)
 
-        def by_runs(ap, run):
-            return ap.rearrange("p t (c i) -> p c t i", i=run)
+        def by_pairs(ap):
+            return ap.rearrange("p t (c i) -> p c t i", i=2)
 
-        def into_runs(ap, run):
-            return ap.rearrange("p (c i t) -> p c t i", i=run, t=W)
-
-        def half_of(ap, h):
-            return ap[:, :, h * HALF : (h + 1) * HALF]
+        def into_pairs(ap):
+            return ap.rearrange("p (c i t) -> p c t i", i=2, t=W)
 
         def block_of(ap, b):
             return ap[:, :, b * P : (b + 1) * P]
 
-        def bank(name, shape, index):
-            return psum.tile(shape, F32, name=name, tag=name, offset=index * 4 * C)[:]
+        g_val, g_bf, g_q, d_q, gate_ps = {}, {}, {}, {}, {}
+        u, x, th, dh, dr_ps, da = {}, {}, {}, {}, {}, {}
 
-        g_val, g_bf, g_q, d_q = {}, {}, {}, {}
-        z, x, th, dh, dr_ps, da = {}, {}, {}, {}, {}, {}
+        def spread_gate(e, index):
+            rows = bank(f"gate_ps{e}", [P, 2, 2, P], index)
+            for i in range(2):
+                for h in range(2):
+                    column = gate_cols[e][:, h, i : i + 1].to_broadcast([P, P])
+                    nc.tensor.transpose(rows[:, i, h, :], column, ident[:])
+            gate_ps[e] = rows.rearrange("p i h q -> p (h q) i")
 
-        def spread_gate(e, index, copy):
-            rows = bank(f"gate_ps{e}", [P, W, P], index)
-            for t in range(W):
-                nc.tensor.transpose(rows[:, t, :], gate_col[e][:, t : t + 1].to_broadcast([P, P]), ident[:])
-            copy(gate_sb[e][:].rearrange("p (c t) -> p c t", t=W), rows.rearrange("p t c -> p c t"))
+        def new_g(e, offset=GV_AT):
+            g_val[e] = placed([P, W, C], F32, f"g_val{e}", offset)[:]
+
+        def window(e, t):
+            return dy[t][:].indirect(offs_sb[:, e * C // 16 : (e + 1) * C // 16])
 
         def gather(e, t):
-            lists = offs_sb[:, e * C // 16 : (e + 1) * C // 16]
-            nc.vector.tensor_tensor(g_val[e][:, t, :], dy[t][:].indirect(lists), gate_sb[e][:], MULT)
+            nc.scalar.activation(g_val[e][:, t, :], window(e, t), ACT.Copy)
 
-        def round_into(dst, src):
-            nc.scalar.copy(into_runs(dst, 4), by_runs(src, 4))
-
-        def round_g(e):
-            place = 0 if 1 < e < E - 1 else 8 * W * HALF
-            g_bf[e] = low.tile([P, W * C], BF16, name=f"g_bf{e}", tag=f"g_bf{e}", align_bytes=64, offset=place)[:]
-            round_into(g_bf[e], g_val[e])
+        def times_gate(e, b0=0, b1=BLOCKS):
+            if b0 == 0:
+                place = SIDE_AT + e % 3 * WHOLE + WHOLE // 2 if e else GB_AT
+                g_bf[e] = placed([P, W * C], BF16, f"g_bf{e}", place)[:]
+            pairs = (b1 - b0) * P // 2
+            factor = gate_ps[e][:, b0 * P // 2 : b1 * P // 2, :].unsqueeze(2).to_broadcast([P, pairs, W, 2])
+            nc.vector.tensor_tensor(
+                into_pairs(g_bf[e][:, W * P * b0 : W * P * b1]),
+                by_pairs(g_val[e][:, :, P * b0 : P * b1]),
+                factor,
+                MULT,
+            )
 
         def quantize(q, c0, bf):
             cols = slice(c0, c0 + bf.shape[1] // W)
             nc.vector.quantize_mx(out=q[0][:, cols].bitcast(E5M2X4), scales=q[1][:, cols], in_=bf)
 
-        def quantize_g(e):
-            g_q[e] = in_turn([P, C], U32, f"g_codes{e}", e, 1), sbuf([P, C], U8, f"g_scales{e % 2}")
-            quantize(g_q[e], 0, g_bf[e])
+        def quantize_g(e, b0=0, b1=BLOCKS):
+            if b0 == 0:
+                g_q[e] = sbuf([P, C], U32, "g_codes"), sbuf([P, C], U8, "g_scales")
+            quantize(g_q[e], b0 * P, g_bf[e][:, W * P * b0 : W * P * b1])
 
         def new_d(e):
             d_q[e] = sbuf([P, 2 * C], U32, f"d_codes{e % 4}"), sbuf([P, 2 * C], U8, f"d_scales{e % 4}")
 
-        def quantize_d(e):
-            new_d(e)
-            quantize(d_q[e], 0, da[e])
+        def make_u(k, t0=0, t1=W):
+            if t0 == 0:
+                u[k] = placed([P, W, HALF], F32, f"u{k}", U_AT + k % 2 * WHOLE // 2)[:]
+            nc.scalar.activation(u[k][:, t0:t1], a1_sb[k][:, t0:t1], ACT.Silu, scale=-1.0)
 
-        def begin_z(e, h):
-            z[e, h] = sbuf([P, W, HALF], F32, f"z{h}{e % 2}")
-            nc.scalar.activation(z[e, h], half_of(slot(e), h), ACT.Silu, scale=-1.0)
+        def new_x(k):
+            side = ((k - 1) // 2 - 1) % 3
+            x[k] = placed([P, W, HALF], F32, f"x{k}", SIDE_AT + side * WHOLE + (k - 1) % 2 * WHOLE // 2)[:]
 
-        def finish_z(e, h):
-            nc.scalar.activation(z[e, h], z[e, h], ACT.Identity, bias=1.0, scale=-1.0)
+        def make_z(k):
+            new_x(k)
+            nc.gpsimd.tensor_scalar(x[k], u[k], -1.0, 1.0, MULT, ADD)
 
-        def make_x(e, h):
-            if (e, h) == (0, 0):
-                x[e, 0] = ring[:, :2, :].rearrange("p a (u c) -> p (a u) c", u=2)
-            else:
-                x[e, h] = in_turn([P, W, HALF], F32, f"x{e}{h}", e - 1, h)
-            nc.gpsimd.tensor_tensor(x[e, h], z[e, h], half_of(a3_sb[e], h), MULT)
+        def make_z_early(k):
+            new_x(k)
+            nc.scalar.activation(x[k], u[k], ACT.Identity, bias=1.0, scale=-1.0)
+
+        def make_x(k):
+            nc.gpsimd.tensor_tensor(x[k], x[k], a3_sb[k], MULT)
 
         def turn(src, name, index):
             dst = bank(name, [P, W, P], index)
@@ -204,13 +222,10 @@ def tile_moe_bdx_glu_silu_kernel(
                 nc.tensor.transpose(dst[:, t, :], src[:, t, :], ident[:])
             return dst
 
-        def make_th(e, b, index):
-            if (e, b // 2) not in th:
-                name = f"th{e}{b // 2}"
-                place = 4 * W * HALF * (b // 2)
-                th[e, b // 2] = low.tile([P, 2, W, P], F32, name=name, tag=name, align_bytes=64, offset=place)[:]
-            a1_ps = turn(block_of(slot(e), b), f"a1_ps{e}{b}", index)
-            nc.scalar.activation(th[e, b // 2][:, b % 2], a1_ps, ACT.Tanh, scale=0.5)
+        def make_th(e, b, bank0=0):
+            th[e, b] = placed([P, W, P], F32, f"th{e}{b}", TH_AT + b * WHOLE // BLOCKS)[:]
+            a1_ps = turn(block_of(a1_sb[2 * e + b // 2], b % 2), f"a1_ps{e}{b}", bank0 + b)
+            nc.scalar.activation(th[e, b], a1_ps, ACT.Tanh, scale=0.5)
 
         def first(e, b):
             codes, scales = g_q[e]
@@ -227,36 +242,18 @@ def tile_moe_bdx_glu_silu_kernel(
             )
 
         def gated(e, b):
-            dr = th[e, b // 2][:, b % 2]
+            dr = th[e, b]
             nc.vector.scalar_tensor_tensor(dr, dr, 1.0, dh[e, b].rearrange("s (m t) -> s t m", t=W), ADD, MULT)
             dr_ps[e, b] = turn(dr, f"dr_ps{e}{b}", BLOCKS + b)
 
         def da_of(e, i, b0, b1):
             return da[e][:, (i * BLOCKS + b0) * W * P : (i * BLOCKS + b1) * W * P]
 
-        def delta(e, b, i, c0=0):
-            factor = block_of(x[e, b // 2], b % 2) if i else block_of(slot(e), b)
-            nc.vector.tensor_tensor(
-                into_runs(da_of(e, i, b, b + 1)[:, W * c0 :], 2),
-                by_runs(factor[:, :, c0:], 2),
-                by_runs(dr_ps[e, b][:, :, c0:], 2),
-                MULT,
-            )
+        def delta(e, b, i):
+            factor = block_of((a1_sb, x)[i][2 * e + b // 2], b % 2)
+            nc.vector.tensor_tensor(into_pairs(da_of(e, i, b, b + 1)), by_pairs(factor), by_pairs(dr_ps[e, b]), MULT)
 
-        def delta_aside(e, b):
-            woven = sbuf([P, ASIDE, W], F32, "woven")
-            nc.scalar.copy(woven, dr_ps[e, b][:, :, :ASIDE].rearrange("p t c -> p c t"))
-            return woven
-
-        def delta_woven(e, b, woven):
-            nc.gpsimd.tensor_tensor(
-                da_of(e, 0, b, b + 1)[:, : W * ASIDE].rearrange("p (c t) -> p c t", t=W),
-                woven,
-                block_of(slot(e), b)[:, :, :ASIDE].rearrange("p t c -> p c t"),
-                MULT,
-            )
-
-        def second_pass(e, kt, i, acc, opens=0):
+        def second_pass(e, kt, i, acc):
             codes, scales = d_q[e]
             w, sc = ((w3_sb, w3_sc), (w1_sb, w1_sc))[i]
             nc.tensor.matmul_mx(
@@ -265,145 +262,121 @@ def tile_moe_bdx_glu_silu_kernel(
                 lhsT_scale=sc[:, e, P * kt : P * (kt + 1)],
                 rhs=codes[:, i * C : (i + 1) * C].bitcast(E5M2X4),
                 rhs_scale=scales[:, i * C : (i + 1) * C],
-                start=i == opens,
-                stop=i != opens,
+                start=i == 0,
+                stop=i == 1,
             )
-            if i != opens:
-                nc.scalar.activation(dx[kt][:, e * C : (e + 1) * C], acc, ACT.Copy, scale=0.5)
 
-        def seconds(jobs, accs):
-            for (e, kt), acc in zip(jobs, accs):
-                for i in range(2):
-                    second_pass(e, kt, i, acc)
+        def take_dx(e, kt, acc):
+            nc.scalar.activation(dx[kt][:, e * C : (e + 1) * C], acc, ACT.Copy, scale=0.5)
 
-        def three_banks(e):
-            return [bank(f"acc{e}{n}", [P, C], BLOCKS - 1 + n) for n in range(KT)]
+        def second(e, kt, index):
+            acc = bank(f"acc{e}{kt}", [P, C], index)
+            for i in range(2):
+                second_pass(e, kt, i, acc)
+            take_dx(e, kt, acc)
 
-        nc.scalar.activation(u_first[:, 0], slot(0)[:, 0, :HALF], ACT.Silu, scale=-1.0)
-        for e in range(4):
-            spread_gate(e, e, nc.vector.tensor_copy if e == 0 else nc.scalar.copy)
-        g_val[0] = sbuf([P, W, C], F32, "dx0")
-        g_val[1] = sbuf([P, W, C], F32, "dx1")
-        g_val[2] = ring[:, 2 : 2 + W, :]
+        make_u(0, 0, 1)
+        spread_gate(0, BLOCKS - 1)
+        new_g(0, DX_AT)
+        new_g(1)
         for t in range(W):
-            for e in range(2):
-                gather(e, t)
-            if t == 1:
-                gather(2, 0)
-        z[0, 0] = u_first
-        nc.scalar.activation(u_first[:, 1:], slot(0)[:, 1:, :HALF], ACT.Silu, scale=-1.0)
-        for b in range(2):
-            make_th(0, b, BLOCKS + b)
-        nc.scalar.activation(u_first, u_first, ACT.Identity, bias=1.0, scale=-1.0)
-        flat = ring[:, :W, :].rearrange("p a c -> p (a c)")
-        g_first = [flat[:, 3 * C :].bitcast(BF16), flat[:, C : 2 * C].bitcast(BF16)]
-        for b in range(2, BLOCKS):
-            make_th(0, b, BLOCKS + b)
-        u_second = sbuf([P, W, HALF], F32, "z10")
-        nc.scalar.activation(u_second, half_of(slot(0), 1), ACT.Silu, scale=-1.0)
-        for h in range(2):
-            round_into(g_first[h], half_of(g_val[0], h))
-        z[0, 1] = half_of(g_val[0], 0)
-        nc.scalar.activation(z[0, 1], u_second, ACT.Identity, bias=1.0, scale=-1.0)
-        g_q[0] = in_turn([P, C], U32, "g_codes0", 0), sbuf([P, C], U8, "g_scales0")
-        for h in range(2):
-            quantize(g_q[0], h * HALF, g_first[h])
-            if h == 0:
-                gather(2, 1)
-            for b in range(2):
-                first(0, 2 * h + b)
-        dx = {}
+            nc.vector.tensor_copy(g_val[0][:, t, :], window(0, t))
+            gather(1, t)
+        make_u(0, 1, W)
+        for b in range(BLOCKS):
+            make_th(0, b, BLOCKS)
+        make_z_early(0)
+        make_x(0)
+        make_u(1)
+        make_z_early(1)
+        make_u(2)
+        times_gate(0, 0, 2)
+        times_gate(0, 2, 3)
+        quantize_g(0, 0, 2)
+        first(0, 0)
+        first(0, 1)
+        times_gate(0, 3, 4)
+        quantize_g(0, 2, 3)
+        first(0, 2)
+        dx = [placed([P, S], F32, f"dx{kt}", DX_AT + kt * 4 * S) for kt in range(KT)]
 
         for e in range(E):
             last = e == E - 1
-            make_x(e, 0)
+            mine = [k for k in (2 * e + 1, 2 * e + 2) if k < HALVES]
+            for k in mine:
+                if k not in x:
+                    make_z(k)
+            for k in mine:
+                make_x(k)
+                if k + 5 < HALVES:
+                    load_a3(k + 5)
+                if k == 1:
+                    load_words(w3_sb, w3_words, 2, E)
+                    load_words(w1_sb, w1_words, 2, E)
+                    load_a1(4)
+                if k == 3:
+                    load_a1(5)
+                    nc.sync.dma_start(pos1_sb[:], pos1)
+                    nc.sync.dma_start(pos2_sb[:], pos2)
             for b in range(BLOCKS):
                 gated(e, b)
-            make_x(e, 1)
-            da[e] = in_turn([P, 2 * W * C], BF16, f"da{e}", e)
-            if e in (0, E - 2):
-                round_g(e + 1)
-            woven = delta_aside(e, 1)
-            if 0 < e < E - 2:
-                round_g(e + 1)
-            if 0 < e < E - 3:
-                spread_gate(e + 3, 2, nc.scalar.copy)
-            if e == 0:
-                dx = [flow.tile([P, S], F32, name=f"dx{kt}", tag=f"dx{kt}", align_bytes=64) for kt in range(KT)]
-            if 0 < e < E - 2:
-                load_a1(e + 2)
-            for h in range(2):
-                if not last:
-                    if (e + 1, h) not in z:
-                        begin_z(e + 1, h)
-                    finish_z(e + 1, h)
-            for pair in range(2):
-                for i in range(2):
-                    for b in (2 * pair, 2 * pair + 1):
-                        if (b, i) != (1, 0):
-                            delta(e, b, i)
-                        else:
-                            delta(e, b, i, ASIDE)
-                            delta_woven(e, b, woven)
-                if pair == 0 and 0 < e < E - 2:
-                    seconds([(e - 1, kt) for kt in range(KT if e < E - 3 else KT - 1)], three_banks(e))
-                if pair == 0 and last:
-                    seconds([(e - 2, 0), (e - 1, 0), (e - 2, 1)], three_banks(e))
+                if (e, b) == (0, 0):
+                    quantize_g(0, 3, 4)
+                    first(0, 3)
+            da[e] = placed([P, 2 * W * C], BF16, f"da{e}", SIDE_AT + e % 3 * WHOLE)[:]
+            for b, i in ((0, 0), (1, 0), (0, 1), (1, 1), (2, 0), (3, 0), (2, 1)):
+                delta(e, b, i)
+                if last and (b, i) == (0, 1):
+                    for kt in range(KT):
+                        second(e - 1, kt, 2 + kt)
+                if 0 < e < E - 1 and b > 0 and i == 1:
+                    second(e - 1, b - 1, BLOCKS + b)
+                if not last and (b, i) == (0, 1):
+                    spread_gate(e + 1, BLOCKS)
+                    for n in range(BLOCKS):
+                        make_th(e + 1, n)
+                    for k in mine:
+                        if k + 2 < HALVES:
+                            make_u(k + 2)
+            if e == E - 2:
+                for n in range(BLOCKS):
+                    second(n, KT - 1, n)
+            new_d(e)
             if last:
                 break
+            times_gate(e + 1)
+            delta(e, 3, 1)
             if e + 2 < E:
-                load_a3(e + 2)
-            for n in range(BLOCKS):
-                make_th(e + 1, n, BLOCKS + (n + 2) % BLOCKS)
-            if e == E - 3:
-                begin_z(E - 1, 0)
-            if e + 2 < E:
-                planes = list(range(W))
-                if e == 0:
-                    planes = planes[2:]
-                else:
-                    g_val[e + 2] = slot(e)
-                gather(e + 2, planes[0])
-                quantize_g(e + 1)
-                for t in planes[1:-1]:
+                new_g(e + 2)
+                for t in range(W):
                     gather(e + 2, t)
-                quantize_d(e)
-                gather(e + 2, planes[-1])
-            else:
-                quantize_g(e + 1)
-                quantize_d(e)
+            quantize_g(e + 1)
             for b in range(BLOCKS):
                 first(e + 1, b)
+            quantize(d_q[e], 0, da[e])
 
         e = E - 1
-        seconds([(e - 1, 1)], [bank("acc_fourth", [P, C], BLOCKS + 2)])
-        new_d(e)
-        for i in range(2):
-            quantize(d_q[e], i * C, da_of(e, i, 0, BLOCKS))
-        places = (0, BLOCKS + 3)
-        accs = [bank(f"acc_last{kt}", [P, C], places[kt]) for kt in range(2)]
-        for kt, i in ((0, 0), (0, 1), (1, 1), (1, 0)):
-            second_pass(e, kt, i, accs[kt], opens=kt)
-        for n in range(4):
-            seconds([(E - 4 + n, KT - 1)], [bank(f"acc_late{n}", [P, C], places[n % 2])])
+        quantize(d_q[e], 0, da_of(e, 0, 0, BLOCKS))
+        delta(e, 3, 1)
+        for h in range(2):
+            quantize(d_q[e], C + h * HALF, da_of(e, 1, 2 * h, 2 * h + 2))
+        accs = [bank(f"acc{e}{kt}", [P, C], (0, 1, BLOCKS + 1)[kt]) for kt in range(KT)]
+        for kt, i in ((0, 0), (1, 0), (0, 1), (1, 1), (2, 0), (2, 1)):
+            second_pass(e, kt, i, accs[kt])
+        take_dx(e, 0, accs[0])
+        for kt in range(1, KT):
+            nc.vector.tensor_scalar(dx[kt][:, e * C : (e + 1) * C], accs[kt], 0.5, None, MULT)
 
-        rows = [ring[:, 3 * n : 3 * n + 3, :].rearrange("p a c -> p (a c)") for n in range(4)]
-        y1 = rows[:KT]
-        y2 = [rows[KT]] + [sbuf([P, T], F32, f"a3_{n}") for n in range(2)]
-
-        def fetch_first(kt, c0=0, c1=T):
-            nc.vector.tensor_copy(y1[kt][:, c0:c1], dx[kt][:].indirect(pos1_sb[:, c0 // 16 : c1 // 16]))
-
-        def add_second(kt, c0, c1):
-            lists = pos2_sb[:, c0 // 16 : c1 // 16]
-            nc.vector.tensor_tensor(y2[kt][:, c0:c1], dx[kt][:].indirect(lists), y1[kt][:, c0:c1], ADD)
-            nc.sync.dma_start(out=out[kt * P : (kt + 1) * P, c0:c1], in_=y2[kt][:, c0:c1])
-
-        for kt in range(KT - 1):
-            fetch_first(kt)
-        for kt in range(KT - 1):
-            add_second(kt, 0, T)
-        fetch_first(KT - 1, 0, T // 2)
-        fetch_first(KT - 1, T // 2, T)
-        for c0, c1 in ((0, T // 2), (T // 2, T - HALF), (T - HALF, T)):
-            add_second(KT - 1, c0, c1)
+        y = [placed([P, T], F32, f"y{n}", A1_AT + n * 4 * T)[:] for n in range(2 * KT)]
+        stores = ((T // 2, T), (T // 2, T), (T // 2, T - HALF, T))
+        for kt in range(KT):
+            y1, y2 = y[2 * kt], y[2 * kt + 1]
+            stored = 0
+            for c0 in range(0, T, HALF):
+                c1 = c0 + HALF
+                lists = slice(c0 // 16, c1 // 16)
+                nc.scalar.activation(y1[:, c0:c1], dx[kt][:].indirect(pos1_sb[:, lists]), ACT.Copy)
+                nc.vector.tensor_tensor(y2[:, c0:c1], dx[kt][:].indirect(pos2_sb[:, lists]), y1[:, c0:c1], ADD)
+                if c1 in stores[kt]:
+                    nc.sync.dma_start(out=out[kt * P : (kt + 1) * P, stored:c1], in_=y2[:, stored:c1])
+                    stored = c1

@@ -84,10 +84,10 @@ def tile_moe_bdx_glu_silu_kernel(
                 out=dst[:, e0:e1].bitcast(I32), in_=words[e0:e1, 0].bitcast(I32).rearrange("e p b -> p e b")
             )
 
-        def load_scales(dst, scales):
-            rows = scales[:, 0].bitcast(I32).rearrange("e f i -> f e i")
+        def load_scales(dst, scales, e0=0, e1=E):
+            rows = scales[e0:e1, 0].bitcast(I32).rearrange("e f i -> f e i")
             for q in range(4):
-                nc.sync.dma_start(out=dst[32 * q : 32 * q + 4].bitcast(I32), in_=rows[4 * q : 4 * q + 4])
+                nc.sync.dma_start(out=dst[32 * q : 32 * q + 4, e0:e1].bitcast(I32), in_=rows[4 * q : 4 * q + 4])
 
         a1_sb, a3_sb = {}, {}
 
@@ -115,22 +115,23 @@ def tile_moe_bdx_glu_silu_kernel(
         for h in range(2):
             a1_sb[h] = placed([P, W, HALF], F32, f"a1_first{h}", A1_AT + h * WHOLE // 2)[:]
         nc.sync.dma_start(out=a1_sb[0][:, 0], in_=a1_rows[:, 0, :HALF])
+        load_gates(0, 1)
         load_dy(0)
         nc.sync.dma_start(offs_sb[:], offs)
         load_dy(1)
         load_dy(2)
         load_dy(3)
-        load_gates(0, 1)
         nc.sync.dma_start(out=a1_sb[0][:, 1:], in_=a1_rows[:, 1:, :HALF])
         load_words(w2_sb, w2_words, 0, 1)
-        load_scales(w2_sc, w2_scales)
+        load_scales(w2_sc, w2_scales, 0, 1)
         nc.sync.dma_start(out=a1_sb[1], in_=a1_rows[:, :, HALF:C])
         load_a3(0)
         load_a3(1)
-        load_gates(1, E)
         load_a1(1)
+        load_gates(1, E)
         load_a3(2)
         load_words(w2_sb, w2_words, 1, 2)
+        load_scales(w2_sc, w2_scales, 1, E)
         load_a1(2)
         load_a3(3)
         load_a3(4)
@@ -165,15 +166,15 @@ def tile_moe_bdx_glu_silu_kernel(
         def new_g(e, offset=GV_AT):
             g_val[e] = placed([P, W, C], F32, f"g_val{e}", offset)[:]
 
-        def window(e, t):
-            return dy[t][:].indirect(offs_sb[:, e * C // 16 : (e + 1) * C // 16])
+        def window(e, t, c0=0, c1=C):
+            return dy[t][:].indirect(offs_sb[:, (e * C + c0) // 16 : (e * C + c1) // 16])
 
         def gather(e, t):
             nc.scalar.activation(g_val[e][:, t, :], window(e, t), ACT.Copy)
 
         def times_gate(e, b0=0, b1=BLOCKS):
             if b0 == 0:
-                place = SIDE_AT + e % 3 * WHOLE + WHOLE // 2 if e else GB_AT
+                place = SIDE_AT + e % 3 * WHOLE + WHOLE // 2
                 g_bf[e] = placed([P, W * C], BF16, f"g_bf{e}", place)[:]
             pairs = (b1 - b0) * P // 2
             factor = gate_ps[e][:, b0 * P // 2 : b1 * P // 2, :].unsqueeze(2).to_broadcast([P, pairs, W, 2])
@@ -182,6 +183,12 @@ def tile_moe_bdx_glu_silu_kernel(
                 by_pairs(g_val[e][:, :, P * b0 : P * b1]),
                 factor,
                 MULT,
+            )
+
+        def round_first(b0, b1):
+            nc.vector.tensor_copy(
+                g_bf[0][:, W * P * b0 : W * P * b1].rearrange("p (c i t) -> p c t i", i=4, t=W),
+                g_val[0][:, :, P * b0 : P * b1].rearrange("p t (c i) -> p c t i", i=4),
             )
 
         def quantize(q, c0, bf):
@@ -214,7 +221,11 @@ def tile_moe_bdx_glu_silu_kernel(
             nc.scalar.activation(x[k], u[k], ACT.Identity, bias=1.0, scale=-1.0)
 
         def make_x(k):
-            nc.gpsimd.tensor_tensor(x[k], x[k], a3_sb[k], MULT)
+            if k == HALVES - 1:
+                new_x(k)
+                nc.gpsimd.tensor_tensor(x[k], u[k], a3_sb[k], MULT)
+            else:
+                nc.gpsimd.tensor_tensor(x[k], x[k], a3_sb[k], MULT)
 
         def turn(src, name, index):
             dst = bank(name, [P, W, P], index)
@@ -247,27 +258,38 @@ def tile_moe_bdx_glu_silu_kernel(
             dr_ps[e, b] = turn(dr, f"dr_ps{e}{b}", BLOCKS + b)
 
         def da_of(e, i, b0, b1):
-            return da[e][:, (i * BLOCKS + b0) * W * P : (i * BLOCKS + b1) * W * P]
+            return da[e][i][:, b0 * W * P : b1 * W * P]
 
         def delta(e, b, i):
             factor = block_of((a1_sb, x)[i][2 * e + b // 2], b % 2)
             nc.vector.tensor_tensor(into_pairs(da_of(e, i, b, b + 1)), by_pairs(factor), by_pairs(dr_ps[e, b]), MULT)
 
-        def second_pass(e, kt, i, acc):
+        def delta_aside(e, b):
+            woven = sbuf([P, P, W], F32, f"woven{b}")
+            nc.scalar.copy(woven, dr_ps[e, b].rearrange("p t c -> p c t"))
+            nc.gpsimd.tensor_tensor(
+                da_of(e, 0, b, b + 1).rearrange("p (c t) -> p c t", t=W),
+                woven,
+                block_of(a1_sb[2 * e + b // 2], b % 2).rearrange("p t c -> p c t"),
+                MULT,
+            )
+
+        def second_pass(e, kt, i, acc, c0=0, c1=C, step=None):
+            step = i if step is None else step
             codes, scales = d_q[e]
             w, sc = ((w3_sb, w3_sc), (w1_sb, w1_sc))[i]
             nc.tensor.matmul_mx(
                 out=acc,
                 lhsT=w[:, e, 2 * P * kt : 2 * P * (kt + 1)].bitcast(E2M1X4),
                 lhsT_scale=sc[:, e, P * kt : P * (kt + 1)],
-                rhs=codes[:, i * C : (i + 1) * C].bitcast(E5M2X4),
-                rhs_scale=scales[:, i * C : (i + 1) * C],
-                start=i == 0,
-                stop=i == 1,
+                rhs=codes[:, i * C + c0 : i * C + c1].bitcast(E5M2X4),
+                rhs_scale=scales[:, i * C + c0 : i * C + c1],
+                start=step == 0,
+                stop=step == 1,
             )
 
-        def take_dx(e, kt, acc):
-            nc.scalar.activation(dx[kt][:, e * C : (e + 1) * C], acc, ACT.Copy, scale=0.5)
+        def take_dx(e, kt, acc, c0=0, c1=C):
+            nc.scalar.activation(dx[kt][:, e * C + c0 : e * C + c1], acc, ACT.Copy, scale=0.5)
 
         def second(e, kt, index):
             acc = bank(f"acc{e}{kt}", [P, C], index)
@@ -276,26 +298,33 @@ def tile_moe_bdx_glu_silu_kernel(
             take_dx(e, kt, acc)
 
         make_u(0, 0, 1)
-        spread_gate(0, BLOCKS - 1)
+        spread_gate(0, 0)
+        gate_first = sbuf([P, C], F32, "gate_first")
+        nc.vector.tensor_copy(gate_first.rearrange("p (c i) -> p c i", i=2), gate_ps[0])
         new_g(0, DX_AT)
         new_g(1)
         for t in range(W):
-            nc.vector.tensor_copy(g_val[0][:, t, :], window(0, t))
+            for c0, c1 in ((0, C),) if t < W - 1 else ((0, HALF), (HALF, C)):
+                nc.vector.tensor_tensor(g_val[0][:, t, c0:c1], window(0, t, c0, c1), gate_first[:, c0:c1], MULT)
             gather(1, t)
         make_u(0, 1, W)
-        for b in range(BLOCKS):
+        for b in range(2):
             make_th(0, b, BLOCKS)
         make_z_early(0)
         make_x(0)
+        for b in range(2, BLOCKS):
+            make_th(0, b, BLOCKS)
         make_u(1)
-        make_z_early(1)
+        make_z(1)
         make_u(2)
-        times_gate(0, 0, 2)
-        times_gate(0, 2, 3)
+        make_z_early(2)
+        g_bf[0] = placed([P, W * C], BF16, "g_bf0", GB_AT)[:]
+        round_first(0, 2)
+        round_first(2, 3)
         quantize_g(0, 0, 2)
         first(0, 0)
         first(0, 1)
-        times_gate(0, 3, 4)
+        round_first(3, 4)
         quantize_g(0, 2, 3)
         first(0, 2)
         dx = [placed([P, S], F32, f"dx{kt}", DX_AT + kt * 4 * S) for kt in range(KT)]
@@ -304,7 +333,7 @@ def tile_moe_bdx_glu_silu_kernel(
             last = e == E - 1
             mine = [k for k in (2 * e + 1, 2 * e + 2) if k < HALVES]
             for k in mine:
-                if k not in x:
+                if k not in x and not last:
                     make_z(k)
             for k in mine:
                 make_x(k)
@@ -323,13 +352,22 @@ def tile_moe_bdx_glu_silu_kernel(
                 if (e, b) == (0, 0):
                     quantize_g(0, 3, 4)
                     first(0, 3)
-            da[e] = placed([P, 2 * W * C], BF16, f"da{e}", SIDE_AT + e % 3 * WHOLE)[:]
-            for b, i in ((0, 0), (1, 0), (0, 1), (1, 1), (2, 0), (3, 0), (2, 1)):
+            da[e] = [
+                placed([P, W * C], BF16, f"da{e}{i}", SIDE_AT + e % 3 * WHOLE + i * WHOLE // 2)[:] for i in range(2)
+            ]
+            steps = ((0, 0), (0, 1), (1, 0), (1, 1)) if e else ((0, 0), (1, 0), (0, 1), (1, 1))
+            if last:
+                steps = ((0, 1), (1, 1))
+                for b in range(2):
+                    delta_aside(e, b)
+            for b, i in steps + ((2, 0), (3, 0), (2, 1)):
+                if (b, i) == (2, 1) and not last:
+                    times_gate(e + 1)
                 delta(e, b, i)
-                if last and (b, i) == (0, 1):
-                    for kt in range(KT):
-                        second(e - 1, kt, 2 + kt)
-                if 0 < e < E - 1 and b > 0 and i == 1:
+                if last and (b, i) == (1, 1):
+                    for n, job in enumerate(((4, 0), (4, 1), (2, 2), (3, 2), (4, 2))):
+                        second(*job, 2 + n % 3)
+                if 0 < e < E - 1 and i == 1 and b in ((1,) if e < 3 else (1, 2)):
                     second(e - 1, b - 1, BLOCKS + b)
                 if not last and (b, i) == (0, 1):
                     spread_gate(e + 1, BLOCKS)
@@ -338,45 +376,57 @@ def tile_moe_bdx_glu_silu_kernel(
                     for k in mine:
                         if k + 2 < HALVES:
                             make_u(k + 2)
+                        if k + 2 == HALVES - 1:
+                            nc.scalar.activation(u[k + 2], u[k + 2], ACT.Identity, bias=1.0, scale=-1.0)
             if e == E - 2:
                 for n in range(BLOCKS):
-                    second(n, KT - 1, n)
+                    second(n // 2, 1 + n % 2, n)
             new_d(e)
             if last:
                 break
-            times_gate(e + 1)
-            delta(e, 3, 1)
             if e + 2 < E:
                 new_g(e + 2)
                 for t in range(W):
                     gather(e + 2, t)
+            if e == 0:
+                delta(e, 3, 1)
             quantize_g(e + 1)
             for b in range(BLOCKS):
                 first(e + 1, b)
-            quantize(d_q[e], 0, da[e])
+            if e > 0:
+                delta(e, 3, 1)
+            for i in range(2):
+                quantize(d_q[e], i * C, da[e][i])
 
         e = E - 1
-        quantize(d_q[e], 0, da_of(e, 0, 0, BLOCKS))
         delta(e, 3, 1)
+        for i, h in ((1, 0), (0, 1), (0, 0), (1, 1)):
+            quantize(d_q[e], i * C + h * HALF, da_of(e, i, 2 * h, 2 * h + 2))
+        places = ((0, 1), (BLOCKS + 1, BLOCKS + 2), (2, BLOCKS + 3))
+        accs = {}
+        for kt, h in ((0, 0), (0, 1), (1, 0), (1, 1), (2, 0), (2, 1)):
+            accs[kt, h] = bank(f"acc{e}{kt}{h}", [P, HALF], places[kt][h])
+            for n in range(2):
+                second_pass(e, kt, n if h else 1 - n, accs[kt, h], h * HALF, (h + 1) * HALF, n)
         for h in range(2):
-            quantize(d_q[e], C + h * HALF, da_of(e, 1, 2 * h, 2 * h + 2))
-        accs = [bank(f"acc{e}{kt}", [P, C], (0, 1, BLOCKS + 1)[kt]) for kt in range(KT)]
-        for kt, i in ((0, 0), (1, 0), (0, 1), (1, 1), (2, 0), (2, 1)):
-            second_pass(e, kt, i, accs[kt])
-        take_dx(e, 0, accs[0])
+            take_dx(e, 0, accs[0, h], h * HALF, (h + 1) * HALF)
         for kt in range(1, KT):
-            nc.vector.tensor_scalar(dx[kt][:, e * C : (e + 1) * C], accs[kt], 0.5, None, MULT)
+            for h in range(2):
+                c0 = e * C + h * HALF
+                nc.vector.tensor_scalar(dx[kt][:, c0 : c0 + HALF], accs[kt, h], 0.5, None, MULT)
 
         y = [placed([P, T], F32, f"y{n}", A1_AT + n * 4 * T)[:] for n in range(2 * KT)]
-        stores = ((T // 2, T), (T // 2, T), (T // 2, T - HALF, T))
+        quarters = tuple(range(T // 4, T + 1, T // 4))
+        ends = (quarters, quarters, quarters[:-1] + (T - P, T))
+        stores = ((T // 2, T), (T // 2, T), (T // 2, 3 * T // 4, T - P, T))
         for kt in range(KT):
             y1, y2 = y[2 * kt], y[2 * kt + 1]
-            stored = 0
-            for c0 in range(0, T, HALF):
-                c1 = c0 + HALF
+            c0 = stored = 0
+            for c1 in ends[kt]:
                 lists = slice(c0 // 16, c1 // 16)
                 nc.scalar.activation(y1[:, c0:c1], dx[kt][:].indirect(pos1_sb[:, lists]), ACT.Copy)
                 nc.vector.tensor_tensor(y2[:, c0:c1], dx[kt][:].indirect(pos2_sb[:, lists]), y1[:, c0:c1], ADD)
                 if c1 in stores[kt]:
                     nc.sync.dma_start(out=out[kt * P : (kt + 1) * P, stored:c1], in_=y2[:, stored:c1])
                     stored = c1
+                c0 = c1

@@ -122,9 +122,9 @@ def tile_moe_bdx_glu_silu_kernel(
         load_dy(2)
         load_dy(3)
         nc.sync.dma_start(out=a1_sb[0][:, 1:], in_=a1_rows[:, 1:, :HALF])
+        nc.sync.dma_start(out=a1_sb[1], in_=a1_rows[:, :, HALF:C])
         load_words(w2_sb, w2_words, 0, 1)
         load_scales(w2_sc, w2_scales, 0, 1)
-        nc.sync.dma_start(out=a1_sb[1], in_=a1_rows[:, :, HALF:C])
         load_a3(0)
         load_a3(1)
         load_a1(1)
@@ -205,12 +205,14 @@ def tile_moe_bdx_glu_silu_kernel(
 
         def make_u(k, t0=0, t1=W):
             if t0 == 0:
-                u[k] = placed([P, W, HALF], F32, f"u{k}", U_AT + k % 2 * WHOLE // 2)[:]
+                place = GB_AT if k == 1 else U_AT + k % 2 * WHOLE // 2
+                u[k] = placed([P, W, HALF], F32, f"u{k}", place)[:]
             nc.scalar.activation(u[k][:, t0:t1], a1_sb[k][:, t0:t1], ACT.Silu, scale=-1.0)
 
         def new_x(k):
             side = ((k - 1) // 2 - 1) % 3
-            x[k] = placed([P, W, HALF], F32, f"x{k}", SIDE_AT + side * WHOLE + (k - 1) % 2 * WHOLE // 2)[:]
+            place = SIDE_AT + side * WHOLE + (k - 1) % 2 * WHOLE // 2 if k else DX_AT
+            x[k] = placed([P, W, HALF], F32, f"x{k}", place)[:]
 
         def make_z(k):
             new_x(k)
@@ -264,15 +266,14 @@ def tile_moe_bdx_glu_silu_kernel(
             factor = block_of((a1_sb, x)[i][2 * e + b // 2], b % 2)
             nc.vector.tensor_tensor(into_pairs(da_of(e, i, b, b + 1)), by_pairs(factor), by_pairs(dr_ps[e, b]), MULT)
 
-        def delta_aside(e, b):
-            woven = sbuf([P, P, W], F32, f"woven{b}")
-            nc.scalar.copy(woven, dr_ps[e, b].rearrange("p t c -> p c t"))
-            nc.gpsimd.tensor_tensor(
-                da_of(e, 0, b, b + 1).rearrange("p (c t) -> p c t", t=W),
-                woven,
-                block_of(a1_sb[2 * e + b // 2], b % 2).rearrange("p t c -> p c t"),
-                MULT,
-            )
+        def woven(src, name, n):
+            dst = placed([P, P, W], F32, name, GV_AT + n * WHOLE // BLOCKS)[:]
+            nc.scalar.copy(dst, src.rearrange("p t c -> p c t"))
+            return dst
+
+        def delta_aside(e, b, factor):
+            dr = woven(dr_ps[e, b], f"dr_woven{b}", 2 + b)
+            nc.gpsimd.tensor_tensor(da_of(e, 0, b, b + 1).rearrange("p (c t) -> p c t", t=W), dr, factor, MULT)
 
         def second_pass(e, kt, i, acc, c0=0, c1=C, step=None):
             step = i if step is None else step
@@ -301,24 +302,16 @@ def tile_moe_bdx_glu_silu_kernel(
         spread_gate(0, 0)
         gate_first = sbuf([P, C], F32, "gate_first")
         nc.vector.tensor_copy(gate_first.rearrange("p (c i) -> p c i", i=2), gate_ps[0])
-        new_g(0, DX_AT)
+        new_g(0, DX_AT + WHOLE)
         new_g(1)
         for t in range(W):
             for c0, c1 in ((0, C),) if t < W - 1 else ((0, HALF), (HALF, C)):
                 nc.vector.tensor_tensor(g_val[0][:, t, c0:c1], window(0, t, c0, c1), gate_first[:, c0:c1], MULT)
             gather(1, t)
         make_u(0, 1, W)
-        for b in range(2):
+        for b in range(BLOCKS):
             make_th(0, b, BLOCKS)
-        make_z_early(0)
-        make_x(0)
-        for b in range(2, BLOCKS):
-            make_th(0, b, BLOCKS)
-        make_u(1)
-        make_z(1)
-        make_u(2)
-        make_z_early(2)
-        g_bf[0] = placed([P, W * C], BF16, "g_bf0", GB_AT)[:]
+        g_bf[0] = placed([P, W * C], BF16, "g_bf0", GB_AT + WHOLE // 4)[:]
         round_first(0, 2)
         round_first(2, 3)
         quantize_g(0, 0, 2)
@@ -327,6 +320,15 @@ def tile_moe_bdx_glu_silu_kernel(
         round_first(3, 4)
         quantize_g(0, 2, 3)
         first(0, 2)
+        gated(0, 0)
+        quantize_g(0, 3, 4)
+        first(0, 3)
+        make_z(0)
+        make_x(0)
+        make_u(1)
+        make_z_early(1)
+        make_u(2)
+        make_z_early(2)
         dx = [placed([P, S], F32, f"dx{kt}", DX_AT + kt * 4 * S) for kt in range(KT)]
 
         for e in range(E):
@@ -347,27 +349,27 @@ def tile_moe_bdx_glu_silu_kernel(
                     load_a1(5)
                     nc.sync.dma_start(pos1_sb[:], pos1)
                     nc.sync.dma_start(pos2_sb[:], pos2)
-            for b in range(BLOCKS):
+            for b in range(0 if e else 1, BLOCKS):
                 gated(e, b)
-                if (e, b) == (0, 0):
-                    quantize_g(0, 3, 4)
-                    first(0, 3)
             da[e] = [
                 placed([P, W * C], BF16, f"da{e}{i}", SIDE_AT + e % 3 * WHOLE + i * WHOLE // 2)[:] for i in range(2)
             ]
-            steps = ((0, 0), (0, 1), (1, 0), (1, 1)) if e else ((0, 0), (1, 0), (0, 1), (1, 1))
+            steps = ((0, 0), (0, 1), (1, 0), (1, 1), (2, 0), (3, 0))
+            if e == 0:
+                steps = ((0, 0), (1, 0), (2, 0), (0, 1), (3, 0), (1, 1))
             if last:
-                steps = ((0, 1), (1, 1))
+                steps = ((0, 1), (1, 1), (2, 0), (3, 0))
+                factors = [woven(block_of(a1_sb[2 * e], b), f"a1_woven{b}", b) for b in range(2)]
                 for b in range(2):
-                    delta_aside(e, b)
-            for b, i in steps + ((2, 0), (3, 0), (2, 1)):
+                    delta_aside(e, b, factors[b])
+            for b, i in steps + ((2, 1),):
                 if (b, i) == (2, 1) and not last:
                     times_gate(e + 1)
                 delta(e, b, i)
                 if last and (b, i) == (1, 1):
                     for n, job in enumerate(((4, 0), (4, 1), (2, 2), (3, 2), (4, 2))):
                         second(*job, 2 + n % 3)
-                if 0 < e < E - 1 and i == 1 and b in ((1,) if e < 3 else (1, 2)):
+                if 0 < e < E - 1 and i == 1 and b > 0:
                     second(e - 1, b - 1, BLOCKS + b)
                 if not last and (b, i) == (0, 1):
                     spread_gate(e + 1, BLOCKS)
@@ -379,8 +381,8 @@ def tile_moe_bdx_glu_silu_kernel(
                         if k + 2 == HALVES - 1:
                             nc.scalar.activation(u[k + 2], u[k + 2], ACT.Identity, bias=1.0, scale=-1.0)
             if e == E - 2:
-                for n in range(BLOCKS):
-                    second(n // 2, 1 + n % 2, n)
+                for n in range(2):
+                    second(n, KT - 1, n)
             new_d(e)
             if last:
                 break
@@ -416,16 +418,25 @@ def tile_moe_bdx_glu_silu_kernel(
                 nc.vector.tensor_scalar(dx[kt][:, c0 : c0 + HALF], accs[kt, h], 0.5, None, MULT)
 
         y = [placed([P, T], F32, f"y{n}", A1_AT + n * 4 * T)[:] for n in range(2 * KT)]
-        quarters = tuple(range(T // 4, T + 1, T // 4))
-        ends = (quarters, quarters, quarters[:-1] + (T - P, T))
-        stores = ((T // 2, T), (T // 2, T), (T // 2, 3 * T // 4, T - P, T))
+        ends = (
+            (T // 4, T // 2, 3 * T // 4, T),
+            (T // 4, T // 2, T - C, T - HALF, T),
+            (T // 4, T // 2, T - C, T - HALF, T),
+        )
+        stores = ((T // 2, T), (T // 2, T), (T // 2, T - HALF, T))
+        nc.vector.tensor_copy(y[2][:, T - HALF :], dx[1][:].indirect(pos1_sb[:, (T - HALF) // 16 :]))
         for kt in range(KT):
             y1, y2 = y[2 * kt], y[2 * kt + 1]
             c0 = stored = 0
             for c1 in ends[kt]:
                 lists = slice(c0 // 16, c1 // 16)
-                nc.scalar.activation(y1[:, c0:c1], dx[kt][:].indirect(pos1_sb[:, lists]), ACT.Copy)
-                nc.vector.tensor_tensor(y2[:, c0:c1], dx[kt][:].indirect(pos2_sb[:, lists]), y1[:, c0:c1], ADD)
+                if (kt, c1) != (1, T):
+                    nc.scalar.activation(y1[:, c0:c1], dx[kt][:].indirect(pos1_sb[:, lists]), ACT.Copy)
+                second_choice = dx[kt][:].indirect(pos2_sb[:, lists])
+                if (kt, c1) == (KT - 1, T):
+                    nc.scalar.activation(y2[:, c0:c1], second_choice, ACT.Copy)
+                    second_choice = y2[:, c0:c1]
+                nc.vector.tensor_tensor(y2[:, c0:c1], second_choice, y1[:, c0:c1], ADD)
                 if c1 in stores[kt]:
                     nc.sync.dma_start(out=out[kt * P : (kt + 1) * P, stored:c1], in_=y2[:, stored:c1])
                     stored = c1

@@ -36,8 +36,7 @@ U_AT = A3_AT + 3 * WHOLE
 TH_AT = U_AT + WHOLE
 SIDE_AT = TH_AT + WHOLE
 GV_AT = SIDE_AT + 3 * WHOLE
-GB_AT = GV_AT + WHOLE
-DX_AT = GB_AT + WHOLE // 2
+DX_AT = GV_AT + WHOLE
 
 
 def tile_moe_bdx_glu_silu_kernel(
@@ -66,13 +65,13 @@ def tile_moe_bdx_glu_silu_kernel(
         w2_sb = keep.tile([P, E, 2 * H], U8, name="w2_sb", align_bytes=64)
         w1_sb = keep.tile([P, E, 2 * K], U8, name="w1_sb", align_bytes=64)
         w3_sb = keep.tile([P, E, 2 * K], U8, name="w3_sb", align_bytes=64)
-        w2_sc = keep.tile([P, E, H], U8, name="w2_sc", align_bytes=64)
+        w2_sc = [keep.tile([P, n, H], U8, name=f"w2_sc{n}", align_bytes=64) for n in (1, E - 1)]
         w1_sc = keep.tile([P, E, K], U8, name="w1_sc", align_bytes=64)
         w3_sc = keep.tile([P, E, K], U8, name="w3_sc", align_bytes=64)
         ident = keep.tile([P, P], F32, name="ident")
 
         make_identity(nc, ident[:])
-        for plane in (w2_sc, w1_sc, w3_sc):
+        for plane in (*w2_sc, w1_sc, w3_sc):
             nc.vector.memset(plane[:].rearrange("p e i -> p (e i)").bitcast(U32), 0)
 
         dy_rows = dyT.rearrange("(p t) c -> t p c", t=W)
@@ -87,24 +86,26 @@ def tile_moe_bdx_glu_silu_kernel(
         def load_scales(dst, scales, e0=0, e1=E):
             rows = scales[e0:e1, 0].bitcast(I32).rearrange("e f i -> f e i")
             for q in range(4):
-                nc.sync.dma_start(out=dst[32 * q : 32 * q + 4, e0:e1].bitcast(I32), in_=rows[4 * q : 4 * q + 4])
+                nc.sync.dma_start(out=dst[32 * q : 32 * q + 4].bitcast(I32), in_=rows[4 * q : 4 * q + 4])
 
         a1_sb, a3_sb = {}, {}
 
-        def load_a1(e):
-            whole = placed([P, W, C], F32, f"a1_{e}", A1_AT + e * WHOLE)[:]
-            nc.sync.dma_start(out=whole, in_=a1_rows[:, :, e * C : (e + 1) * C])
-            for h in range(2):
-                a1_sb[2 * e + h] = whole[:, :, h * HALF : (h + 1) * HALF]
+        def load_halves(held, rows, name, place, k0, k1):
+            tile = placed([P, W, (k1 - k0) * HALF], F32, f"{name}_{k0}", place)[:]
+            nc.sync.dma_start(out=tile, in_=rows[:, :, k0 * HALF : k1 * HALF])
+            for k in range(k0, k1):
+                held[k] = tile[:, :, (k - k0) * HALF : (k - k0 + 1) * HALF]
 
-        def load_a3(k):
-            a3_sb[k] = placed([P, W, HALF], F32, f"a3_{k}", A3_AT + k % 6 * WHOLE // 2)[:]
-            nc.sync.dma_start(out=a3_sb[k], in_=a3_rows[:, :, k * HALF : (k + 1) * HALF])
+        def load_a1(k0, k1):
+            load_halves(a1_sb, a1_rows, "a1", A1_AT + k0 * WHOLE // 2, k0, k1)
+
+        def load_a3(k0, k1):
+            load_halves(a3_sb, a3_rows, "a3", A3_AT + (k0 - 1) % 6 * WHOLE // 2, k0, k1)
 
         gate_cols = {}
 
-        def load_gates(e0, e1):
-            cols = keep.tile([P, 2 * (e1 - e0), 2], F32, name=f"gate_cols{e0}")[:]
+        def load_gates(e0, e1, room):
+            cols = room[:, : 4 * (e1 - e0)].rearrange("p (k i) -> p k i", i=2)
             nc.sync.dma_start(out=cols, in_=gate[0, e0 * C : e1 * C].rearrange("(k q i) -> q k i", q=P, i=2))
             for e in range(e0, e1):
                 gate_cols[e] = cols[:, 2 * (e - e0) : 2 * (e - e0 + 1), :]
@@ -112,36 +113,33 @@ def tile_moe_bdx_glu_silu_kernel(
         def load_dy(t):
             nc.sync.dma_start(out=dy[t][:], in_=dy_rows[t])
 
-        for h in range(2):
-            a1_sb[h] = placed([P, W, HALF], F32, f"a1_first{h}", A1_AT + h * WHOLE // 2)[:]
+        a1_sb[0] = placed([P, W, HALF], F32, "a1_0", A1_AT)[:]
         nc.sync.dma_start(out=a1_sb[0][:, 0], in_=a1_rows[:, 0, :HALF])
-        load_gates(0, 1)
+        third = placed([P, W, C], F32, "g_val2", GV_AT)[:]
+        load_gates(0, 2, third[:, 0])
         load_dy(0)
         nc.sync.dma_start(offs_sb[:], offs)
-        load_dy(1)
-        load_dy(2)
-        load_dy(3)
+        load_scales(w2_sc[0], w2_scales, 0, 1)
+        for t in range(1, W):
+            load_dy(t)
         nc.sync.dma_start(out=a1_sb[0][:, 1:], in_=a1_rows[:, 1:, :HALF])
-        nc.sync.dma_start(out=a1_sb[1], in_=a1_rows[:, :, HALF:C])
+        load_a1(1, 2)
         load_words(w2_sb, w2_words, 0, 1)
-        load_scales(w2_sc, w2_scales, 0, 1)
-        load_a3(0)
-        load_a3(1)
-        load_a1(1)
-        load_gates(1, E)
-        load_a3(2)
+        load_a3(0, 1)
+        load_a3(1, 2)
+        load_a1(2, 4)
+        load_gates(2, E, sbuf([P, 4 * (E - 2)], F32, "late_gates"))
+        load_a3(2, 3)
         load_words(w2_sb, w2_words, 1, 2)
-        load_scales(w2_sc, w2_scales, 1, E)
-        load_a1(2)
-        load_a3(3)
-        load_a3(4)
-        load_a1(3)
+        load_scales(w2_sc[1], w2_scales, 1, E)
+        load_a1(4, 6)
+        load_a3(3, 5)
+        load_a1(6, 8)
         load_words(w3_sb, w3_words, 0, 2)
         load_words(w1_sb, w1_words, 0, 2)
         load_scales(w3_sc, w3_scales)
         load_scales(w1_sc, w1_scales)
         load_words(w2_sb, w2_words, 2, E)
-        load_a3(5)
 
         def by_pairs(ap):
             return ap.rearrange("p t (c i) -> p c t i", i=2)
@@ -197,7 +195,8 @@ def tile_moe_bdx_glu_silu_kernel(
 
         def quantize_g(e, b0=0, b1=BLOCKS):
             if b0 == 0:
-                g_q[e] = sbuf([P, C], U32, "g_codes"), sbuf([P, C], U8, "g_scales")
+                codes = placed([P, C], U32, "g_codes1", A1_AT + WHOLE // 2)[:] if e == 1 else sbuf([P, C], U32, "g_codes")
+                g_q[e] = codes, sbuf([P, C], U8, "g_scales")
             quantize(g_q[e], b0 * P, g_bf[e][:, W * P * b0 : W * P * b1])
 
         def new_d(e):
@@ -205,14 +204,12 @@ def tile_moe_bdx_glu_silu_kernel(
 
         def make_u(k, t0=0, t1=W):
             if t0 == 0:
-                place = GB_AT if k == 1 else U_AT + k % 2 * WHOLE // 2
-                u[k] = placed([P, W, HALF], F32, f"u{k}", place)[:]
+                u[k] = placed([P, W, HALF], F32, f"u{k}", U_AT + k % 2 * WHOLE // 2)[:]
             nc.scalar.activation(u[k][:, t0:t1], a1_sb[k][:, t0:t1], ACT.Silu, scale=-1.0)
 
         def new_x(k):
             side = ((k - 1) // 2 - 1) % 3
-            place = SIDE_AT + side * WHOLE + (k - 1) % 2 * WHOLE // 2 if k else DX_AT
-            x[k] = placed([P, W, HALF], F32, f"x{k}", place)[:]
+            x[k] = placed([P, W, HALF], F32, f"x{k}", SIDE_AT + side * WHOLE + (k - 1) % 2 * WHOLE // 2)[:]
 
         def make_z(k):
             new_x(k)
@@ -235,9 +232,9 @@ def tile_moe_bdx_glu_silu_kernel(
                 nc.tensor.transpose(dst[:, t, :], src[:, t, :], ident[:])
             return dst
 
-        def make_th(e, b, bank0=0):
+        def make_th(e, b, index):
             th[e, b] = placed([P, W, P], F32, f"th{e}{b}", TH_AT + b * WHOLE // BLOCKS)[:]
-            a1_ps = turn(block_of(a1_sb[2 * e + b // 2], b % 2), f"a1_ps{e}{b}", bank0 + b)
+            a1_ps = turn(block_of(a1_sb[2 * e + b // 2], b % 2), f"a1_ps{e}{b}", index)
             nc.scalar.activation(th[e, b], a1_ps, ACT.Tanh, scale=0.5)
 
         def first(e, b):
@@ -249,7 +246,7 @@ def tile_moe_bdx_glu_silu_kernel(
                 lhsT=codes[:, cols].bitcast(E5M2X4),
                 lhsT_scale=scales[:, cols],
                 rhs=w2_sb[:, e].bitcast(E2M1X4),
-                rhs_scale=w2_sc[:, e],
+                rhs_scale=w2_sc[1][:, e - 1] if e else w2_sc[0][:, 0],
                 start=True,
                 stop=True,
             )
@@ -302,28 +299,36 @@ def tile_moe_bdx_glu_silu_kernel(
         spread_gate(0, 0)
         gate_first = sbuf([P, C], F32, "gate_first")
         nc.vector.tensor_copy(gate_first.rearrange("p (c i) -> p c i", i=2), gate_ps[0])
+        spread_gate(1, 2 * BLOCKS - 1)
         new_g(0, DX_AT + WHOLE)
-        new_g(1)
+        new_g(1, DX_AT + 3 * WHOLE)
+        g_val[2] = third
         for t in range(W):
             for c0, c1 in ((0, C),) if t < W - 1 else ((0, HALF), (HALF, C)):
                 nc.vector.tensor_tensor(g_val[0][:, t, c0:c1], window(0, t, c0, c1), gate_first[:, c0:c1], MULT)
             gather(1, t)
+            if t == 0:
+                nc.vector.tensor_copy(g_val[2][:, t, :], window(2, t))
+            if t == 1:
+                gather(2, t)
         make_u(0, 1, W)
         for b in range(BLOCKS):
-            make_th(0, b, BLOCKS)
-        g_bf[0] = placed([P, W * C], BF16, "g_bf0", GB_AT + WHOLE // 4)[:]
+            make_th(0, b, BLOCKS + b % 3)
+        spare = g_val[2][:, 2:, :].rearrange("p t c -> p (t c)")
+        g_bf[0] = spare.bitcast(BF16)
         round_first(0, 2)
         round_first(2, 3)
         quantize_g(0, 0, 2)
         first(0, 0)
         first(0, 1)
         round_first(3, 4)
-        quantize_g(0, 2, 3)
+        times_gate(1, 0, 1)
+        quantize_g(0, 2, 4)
         first(0, 2)
-        gated(0, 0)
-        quantize_g(0, 3, 4)
         first(0, 3)
-        make_z(0)
+        times_gate(1, 1, BLOCKS)
+        x[0] = spare.rearrange("p (t c) -> p t c", t=W)
+        nc.gpsimd.tensor_scalar(x[0], u[0], -1.0, 1.0, MULT, ADD)
         make_x(0)
         make_u(1)
         make_z_early(1)
@@ -339,18 +344,23 @@ def tile_moe_bdx_glu_silu_kernel(
                     make_z(k)
             for k in mine:
                 make_x(k)
-                if k + 5 < HALVES:
-                    load_a3(k + 5)
-                if k == 1:
-                    load_words(w3_sb, w3_words, 2, E)
-                    load_words(w1_sb, w1_words, 2, E)
-                    load_a1(4)
-                if k == 3:
-                    load_a1(5)
-                    nc.sync.dma_start(pos1_sb[:], pos1)
-                    nc.sync.dma_start(pos2_sb[:], pos2)
-            for b in range(0 if e else 1, BLOCKS):
+            if e == 0:
+                load_a3(5, 7)
+                load_a1(8, 10)
+                load_words(w3_sb, w3_words, 2, E)
+                load_words(w1_sb, w1_words, 2, E)
+                load_a3(7, 9)
+                load_a1(10, 12)
+                nc.sync.dma_start(pos1_sb[:], pos1)
+                nc.sync.dma_start(pos2_sb[:], pos2)
+            if e == 1:
+                load_a3(9, 11)
+            if e == 2:
+                load_a3(11, 12)
+            for b in range(BLOCKS):
                 gated(e, b)
+            if 0 < e < E - 1:
+                spread_gate(e + 1, 0)
             da[e] = [
                 placed([P, W * C], BF16, f"da{e}{i}", SIDE_AT + e % 3 * WHOLE + i * WHOLE // 2)[:] for i in range(2)
             ]
@@ -363,7 +373,7 @@ def tile_moe_bdx_glu_silu_kernel(
                 for b in range(2):
                     delta_aside(e, b, factors[b])
             for b, i in steps + ((2, 1),):
-                if (b, i) == (2, 1) and not last:
+                if (b, i) == (2, 1) and 0 < e < E - 1:
                     times_gate(e + 1)
                 delta(e, b, i)
                 if last and (b, i) == (1, 1):
@@ -372,23 +382,25 @@ def tile_moe_bdx_glu_silu_kernel(
                 if 0 < e < E - 1 and i == 1 and b > 0:
                     second(e - 1, b - 1, BLOCKS + b)
                 if not last and (b, i) == (0, 1):
-                    spread_gate(e + 1, BLOCKS)
-                    for n in range(BLOCKS):
-                        make_th(e + 1, n)
+                    for n in (1, 2, 3, 0):
+                        make_th(e + 1, n, n if n or not e else BLOCKS)
+                    if e in ():
+                        second(e - 1, KT - 1, 1)
+                    if e == E - 2:
+                        for n, early in enumerate((0, 1)):
+                            second(early, KT - 1, 2 + n)
                     for k in mine:
                         if k + 2 < HALVES:
                             make_u(k + 2)
                         if k + 2 == HALVES - 1:
                             nc.scalar.activation(u[k + 2], u[k + 2], ACT.Identity, bias=1.0, scale=-1.0)
-            if e == E - 2:
-                for n in range(2):
-                    second(n, KT - 1, n)
             new_d(e)
             if last:
                 break
             if e + 2 < E:
-                new_g(e + 2)
-                for t in range(W):
+                if e > 0:
+                    new_g(e + 2)
+                for t in range(0 if e else 2, W):
                     gather(e + 2, t)
             if e == 0:
                 delta(e, 3, 1)
@@ -423,7 +435,7 @@ def tile_moe_bdx_glu_silu_kernel(
             (T // 4, T // 2, T - C, T - HALF, T),
             (T // 4, T // 2, T - C, T - HALF, T),
         )
-        stores = ((T // 2, T), (T // 2, T), (T // 2, T - HALF, T))
+        stores = ((T // 2, T), (T // 2, T), (T // 2, T - C, T - HALF, T))
         nc.vector.tensor_copy(y[2][:, T - HALF :], dx[1][:].indirect(pos1_sb[:, (T - HALF) // 16 :]))
         for kt in range(KT):
             y1, y2 = y[2 * kt], y[2 * kt + 1]

@@ -34,9 +34,10 @@ A1_AT = 0
 A3_AT = A1_AT + E * WHOLE
 U_AT = A3_AT + 3 * WHOLE
 TH_AT = U_AT + WHOLE
-SIDE_AT = TH_AT + WHOLE
-GV_AT = SIDE_AT + 3 * WHOLE
-DX_AT = GV_AT + WHOLE
+GV_AT = TH_AT + WHOLE
+LANE_AT = GV_AT + WHOLE // 2
+RING_AT = LANE_AT + (E + 1) * WHOLE // 2
+DX_AT = RING_AT + WHOLE
 
 
 def tile_moe_bdx_glu_silu_kernel(
@@ -100,7 +101,7 @@ def tile_moe_bdx_glu_silu_kernel(
             load_halves(a1_sb, a1_rows, "a1", A1_AT + k0 * WHOLE // 2, k0, k1)
 
         def load_a3(k0, k1):
-            load_halves(a3_sb, a3_rows, "a3", A3_AT + (k0 - 1) % 6 * WHOLE // 2, k0, k1)
+            load_halves(a3_sb, a3_rows, "a3", A3_AT + k0 % 6 * WHOLE // 2, k0, k1)
 
         gate_cols = {}
 
@@ -115,7 +116,7 @@ def tile_moe_bdx_glu_silu_kernel(
 
         a1_sb[0] = placed([P, W, HALF], F32, "a1_0", A1_AT)[:]
         nc.sync.dma_start(out=a1_sb[0][:, 0], in_=a1_rows[:, 0, :HALF])
-        third = placed([P, W, C], F32, "g_val2", GV_AT)[:]
+        third = placed([P, W, C], F32, "g_val2", A1_AT + (E - 1) * WHOLE)[:]
         load_gates(0, 2, third[:, 0])
         load_dy(0)
         nc.sync.dma_start(offs_sb[:], offs)
@@ -128,18 +129,19 @@ def tile_moe_bdx_glu_silu_kernel(
         load_a3(0, 1)
         load_a3(1, 2)
         load_a1(2, 4)
-        load_gates(2, E, sbuf([P, 4 * (E - 2)], F32, "late_gates"))
-        load_a3(2, 3)
         load_words(w2_sb, w2_words, 1, 2)
         load_scales(w2_sc[1], w2_scales, 1, E)
+        load_a3(2, 4)
+        load_gates(2, E, sbuf([P, 4 * (E - 2)], F32, "late_gates"))
         load_a1(4, 6)
-        load_a3(3, 5)
-        load_a1(6, 8)
         load_words(w3_sb, w3_words, 0, 2)
         load_words(w1_sb, w1_words, 0, 2)
         load_scales(w3_sc, w3_scales)
         load_scales(w1_sc, w1_scales)
-        load_words(w2_sb, w2_words, 2, E)
+        load_words(w2_sb, w2_words, 2, 3)
+        load_a3(4, 6)
+        load_a1(6, 8)
+        load_words(w2_sb, w2_words, 3, 4)
 
         def by_pairs(ap):
             return ap.rearrange("p t (c i) -> p c t i", i=2)
@@ -172,7 +174,7 @@ def tile_moe_bdx_glu_silu_kernel(
 
         def times_gate(e, b0=0, b1=BLOCKS):
             if b0 == 0:
-                place = SIDE_AT + e % 3 * WHOLE + WHOLE // 2
+                place = LANE_AT + (e - 1) * WHOLE // 2
                 g_bf[e] = placed([P, W * C], BF16, f"g_bf{e}", place)[:]
             pairs = (b1 - b0) * P // 2
             factor = gate_ps[e][:, b0 * P // 2 : b1 * P // 2, :].unsqueeze(2).to_broadcast([P, pairs, W, 2])
@@ -200,27 +202,31 @@ def tile_moe_bdx_glu_silu_kernel(
             quantize(g_q[e], b0 * P, g_bf[e][:, W * P * b0 : W * P * b1])
 
         def new_d(e):
-            d_q[e] = sbuf([P, 2 * C], U32, f"d_codes{e % 4}"), sbuf([P, 2 * C], U8, f"d_scales{e % 4}")
+            codes = placed([P, 2 * C], U32, f"d_codes{e}", LANE_AT + e * WHOLE // 2)[:]
+            d_q[e] = codes, sbuf([P, 2 * C], U8, f"d_scales{e}")
 
         def make_u(k, t0=0, t1=W):
             if t0 == 0:
-                u[k] = placed([P, W, HALF], F32, f"u{k}", U_AT + k % 2 * WHOLE // 2)[:]
+                u[k] = placed([P, W, HALF], F32, f"u{k}", (GV_AT if k == HALVES - 1 else U_AT) + k % 2 * WHOLE // 2)[:]
             nc.scalar.activation(u[k][:, t0:t1], a1_sb[k][:, t0:t1], ACT.Silu, scale=-1.0)
 
         def new_x(k):
-            side = ((k - 1) // 2 - 1) % 3
-            x[k] = placed([P, W, HALF], F32, f"x{k}", SIDE_AT + side * WHOLE + (k - 1) % 2 * WHOLE // 2)[:]
+            e = k // 2
+            place = RING_AT + (e - 1) % 2 * WHOLE // 2 if k % 2 else LANE_AT + e * WHOLE // 2
+            x[k] = placed([P, W, HALF], F32, f"x{k}", place)[:]
 
         def make_z(k):
             new_x(k)
             nc.gpsimd.tensor_scalar(x[k], u[k], -1.0, 1.0, MULT, ADD)
 
         def make_z_early(k):
-            new_x(k)
             nc.scalar.activation(x[k], u[k], ACT.Identity, bias=1.0, scale=-1.0)
 
+        def make_z_in_place(k):
+            nc.gpsimd.tensor_scalar(u[k], u[k], -1.0, 1.0, MULT, ADD)
+
         def make_x(k):
-            if k == HALVES - 1:
+            if k not in x:
                 new_x(k)
                 nc.gpsimd.tensor_tensor(x[k], u[k], a3_sb[k], MULT)
             else:
@@ -269,7 +275,7 @@ def tile_moe_bdx_glu_silu_kernel(
             return dst
 
         def delta_aside(e, b, factor):
-            dr = woven(dr_ps[e, b], f"dr_woven{b}", 2 + b)
+            dr = woven(dr_ps[e, b], f"dr_woven{b}", 1 + b)
             nc.gpsimd.tensor_tensor(da_of(e, 0, b, b + 1).rearrange("p (c t) -> p c t", t=W), dr, factor, MULT)
 
         def second_pass(e, kt, i, acc, c0=0, c1=C, step=None):
@@ -314,107 +320,107 @@ def tile_moe_bdx_glu_silu_kernel(
         make_u(0, 1, W)
         for b in range(BLOCKS):
             make_th(0, b, BLOCKS + b % 3)
-        spare = g_val[2][:, 2:, :].rearrange("p t c -> p (t c)")
-        g_bf[0] = spare.bitcast(BF16)
+        g_bf[0] = placed([P, W * C], BF16, "g_bf0", DX_AT)[:]
         round_first(0, 2)
-        round_first(2, 3)
+        round_first(2, 4)
         quantize_g(0, 0, 2)
         first(0, 0)
         first(0, 1)
-        round_first(3, 4)
-        times_gate(1, 0, 1)
         quantize_g(0, 2, 4)
         first(0, 2)
         first(0, 3)
-        times_gate(1, 1, BLOCKS)
-        x[0] = spare.rearrange("p (t c) -> p t c", t=W)
+        times_gate(1)
+        x[0] = placed([P, W, HALF], F32, "x0", DX_AT)[:]
+        x[1] = g_val[2][:, 2:, :].rearrange("p t c -> p (t c)").rearrange("p (t c) -> p t c", t=W)
         nc.gpsimd.tensor_scalar(x[0], u[0], -1.0, 1.0, MULT, ADD)
         make_x(0)
         make_u(1)
         make_z_early(1)
-        make_u(2)
-        make_z_early(2)
         dx = [placed([P, S], F32, f"dx{kt}", DX_AT + kt * 4 * S) for kt in range(KT)]
 
         for e in range(E):
             last = e == E - 1
-            mine = [k for k in (2 * e + 1, 2 * e + 2) if k < HALVES]
-            for k in mine:
-                if k not in x and not last:
-                    make_z(k)
-            for k in mine:
-                make_x(k)
+            if e > 0:
+                make_x(2 * e)
+            if 0 < e < E - 1:
+                make_z(2 * e + 1)
+            make_x(2 * e + 1)
+            if not last:
+                make_u(2 * e + 2)
+                make_z_in_place(2 * e + 2)
             if e == 0:
-                load_a3(5, 7)
+                load_a3(6, 8)
                 load_a1(8, 10)
                 load_words(w3_sb, w3_words, 2, E)
                 load_words(w1_sb, w1_words, 2, E)
-                load_a3(7, 9)
+                load_words(w2_sb, w2_words, 4, E)
+            if e == 1:
+                load_a3(8, 10)
+            if e == 2:
                 load_a1(10, 12)
+                load_a3(10, 12)
                 nc.sync.dma_start(pos1_sb[:], pos1)
                 nc.sync.dma_start(pos2_sb[:], pos2)
-            if e == 1:
-                load_a3(9, 11)
-            if e == 2:
-                load_a3(11, 12)
             for b in range(BLOCKS):
                 gated(e, b)
             if 0 < e < E - 1:
                 spread_gate(e + 1, 0)
             da[e] = [
-                placed([P, W * C], BF16, f"da{e}{i}", SIDE_AT + e % 3 * WHOLE + i * WHOLE // 2)[:] for i in range(2)
+                placed([P, W * C], BF16, f"da{e}{i}", place)[:]
+                for i, place in enumerate((LANE_AT + (e + 1) * WHOLE // 2, RING_AT + e % 2 * WHOLE // 2))
             ]
-            steps = ((0, 0), (0, 1), (1, 0), (1, 1), (2, 0), (3, 0))
+            steps = ((0, 0), (1, 0), (0, 1), (1, 1), (2, 0), (3, 0))
             if e == 0:
-                steps = ((0, 0), (1, 0), (2, 0), (0, 1), (3, 0), (1, 1))
+                steps = ((0, 0), (1, 0), (2, 0), (0, 1), (1, 1), (3, 0))
             if last:
-                steps = ((0, 1), (1, 1), (2, 0), (3, 0))
-                factors = [woven(block_of(a1_sb[2 * e], b), f"a1_woven{b}", b) for b in range(2)]
-                for b in range(2):
+                steps = ((1, 0), (2, 0), (3, 0), (0, 1), (1, 1))
+                factors = [woven(block_of(a1_sb[2 * e], b), f"a1_woven{b}", b) for b in range(1)]
+                for b in range(1):
                     delta_aside(e, b, factors[b])
             for b, i in steps + ((2, 1),):
                 if (b, i) == (2, 1) and 0 < e < E - 1:
                     times_gate(e + 1)
+                    if e == E - 2:
+                        k = HALVES - 1
+                        make_u(k)
+                        nc.scalar.activation(u[k], u[k], ACT.Identity, bias=1.0, scale=-1.0)
                 delta(e, b, i)
                 if last and (b, i) == (1, 1):
                     for n, job in enumerate(((4, 0), (4, 1), (2, 2), (3, 2), (4, 2))):
                         second(*job, 2 + n % 3)
-                if 0 < e < E - 1 and i == 1 and b > 0:
-                    second(e - 1, b - 1, BLOCKS + b)
+                if 0 < e < E - 1 and (b, i) == (1, 1):
+                    second(e - 1, 1, BLOCKS + b)
                 if not last and (b, i) == (0, 1):
-                    for n in (1, 2, 3, 0):
+                    for n in (1, 2, 3, 0) if e else range(BLOCKS):
                         make_th(e + 1, n, n if n or not e else BLOCKS)
-                    if e in ():
-                        second(e - 1, KT - 1, 1)
+                    if e > 0:
+                        second(e - 1, 0, 1)
+                    if e == 1:
+                        second(0, KT - 1, 2)
                     if e == E - 2:
-                        for n, early in enumerate((0, 1)):
-                            second(early, KT - 1, 2 + n)
-                    for k in mine:
-                        if k + 2 < HALVES:
-                            make_u(k + 2)
-                        if k + 2 == HALVES - 1:
-                            nc.scalar.activation(u[k + 2], u[k + 2], ACT.Identity, bias=1.0, scale=-1.0)
+                        second(1, KT - 1, 2)
+                    if e < E - 2:
+                        make_u(2 * e + 3)
             new_d(e)
             if last:
                 break
-            if e + 2 < E:
-                if e > 0:
-                    new_g(e + 2)
-                for t in range(0 if e else 2, W):
+            if 0 < e < E - 2:
+                new_g(e + 2)
+                for t in range(W):
                     gather(e + 2, t)
-            if e == 0:
-                delta(e, 3, 1)
             quantize_g(e + 1)
             for b in range(BLOCKS):
                 first(e + 1, b)
-            if e > 0:
-                delta(e, 3, 1)
+            delta(e, 3, 1)
+            if e == 0:
+                for t in range(2, W):
+                    gather(2, t)
             for i in range(2):
                 quantize(d_q[e], i * C, da[e][i])
 
         e = E - 1
         delta(e, 3, 1)
-        for i, h in ((1, 0), (0, 1), (0, 0), (1, 1)):
+        for i, h in ((0, 1), (1, 0), (1, 1), (0, 0)):
             quantize(d_q[e], i * C + h * HALF, da_of(e, i, 2 * h, 2 * h + 2))
         places = ((0, 1), (BLOCKS + 1, BLOCKS + 2), (2, BLOCKS + 3))
         accs = {}
@@ -435,7 +441,7 @@ def tile_moe_bdx_glu_silu_kernel(
             (T // 4, T // 2, T - C, T - HALF, T),
             (T // 4, T // 2, T - C, T - HALF, T),
         )
-        stores = ((T // 2, T), (T // 2, T), (T // 2, T - C, T - HALF, T))
+        stores = ((T // 2, T), (T // 2, T), ends[-1])
         nc.vector.tensor_copy(y[2][:, T - HALF :], dx[1][:].indirect(pos1_sb[:, (T - HALF) // 16 :]))
         for kt in range(KT):
             y1, y2 = y[2 * kt], y[2 * kt + 1]

@@ -28,6 +28,7 @@ KT = K // P
 HALF = C // 2
 BLOCKS = C // P
 HALVES = 2 * E
+LEAD = 64
 
 WHOLE = 4 * W * C
 A1_AT = 0
@@ -115,14 +116,15 @@ def tile_moe_bdx_glu_silu_kernel(
             nc.sync.dma_start(out=dy[t][:], in_=dy_rows[t])
 
         a1_sb[0] = placed([P, W, HALF], F32, "a1_0", A1_AT)[:]
-        nc.sync.dma_start(out=a1_sb[0][:, 0], in_=a1_rows[:, 0, :HALF])
+        nc.sync.dma_start(out=a1_sb[0][:, 0, :LEAD], in_=a1_rows[:, 0, :LEAD])
         third = placed([P, W, C], F32, "g_val2", A1_AT + (E - 1) * WHOLE)[:]
         load_gates(0, 2, third[:, 0])
         load_dy(0)
         nc.sync.dma_start(offs_sb[:], offs)
-        load_scales(w2_sc[0], w2_scales, 0, 1)
         for t in range(1, W):
             load_dy(t)
+        load_scales(w2_sc[0], w2_scales, 0, 1)
+        nc.sync.dma_start(out=a1_sb[0][:, 0, LEAD:], in_=a1_rows[:, 0, LEAD:HALF])
         nc.sync.dma_start(out=a1_sb[0][:, 1:], in_=a1_rows[:, 1:, :HALF])
         load_a1(1, 2)
         load_words(w2_sb, w2_words, 0, 1)
@@ -301,7 +303,8 @@ def tile_moe_bdx_glu_silu_kernel(
                 second_pass(e, kt, i, acc)
             take_dx(e, kt, acc)
 
-        make_u(0, 0, 1)
+        u[0] = placed([P, W, HALF], F32, "u0", U_AT)[:]
+        nc.scalar.activation(u[0][:, 0, :LEAD], a1_sb[0][:, 0, :LEAD], ACT.Silu, scale=-1.0)
         spread_gate(0, 0)
         gate_first = sbuf([P, C], F32, "gate_first")
         nc.vector.tensor_copy(gate_first.rearrange("p (c i) -> p c i", i=2), gate_ps[0])
@@ -317,6 +320,7 @@ def tile_moe_bdx_glu_silu_kernel(
                 nc.vector.tensor_copy(g_val[2][:, t, :], window(2, t))
             if t == 1:
                 gather(2, t)
+        nc.scalar.activation(u[0][:, 0, LEAD:], a1_sb[0][:, 0, LEAD:], ACT.Silu, scale=-1.0)
         make_u(0, 1, W)
         for b in range(BLOCKS):
             make_th(0, b, BLOCKS + b % 3)

@@ -87,8 +87,8 @@ def tile_moe_bdx_glu_silu_kernel(
 
         def load_scales(dst, scales, e0=0, e1=E):
             rows = scales[e0:e1, 0].bitcast(I32).rearrange("e f i -> f e i")
-            for q in range(4):
-                nc.sync.dma_start(out=dst[32 * q : 32 * q + 4].bitcast(I32), in_=rows[4 * q : 4 * q + 4])
+            for r in range(4):
+                nc.sync.dma_start(out=dst[r:P:32].bitcast(I32), in_=rows[r:16:4])
 
         a1_sb, a3_sb = {}, {}
 

@@ -29,6 +29,8 @@ HALF = C // 2
 BLOCKS = C // P
 HALVES = 2 * E
 LEAD = 64
+SHARE = 128
+OWN = C - SHARE
 
 WHOLE = 4 * W * C
 A1_AT = 0
@@ -112,6 +114,14 @@ def tile_moe_bdx_glu_silu_kernel(
             for e in range(e0, e1):
                 gate_cols[e] = cols[:, 2 * (e - e0) : 2 * (e - e0 + 1), :]
 
+        gate_share = {}
+
+        def load_share(e0, e1):
+            rows = sbuf([P, e1 - e0, SHARE], F32, f"gate_share{e0}")
+            nc.sync.dma_start(out=rows, in_=gate[:P, e0 * C : e1 * C].rearrange("p (e c) -> p e c", c=C)[:, :, OWN:])
+            for e in range(e0, e1):
+                gate_share[e] = rows[:, e - e0].rearrange("p (c i) -> p c i", i=2)
+
         def load_dy(t):
             nc.sync.dma_start(out=dy[t][:], in_=dy_rows[t])
 
@@ -135,6 +145,7 @@ def tile_moe_bdx_glu_silu_kernel(
         load_scales(w2_sc[1], w2_scales, 1, E)
         load_a3(2, 4)
         load_gates(2, E, sbuf([P, 4 * (E - 2)], F32, "late_gates"))
+        load_share(2, 3)
         load_a1(4, 6)
         load_words(w3_sb, w3_words, 0, 2)
         load_words(w1_sb, w1_words, 0, 2)
@@ -174,16 +185,19 @@ def tile_moe_bdx_glu_silu_kernel(
         def gather(e, t):
             nc.scalar.activation(g_val[e][:, t, :], window(e, t), ACT.Copy)
 
-        def times_gate(e, b0=0, b1=BLOCKS):
-            if b0 == 0:
-                place = LANE_AT + (e - 1) * WHOLE // 2
-                g_bf[e] = placed([P, W * C], BF16, f"g_bf{e}", place)[:]
-            pairs = (b1 - b0) * P // 2
-            factor = gate_ps[e][:, b0 * P // 2 : b1 * P // 2, :].unsqueeze(2).to_broadcast([P, pairs, W, 2])
-            nc.vector.tensor_tensor(
-                into_pairs(g_bf[e][:, W * P * b0 : W * P * b1]),
-                by_pairs(g_val[e][:, :, P * b0 : P * b1]),
-                factor,
+        def ring(e):
+            return RING_AT + e % 2 * WHOLE // 2
+
+        def lane(e):
+            return LANE_AT + e * WHOLE // 2
+
+        def times_gate(engine, e, c0, c1, factor):
+            if e not in g_bf:
+                g_bf[e] = placed([P, W * C], BF16, f"g_bf{e}", ring(e - 1))[:]
+            engine.tensor_tensor(
+                into_pairs(g_bf[e][:, W * c0 : W * c1]),
+                by_pairs(g_val[e][:, :, c0:c1]),
+                factor.unsqueeze(2).to_broadcast([P, (c1 - c0) // 2, W, 2]),
                 MULT,
             )
 
@@ -204,22 +218,21 @@ def tile_moe_bdx_glu_silu_kernel(
             quantize(g_q[e], b0 * P, g_bf[e][:, W * P * b0 : W * P * b1])
 
         def new_d(e):
-            codes = placed([P, 2 * C], U32, f"d_codes{e}", LANE_AT + e * WHOLE // 2)[:]
+            codes = placed([P, 2 * C], U32, f"d_codes{e}", lane(e) if e < E - 1 else ring(e))[:]
             d_q[e] = codes, sbuf([P, 2 * C], U8, f"d_scales{e}")
 
         def make_u(k, t0=0, t1=W):
             if t0 == 0:
-                u[k] = placed([P, W, HALF], F32, f"u{k}", (GV_AT if k == HALVES - 1 else U_AT) + k % 2 * WHOLE // 2)[:]
+                u[k] = placed([P, W, HALF], F32, f"u{k}", U_AT + k % 2 * WHOLE // 2)[:]
             nc.scalar.activation(u[k][:, t0:t1], a1_sb[k][:, t0:t1], ACT.Silu, scale=-1.0)
 
         def new_x(k):
             e = k // 2
-            place = RING_AT + (e - 1) % 2 * WHOLE // 2 if k % 2 else LANE_AT + e * WHOLE // 2
+            place = lane(e) if k % 2 else ring(e)
             x[k] = placed([P, W, HALF], F32, f"x{k}", place)[:]
 
-        def make_z(k):
-            new_x(k)
-            nc.gpsimd.tensor_scalar(x[k], u[k], -1.0, 1.0, MULT, ADD)
+        def make_z_on_scalar(k):
+            nc.scalar.activation(u[k], u[k], ACT.Identity, bias=1.0, scale=-1.0)
 
         def make_z_early(k):
             nc.scalar.activation(x[k], u[k], ACT.Identity, bias=1.0, scale=-1.0)
@@ -333,26 +346,32 @@ def tile_moe_bdx_glu_silu_kernel(
         quantize_g(0, 2, 4)
         first(0, 2)
         first(0, 3)
-        times_gate(1)
+        times_gate(nc.vector, 1, 0, C, gate_ps[1])
         x[0] = placed([P, W, HALF], F32, "x0", DX_AT)[:]
-        x[1] = g_val[2][:, 2:, :].rearrange("p t c -> p (t c)").rearrange("p (t c) -> p t c", t=W)
         nc.gpsimd.tensor_scalar(x[0], u[0], -1.0, 1.0, MULT, ADD)
         make_x(0)
-        make_u(1)
+        u[1] = g_val[2][:, 2:, :].rearrange("p t c -> p (t c)").rearrange("p (t c) -> p t c", t=W)
+        nc.scalar.activation(u[1], a1_sb[1], ACT.Silu, scale=-1.0)
+        new_x(1)
         make_z_early(1)
+        for t in range(2, W):
+            gather(2, t)
         dx = [placed([P, S], F32, f"dx{kt}", DX_AT + kt * 4 * S) for kt in range(KT)]
 
+        waiting = []
         for e in range(E):
             last = e == E - 1
+            n = e + 1
             if e > 0:
                 make_x(2 * e)
-            if 0 < e < E - 1:
-                make_z(2 * e + 1)
+            if e in (2, 3, 4):
+                new_x(2 * e + 1)
+                nc.gpsimd.tensor_scalar(x[2 * e + 1], u[2 * e + 1], -1.0, 1.0, MULT, ADD)
             make_x(2 * e + 1)
             if not last:
-                make_u(2 * e + 2)
-                make_z_in_place(2 * e + 2)
+                make_u(2 * n)
             if e == 0:
+                make_z_on_scalar(2 * n)
                 load_a3(6, 8)
                 load_a1(8, 10)
                 load_words(w3_sb, w3_words, 2, E)
@@ -368,65 +387,57 @@ def tile_moe_bdx_glu_silu_kernel(
             for b in range(BLOCKS):
                 gated(e, b)
             if 0 < e < E - 1:
-                spread_gate(e + 1, 0)
+                spread_gate(n, 0)
             da[e] = [
-                placed([P, W * C], BF16, f"da{e}{i}", place)[:]
-                for i, place in enumerate((LANE_AT + (e + 1) * WHOLE // 2, RING_AT + e % 2 * WHOLE // 2))
+                placed([P, W * C], BF16, f"da{e}{i}", place)[:] for i, place in enumerate((ring(n), lane(n)))
             ]
             steps = ((0, 0), (1, 0), (0, 1), (1, 1), (2, 0), (3, 0))
             if e == 0:
                 steps = ((0, 0), (1, 0), (2, 0), (0, 1), (1, 1), (3, 0))
             if last:
-                steps = ((1, 0), (2, 0), (3, 0), (0, 1), (1, 1))
-                factors = [woven(block_of(a1_sb[2 * e], b), f"a1_woven{b}", b) for b in range(1)]
-                for b in range(1):
-                    delta_aside(e, b, factors[b])
-            for b, i in steps + ((2, 1),):
-                if (b, i) == (2, 1) and 0 < e < E - 1:
-                    times_gate(e + 1)
-                    if e == E - 2:
-                        k = HALVES - 1
-                        make_u(k)
-                        nc.scalar.activation(u[k], u[k], ACT.Identity, bias=1.0, scale=-1.0)
+                steps = ((1, 0), (0, 1), (1, 1), (2, 0), (3, 0))
+                delta_aside(e, 0, woven(block_of(a1_sb[2 * e], 0), "a1_woven", 0))
+            for b, i in steps:
                 delta(e, b, i)
                 if last and (b, i) == (1, 1):
-                    for n, job in enumerate(((4, 0), (4, 1), (2, 2), (3, 2), (4, 2))):
-                        second(*job, 2 + n % 3)
-                if 0 < e < E - 1 and (b, i) == (1, 1):
-                    second(e - 1, 1, BLOCKS + b)
+                    for m, job in enumerate(waiting):
+                        second(*job, BLOCKS - 1 + m % 3)
                 if not last and (b, i) == (0, 1):
-                    for n in (1, 2, 3, 0) if e else range(BLOCKS):
-                        make_th(e + 1, n, n if n or not e else BLOCKS)
-                    if e > 0:
-                        second(e - 1, 0, 1)
-                    if e == 1:
-                        second(0, KT - 1, 2)
-                    if e == E - 2:
-                        second(1, KT - 1, 2)
-                    if e < E - 2:
-                        make_u(2 * e + 3)
+                    for m in (1, 2, 3, 0) if e else range(BLOCKS):
+                        make_th(n, m, m if m or not e else BLOCKS)
+                    make_u(2 * n + 1)
+                    if n not in (2, 3, 4):
+                        make_z_on_scalar(2 * n + 1)
+                if not last and (b, i) == (1, 1):
+                    for index in ((), (1, 2, 5), (1, 5), (1, 5), (1, 2, 5))[e]:
+                        second(*waiting.pop(0), index)
+            if 0 < e < E - 1:
+                own = OWN if n in gate_share else C
+                if own < C:
+                    times_gate(nc.gpsimd, n, own, C, gate_share[n])
+                make_z_in_place(2 * n)
+                times_gate(nc.vector, n, 0, own, gate_ps[n][:, : own // 2])
+            delta(e, 2, 1)
             new_d(e)
             if last:
                 break
+            delta(e, 3, 1)
             if 0 < e < E - 2:
                 new_g(e + 2)
                 for t in range(W):
                     gather(e + 2, t)
-            quantize_g(e + 1)
+            quantize_g(n)
             for b in range(BLOCKS):
-                first(e + 1, b)
-            delta(e, 3, 1)
-            if e == 0:
-                for t in range(2, W):
-                    gather(2, t)
+                first(n, b)
             for i in range(2):
                 quantize(d_q[e], i * C, da[e][i])
+            waiting += [(e, kt) for kt in range(KT)]
 
         e = E - 1
         delta(e, 3, 1)
         for i, h in ((0, 1), (1, 0), (1, 1), (0, 0)):
             quantize(d_q[e], i * C + h * HALF, da_of(e, i, 2 * h, 2 * h + 2))
-        places = ((0, 1), (BLOCKS + 1, BLOCKS + 2), (2, BLOCKS + 3))
+        places = ((0, 1), (2, BLOCKS + 2), (BLOCKS + 1, BLOCKS + 3))
         accs = {}
         for kt, h in ((0, 0), (0, 1), (1, 0), (1, 1), (2, 0), (2, 1)):
             accs[kt, h] = bank(f"acc{e}{kt}{h}", [P, HALF], places[kt][h])

@@ -29,8 +29,7 @@ HALF = C // 2
 BLOCKS = C // P
 HALVES = 2 * E
 LEAD = 64
-SHARE = 128
-OWN = C - SHARE
+SHARE = {2: 128, 3: 64, 4: 64, 5: 64}
 
 WHOLE = 4 * W * C
 A1_AT = 0
@@ -39,8 +38,8 @@ U_AT = A3_AT + 3 * WHOLE
 TH_AT = U_AT + WHOLE
 GV_AT = TH_AT + WHOLE
 LANE_AT = GV_AT + WHOLE // 2
-RING_AT = LANE_AT + (E + 1) * WHOLE // 2
-DX_AT = RING_AT + WHOLE
+RING_AT = LANE_AT + (E + 2) * WHOLE // 2
+DX_AT = RING_AT + WHOLE // 2
 
 
 def tile_moe_bdx_glu_silu_kernel(
@@ -117,8 +116,9 @@ def tile_moe_bdx_glu_silu_kernel(
         gate_share = {}
 
         def load_share(e0, e1):
-            rows = sbuf([P, e1 - e0, SHARE], F32, f"gate_share{e0}")
-            nc.sync.dma_start(out=rows, in_=gate[:P, e0 * C : e1 * C].rearrange("p (e c) -> p e c", c=C)[:, :, OWN:])
+            rows = sbuf([P, e1 - e0, SHARE[e0]], F32, f"gate_share{e0}")
+            experts = gate[:P, e0 * C : e1 * C].rearrange("p (e c) -> p e c", c=C)
+            nc.sync.dma_start(out=rows, in_=experts[:, :, C - SHARE[e0] :])
             for e in range(e0, e1):
                 gate_share[e] = rows[:, e - e0].rearrange("p (c i) -> p c i", i=2)
 
@@ -155,6 +155,7 @@ def tile_moe_bdx_glu_silu_kernel(
         load_a3(4, 6)
         load_a1(6, 8)
         load_words(w2_sb, w2_words, 3, 4)
+        load_share(3, E)
 
         def by_pairs(ap):
             return ap.rearrange("p t (c i) -> p c t i", i=2)
@@ -185,15 +186,12 @@ def tile_moe_bdx_glu_silu_kernel(
         def gather(e, t):
             nc.scalar.activation(g_val[e][:, t, :], window(e, t), ACT.Copy)
 
-        def ring(e):
-            return RING_AT + e % 2 * WHOLE // 2
-
         def lane(e):
             return LANE_AT + e * WHOLE // 2
 
         def times_gate(engine, e, c0, c1, factor):
             if e not in g_bf:
-                g_bf[e] = placed([P, W * C], BF16, f"g_bf{e}", ring(e - 1))[:]
+                g_bf[e] = placed([P, W * C], BF16, f"g_bf{e}", RING_AT)[:]
             engine.tensor_tensor(
                 into_pairs(g_bf[e][:, W * c0 : W * c1]),
                 by_pairs(g_val[e][:, :, c0:c1]),
@@ -218,7 +216,7 @@ def tile_moe_bdx_glu_silu_kernel(
             quantize(g_q[e], b0 * P, g_bf[e][:, W * P * b0 : W * P * b1])
 
         def new_d(e):
-            codes = placed([P, 2 * C], U32, f"d_codes{e}", lane(e) if e < E - 1 else ring(e))[:]
+            codes = placed([P, 2 * C], U32, f"d_codes{e}", lane(e) if e < E - 1 else RING_AT)[:]
             d_q[e] = codes, sbuf([P, 2 * C], U8, f"d_scales{e}")
 
         def make_u(k, t0=0, t1=W):
@@ -228,7 +226,7 @@ def tile_moe_bdx_glu_silu_kernel(
 
         def new_x(k):
             e = k // 2
-            place = lane(e) if k % 2 else ring(e)
+            place = lane(e) if k % 2 else RING_AT
             x[k] = placed([P, W, HALF], F32, f"x{k}", place)[:]
 
         def make_z_on_scalar(k):
@@ -364,14 +362,14 @@ def tile_moe_bdx_glu_silu_kernel(
             n = e + 1
             if e > 0:
                 make_x(2 * e)
-            if e in (2, 3, 4):
+            if 1 < e < E - 1:
                 new_x(2 * e + 1)
                 nc.gpsimd.tensor_scalar(x[2 * e + 1], u[2 * e + 1], -1.0, 1.0, MULT, ADD)
             make_x(2 * e + 1)
             if not last:
                 make_u(2 * n)
             if e == 0:
-                make_z_on_scalar(2 * n)
+                make_z_in_place(2 * n)
                 load_a3(6, 8)
                 load_a1(8, 10)
                 load_words(w3_sb, w3_words, 2, E)
@@ -388,9 +386,8 @@ def tile_moe_bdx_glu_silu_kernel(
                 gated(e, b)
             if 0 < e < E - 1:
                 spread_gate(n, 0)
-            da[e] = [
-                placed([P, W * C], BF16, f"da{e}{i}", place)[:] for i, place in enumerate((ring(n), lane(n)))
-            ]
+            both = placed([P, 2 * W * C], BF16, f"da{e}", lane(n))[:]
+            da[e] = [both[:, : W * C], both[:, W * C :]]
             steps = ((0, 0), (1, 0), (0, 1), (1, 1), (2, 0), (3, 0))
             if e == 0:
                 steps = ((0, 0), (1, 0), (2, 0), (0, 1), (1, 1), (3, 0))
@@ -400,23 +397,27 @@ def tile_moe_bdx_glu_silu_kernel(
             for b, i in steps:
                 delta(e, b, i)
                 if last and (b, i) == (1, 1):
-                    for m, job in enumerate(waiting):
-                        second(*job, BLOCKS - 1 + m % 3)
+                    for m, job in enumerate(waiting[:-1]):
+                        second(*job, m)
                 if not last and (b, i) == (0, 1):
                     for m in (1, 2, 3, 0) if e else range(BLOCKS):
                         make_th(n, m, m if m or not e else BLOCKS)
-                    make_u(2 * n + 1)
-                    if n not in (2, 3, 4):
-                        make_z_on_scalar(2 * n + 1)
-                if not last and (b, i) == (1, 1):
-                    for index in ((), (1, 2, 5), (1, 5), (1, 5), (1, 2, 5))[e]:
+                    for index in ((), (1, 2), (1,), (1,), (1,))[e]:
                         second(*waiting.pop(0), index)
+                    if n < E - 1:
+                        make_u(2 * n + 1)
+                    if n == 1:
+                        make_z_on_scalar(2 * n + 1)
+                if 0 < e < E - 1 and (b, i) == (1, 1):
+                    second(*waiting.pop(0), BLOCKS + b)
+            if n == E - 1:
+                make_u(2 * n + 1)
+                make_z_on_scalar(2 * n + 1)
             if 0 < e < E - 1:
-                own = OWN if n in gate_share else C
-                if own < C:
-                    times_gate(nc.gpsimd, n, own, C, gate_share[n])
-                make_z_in_place(2 * n)
+                own = C - SHARE[n]
                 times_gate(nc.vector, n, 0, own, gate_ps[n][:, : own // 2])
+                times_gate(nc.gpsimd, n, own, C, gate_share[n])
+                make_z_in_place(2 * n)
             delta(e, 2, 1)
             new_d(e)
             if last:
@@ -429,15 +430,17 @@ def tile_moe_bdx_glu_silu_kernel(
             quantize_g(n)
             for b in range(BLOCKS):
                 first(n, b)
-            for i in range(2):
-                quantize(d_q[e], i * C, da[e][i])
+            quantize(d_q[e], 0, both)
             waiting += [(e, kt) for kt in range(KT)]
 
         e = E - 1
+        spare = bank("acc_spare", [P, C], BLOCKS + 2)
+        for step in range(2):
+            second_pass(*waiting[-1], step, spare)
         delta(e, 3, 1)
         for i, h in ((0, 1), (1, 0), (1, 1), (0, 0)):
             quantize(d_q[e], i * C + h * HALF, da_of(e, i, 2 * h, 2 * h + 2))
-        places = ((0, 1), (2, BLOCKS + 2), (BLOCKS + 1, BLOCKS + 3))
+        places = ((0, 1), (2, 3), (BLOCKS + 1, BLOCKS + 3))
         accs = {}
         for kt, h in ((0, 0), (0, 1), (1, 0), (1, 1), (2, 0), (2, 1)):
             accs[kt, h] = bank(f"acc{e}{kt}{h}", [P, HALF], places[kt][h])
@@ -445,6 +448,7 @@ def tile_moe_bdx_glu_silu_kernel(
                 second_pass(e, kt, n if h else 1 - n, accs[kt, h], h * HALF, (h + 1) * HALF, n)
         for h in range(2):
             take_dx(e, 0, accs[0, h], h * HALF, (h + 1) * HALF)
+        nc.vector.tensor_scalar(dx[KT - 1][:, (e - 1) * C : e * C], spare, 0.5, None, MULT)
         for kt in range(1, KT):
             for h in range(2):
                 c0 = e * C + h * HALF

@@ -29,7 +29,8 @@ HALF = C // 2
 BLOCKS = C // P
 HALVES = 2 * E
 LEAD = 64
-SHARE = {2: 128, 3: 64, 4: 64, 5: 64}
+ASIDE = 96
+SHARE = {2: 128}
 
 WHOLE = 4 * W * C
 A1_AT = 0
@@ -155,7 +156,6 @@ def tile_moe_bdx_glu_silu_kernel(
         load_a3(4, 6)
         load_a1(6, 8)
         load_words(w2_sb, w2_words, 3, 4)
-        load_share(3, E)
 
         def by_pairs(ap):
             return ap.rearrange("p t (c i) -> p c t i", i=2)
@@ -283,13 +283,18 @@ def tile_moe_bdx_glu_silu_kernel(
             nc.vector.tensor_tensor(into_pairs(da_of(e, i, b, b + 1)), by_pairs(factor), by_pairs(dr_ps[e, b]), MULT)
 
         def woven(src, name, n):
-            dst = placed([P, P, W], F32, name, GV_AT + n * WHOLE // BLOCKS)[:]
+            src = src[:, :, :ASIDE]
+            dst = placed([P, ASIDE, W], F32, name, GV_AT + n * WHOLE // BLOCKS)[:]
             nc.scalar.copy(dst, src.rearrange("p t c -> p c t"))
             return dst
 
         def delta_aside(e, b, factor):
             dr = woven(dr_ps[e, b], f"dr_woven{b}", 1 + b)
-            nc.gpsimd.tensor_tensor(da_of(e, 0, b, b + 1).rearrange("p (c t) -> p c t", t=W), dr, factor, MULT)
+            share = da_of(e, 0, b, b + 1)[:, : W * ASIDE]
+            nc.gpsimd.tensor_tensor(share.rearrange("p (c t) -> p c t", t=W), dr, factor, MULT)
+            rest = da_of(e, 0, b, b + 1)[:, W * ASIDE :]
+            a1_rest = block_of(a1_sb[2 * e], b)[:, :, ASIDE:]
+            nc.vector.tensor_tensor(into_pairs(rest), by_pairs(a1_rest), by_pairs(dr_ps[e, b][:, :, ASIDE:]), MULT)
 
         def second_pass(e, kt, i, acc, c0=0, c1=C, step=None):
             step = i if step is None else step
@@ -369,7 +374,7 @@ def tile_moe_bdx_glu_silu_kernel(
             if not last:
                 make_u(2 * n)
             if e == 0:
-                make_z_in_place(2 * n)
+                make_z_on_scalar(2 * n)
                 load_a3(6, 8)
                 load_a1(8, 10)
                 load_words(w3_sb, w3_words, 2, E)
@@ -414,9 +419,10 @@ def tile_moe_bdx_glu_silu_kernel(
                 make_u(2 * n + 1)
                 make_z_on_scalar(2 * n + 1)
             if 0 < e < E - 1:
-                own = C - SHARE[n]
+                own = C - SHARE.get(n, 0)
                 times_gate(nc.vector, n, 0, own, gate_ps[n][:, : own // 2])
-                times_gate(nc.gpsimd, n, own, C, gate_share[n])
+                if own < C:
+                    times_gate(nc.gpsimd, n, own, C, gate_share[n])
                 make_z_in_place(2 * n)
             delta(e, 2, 1)
             new_d(e)

@@ -403,7 +403,7 @@ def tile_moe_bdx_glu_silu_kernel(
                 delta(e, b, i)
                 if last and (b, i) == (1, 1):
                     for m, job in enumerate(waiting[:-1]):
-                        second(*job, m)
+                        second(*job, 1 + m)
                 if not last and (b, i) == (0, 1):
                     for m in (1, 2, 3, 0) if e else range(BLOCKS):
                         make_th(n, m, m if m or not e else BLOCKS)
@@ -425,6 +425,8 @@ def tile_moe_bdx_glu_silu_kernel(
                     times_gate(nc.gpsimd, n, own, C, gate_share[n])
                 make_z_in_place(2 * n)
             delta(e, 2, 1)
+            if e == 0:
+                quantize_g(n, 0, 2)
             new_d(e)
             if last:
                 break
@@ -433,7 +435,7 @@ def tile_moe_bdx_glu_silu_kernel(
                 new_g(e + 2)
                 for t in range(W):
                     gather(e + 2, t)
-            quantize_g(n)
+            quantize_g(n, 0 if e else 2)
             for b in range(BLOCKS):
                 first(n, b)
             quantize(d_q[e], 0, both)

@@ -30,7 +30,7 @@ BLOCKS = C // P
 HALVES = 2 * E
 LEAD = 64
 ASIDE = 96
-SHARE = {2: 128}
+SHARE = {2: 128, 5: 128}
 
 WHOLE = 4 * W * C
 A1_AT = 0
@@ -116,12 +116,13 @@ def tile_moe_bdx_glu_silu_kernel(
 
         gate_share = {}
 
-        def load_share(e0, e1):
-            rows = sbuf([P, e1 - e0, SHARE[e0]], F32, f"gate_share{e0}")
-            experts = gate[:P, e0 * C : e1 * C].rearrange("p (e c) -> p e c", c=C)
-            nc.sync.dma_start(out=rows, in_=experts[:, :, C - SHARE[e0] :])
-            for e in range(e0, e1):
-                gate_share[e] = rows[:, e - e0].rearrange("p (c i) -> p c i", i=2)
+        def load_shares():
+            widest = max(SHARE.values())
+            rows = sbuf([P, 2, widest], F32, "gate_shares")
+            experts = gate[:P].rearrange("p (e c) -> p e c", c=C)
+            nc.sync.dma_start(out=rows, in_=experts[:, 2:E:3, C - widest :])
+            for m, e in enumerate(SHARE):
+                gate_share[e] = rows[:, m, widest - SHARE[e] :].rearrange("p (c i) -> p c i", i=2)
 
         def load_dy(t):
             nc.sync.dma_start(out=dy[t][:], in_=dy_rows[t])
@@ -146,7 +147,7 @@ def tile_moe_bdx_glu_silu_kernel(
         load_scales(w2_sc[1], w2_scales, 1, E)
         load_a3(2, 4)
         load_gates(2, E, sbuf([P, 4 * (E - 2)], F32, "late_gates"))
-        load_share(2, 3)
+        load_shares()
         load_a1(4, 6)
         load_words(w3_sb, w3_words, 0, 2)
         load_words(w1_sb, w1_words, 0, 2)
@@ -221,7 +222,7 @@ def tile_moe_bdx_glu_silu_kernel(
 
         def make_u(k, t0=0, t1=W):
             if t0 == 0:
-                u[k] = placed([P, W, HALF], F32, f"u{k}", U_AT + k % 2 * WHOLE // 2)[:]
+                u[k] = placed([P, W, HALF], F32, f"u{k}", (GV_AT if k == HALVES - 1 else U_AT) + k % 2 * WHOLE // 2)[:]
             nc.scalar.activation(u[k][:, t0:t1], a1_sb[k][:, t0:t1], ACT.Silu, scale=-1.0)
 
         def new_x(k):
@@ -282,18 +283,13 @@ def tile_moe_bdx_glu_silu_kernel(
             factor = block_of((a1_sb, x)[i][2 * e + b // 2], b % 2)
             nc.vector.tensor_tensor(into_pairs(da_of(e, i, b, b + 1)), by_pairs(factor), by_pairs(dr_ps[e, b]), MULT)
 
-        def woven(src, name, n):
-            src = src[:, :, :ASIDE]
-            dst = placed([P, ASIDE, W], F32, name, GV_AT + n * WHOLE // BLOCKS)[:]
-            nc.scalar.copy(dst, src.rearrange("p t c -> p c t"))
-            return dst
-
-        def delta_aside(e, b, factor):
-            dr = woven(dr_ps[e, b], f"dr_woven{b}", 1 + b)
+        def delta_aside(e, b):
+            dr = placed([P, ASIDE // 2, W, 2], F32, "dr_aside", GV_AT)[:]
+            nc.scalar.copy(dr, by_pairs(dr_ps[e, b][:, :, :ASIDE]))
             share = da_of(e, 0, b, b + 1)[:, : W * ASIDE]
-            nc.gpsimd.tensor_tensor(share.rearrange("p (c t) -> p c t", t=W), dr, factor, MULT)
+            nc.gpsimd.tensor_tensor(into_pairs(share), dr, by_pairs(block_of(a1_sb[2 * e + b // 2], b % 2)[:, :, :ASIDE]), MULT)
             rest = da_of(e, 0, b, b + 1)[:, W * ASIDE :]
-            a1_rest = block_of(a1_sb[2 * e], b)[:, :, ASIDE:]
+            a1_rest = block_of(a1_sb[2 * e + b // 2], b % 2)[:, :, ASIDE:]
             nc.vector.tensor_tensor(into_pairs(rest), by_pairs(a1_rest), by_pairs(dr_ps[e, b][:, :, ASIDE:]), MULT)
 
         def second_pass(e, kt, i, acc, c0=0, c1=C, step=None):
@@ -397,8 +393,7 @@ def tile_moe_bdx_glu_silu_kernel(
             if e == 0:
                 steps = ((0, 0), (1, 0), (2, 0), (0, 1), (1, 1), (3, 0))
             if last:
-                steps = ((1, 0), (0, 1), (1, 1), (2, 0), (3, 0))
-                delta_aside(e, 0, woven(block_of(a1_sb[2 * e], 0), "a1_woven", 0))
+                steps = steps[:-1]
             for b, i in steps:
                 delta(e, b, i)
                 if last and (b, i) == (1, 1):
@@ -407,7 +402,7 @@ def tile_moe_bdx_glu_silu_kernel(
                 if not last and (b, i) == (0, 1):
                     for m in (1, 2, 3, 0) if e else range(BLOCKS):
                         make_th(n, m, m if m or not e else BLOCKS)
-                    for index in ((), (1, 2), (1,), (1,), (1,))[e]:
+                    for index in ((), (1, 2), (1,), (), (1, 2))[e]:
                         second(*waiting.pop(0), index)
                     if n < E - 1:
                         make_u(2 * n + 1)
@@ -415,15 +410,19 @@ def tile_moe_bdx_glu_silu_kernel(
                         make_z_on_scalar(2 * n + 1)
                 if 0 < e < E - 1 and (b, i) == (1, 1):
                     second(*waiting.pop(0), BLOCKS + b)
-            if n == E - 1:
-                make_u(2 * n + 1)
-                make_z_on_scalar(2 * n + 1)
             if 0 < e < E - 1:
                 own = C - SHARE.get(n, 0)
                 times_gate(nc.vector, n, 0, own, gate_ps[n][:, : own // 2])
                 if own < C:
                     times_gate(nc.gpsimd, n, own, C, gate_share[n])
-                make_z_in_place(2 * n)
+                if n < E - 1:
+                    make_z_in_place(2 * n)
+                else:
+                    make_z_on_scalar(2 * n)
+                    make_u(2 * n + 1)
+                    make_z_on_scalar(2 * n + 1)
+            if last:
+                delta_aside(e, BLOCKS - 1)
             delta(e, 2, 1)
             if e == 0:
                 quantize_g(n, 0, 2)
@@ -446,14 +445,14 @@ def tile_moe_bdx_glu_silu_kernel(
         for step in range(2):
             second_pass(*waiting[-1], step, spare)
         delta(e, 3, 1)
-        for i, h in ((0, 1), (1, 0), (1, 1), (0, 0)):
+        for i, h in ((0, 0), (1, 0), (1, 1), (0, 1)):
             quantize(d_q[e], i * C + h * HALF, da_of(e, i, 2 * h, 2 * h + 2))
         places = ((0, 1), (2, 3), (BLOCKS + 1, BLOCKS + 3))
         accs = {}
         for kt, h in ((0, 0), (0, 1), (1, 0), (1, 1), (2, 0), (2, 1)):
             accs[kt, h] = bank(f"acc{e}{kt}{h}", [P, HALF], places[kt][h])
             for n in range(2):
-                second_pass(e, kt, n if h else 1 - n, accs[kt, h], h * HALF, (h + 1) * HALF, n)
+                second_pass(e, kt, 1 - n if h else n, accs[kt, h], h * HALF, (h + 1) * HALF, n)
         for h in range(2):
             take_dx(e, 0, accs[0, h], h * HALF, (h + 1) * HALF)
         nc.vector.tensor_scalar(dx[KT - 1][:, (e - 1) * C : e * C], spare, 0.5, None, MULT)
@@ -466,9 +465,9 @@ def tile_moe_bdx_glu_silu_kernel(
         ends = (
             (T // 4, T // 2, 3 * T // 4, T),
             (T // 4, T // 2, T - C, T - HALF, T),
-            (T // 4, T // 2, T - C, T - HALF, T),
+            (T // 4, T // 2, T - C, T - 3 * P, T - P, T),
         )
-        stores = ((T // 2, T), (T // 2, T), ends[-1])
+        stores = ((T // 2, T), (T // 2, T), (T // 4, T // 2, T - C, T - P, T))
         nc.vector.tensor_copy(y[2][:, T - HALF :], dx[1][:].indirect(pos1_sb[:, (T - HALF) // 16 :]))
         for kt in range(KT):
             y1, y2 = y[2 * kt], y[2 * kt + 1]
@@ -478,7 +477,7 @@ def tile_moe_bdx_glu_silu_kernel(
                 if (kt, c1) != (1, T):
                     nc.scalar.activation(y1[:, c0:c1], dx[kt][:].indirect(pos1_sb[:, lists]), ACT.Copy)
                 second_choice = dx[kt][:].indirect(pos2_sb[:, lists])
-                if (kt, c1) == (KT - 1, T):
+                if kt == KT - 1 and c1 >= T - P:
                     nc.scalar.activation(y2[:, c0:c1], second_choice, ACT.Copy)
                     second_choice = y2[:, c0:c1]
                 nc.vector.tensor_tensor(y2[:, c0:c1], second_choice, y1[:, c0:c1], ADD)

@@ -29,8 +29,9 @@ HALF = C // 2
 BLOCKS = C // P
 HALVES = 2 * E
 LEAD = 64
-ASIDE = 96
-SHARE = {2: 128, 5: 128}
+EARLY = 96
+ASIDE = 80
+SHARE = {2: 160, 5: 128}
 
 WHOLE = 4 * W * C
 A1_AT = 0
@@ -40,7 +41,7 @@ TH_AT = U_AT + WHOLE
 GV_AT = TH_AT + WHOLE
 LANE_AT = GV_AT + WHOLE // 2
 RING_AT = LANE_AT + (E + 2) * WHOLE // 2
-DX_AT = RING_AT + WHOLE // 2
+DX_AT = RING_AT + WHOLE
 
 
 def tile_moe_bdx_glu_silu_kernel(
@@ -116,13 +117,9 @@ def tile_moe_bdx_glu_silu_kernel(
 
         gate_share = {}
 
-        def load_shares():
-            widest = max(SHARE.values())
-            rows = sbuf([P, 2, widest], F32, "gate_shares")
-            experts = gate[:P].rearrange("p (e c) -> p e c", c=C)
-            nc.sync.dma_start(out=rows, in_=experts[:, 2:E:3, C - widest :])
-            for m, e in enumerate(SHARE):
-                gate_share[e] = rows[:, m, widest - SHARE[e] :].rearrange("p (c i) -> p c i", i=2)
+        def load_share(e, c0, rows):
+            nc.sync.dma_start(out=rows, in_=gate[:P, e * C + c0 : e * C + c0 + rows.shape[1]])
+            gate_share[e, c0] = rows.rearrange("p (c i) -> p c i", i=2)
 
         def load_dy(t):
             nc.sync.dma_start(out=dy[t][:], in_=dy_rows[t])
@@ -143,12 +140,13 @@ def tile_moe_bdx_glu_silu_kernel(
         load_a3(0, 1)
         load_a3(1, 2)
         load_a1(2, 4)
+        load_share(2, C - SHARE[2], sbuf([P, EARLY], F32, "early_share"))
         load_words(w2_sb, w2_words, 1, 2)
         load_scales(w2_sc[1], w2_scales, 1, E)
         load_a3(2, 4)
         load_gates(2, E, sbuf([P, 4 * (E - 2)], F32, "late_gates"))
-        load_shares()
         load_a1(4, 6)
+        load_share(2, C - SHARE[2] + EARLY, sbuf([P, SHARE[2] - EARLY], F32, "late_share"))
         load_words(w3_sb, w3_words, 0, 2)
         load_words(w1_sb, w1_words, 0, 2)
         load_scales(w3_sc, w3_scales)
@@ -157,6 +155,7 @@ def tile_moe_bdx_glu_silu_kernel(
         load_a3(4, 6)
         load_a1(6, 8)
         load_words(w2_sb, w2_words, 3, 4)
+        load_share(E - 1, C - SHARE[E - 1], sbuf([P, SHARE[E - 1]], F32, "last_share"))
 
         def by_pairs(ap):
             return ap.rearrange("p t (c i) -> p c t i", i=2)
@@ -190,9 +189,12 @@ def tile_moe_bdx_glu_silu_kernel(
         def lane(e):
             return LANE_AT + e * WHOLE // 2
 
+        def ring(e):
+            return RING_AT + (e == 1) * WHOLE // 2
+
         def times_gate(engine, e, c0, c1, factor):
             if e not in g_bf:
-                g_bf[e] = placed([P, W * C], BF16, f"g_bf{e}", RING_AT)[:]
+                g_bf[e] = placed([P, W * C], BF16, f"g_bf{e}", ring(e))[:]
             engine.tensor_tensor(
                 into_pairs(g_bf[e][:, W * c0 : W * c1]),
                 by_pairs(g_val[e][:, :, c0:c1]),
@@ -227,7 +229,7 @@ def tile_moe_bdx_glu_silu_kernel(
 
         def new_x(k):
             e = k // 2
-            place = lane(e) if k % 2 else RING_AT
+            place = lane(e) if k % 2 else ring(e)
             x[k] = placed([P, W, HALF], F32, f"x{k}", place)[:]
 
         def make_z_on_scalar(k):
@@ -371,6 +373,7 @@ def tile_moe_bdx_glu_silu_kernel(
                 make_u(2 * n)
             if e == 0:
                 make_z_on_scalar(2 * n)
+                times_gate(nc.gpsimd, 2, C - SHARE[2], C - SHARE[2] + EARLY, gate_share[2, C - SHARE[2]])
                 load_a3(6, 8)
                 load_a1(8, 10)
                 load_words(w3_sb, w3_words, 2, E)
@@ -402,7 +405,7 @@ def tile_moe_bdx_glu_silu_kernel(
                 if not last and (b, i) == (0, 1):
                     for m in (1, 2, 3, 0) if e else range(BLOCKS):
                         make_th(n, m, m if m or not e else BLOCKS)
-                    for index in ((), (1, 2), (1,), (), (1, 2))[e]:
+                    for index in ((), (1, 2), (), (), (1, 2))[e]:
                         second(*waiting.pop(0), index)
                     if n < E - 1:
                         make_u(2 * n + 1)
@@ -414,7 +417,8 @@ def tile_moe_bdx_glu_silu_kernel(
                 own = C - SHARE.get(n, 0)
                 times_gate(nc.vector, n, 0, own, gate_ps[n][:, : own // 2])
                 if own < C:
-                    times_gate(nc.gpsimd, n, own, C, gate_share[n])
+                    done = EARLY if n == 2 else 0
+                    times_gate(nc.gpsimd, n, own + done, C, gate_share[n, own + done])
                 if n < E - 1:
                     make_z_in_place(2 * n)
                 else:
@@ -439,6 +443,8 @@ def tile_moe_bdx_glu_silu_kernel(
                 first(n, b)
             quantize(d_q[e], 0, both)
             waiting += [(e, kt) for kt in range(KT)]
+            if n == E - 1:
+                second(*waiting.pop(-KT), 2 * BLOCKS - 1)
 
         e = E - 1
         spare = bank("acc_spare", [P, C], BLOCKS + 2)

@@ -70,13 +70,13 @@ def tile_moe_bdx_glu_silu_kernel(
         w2_sb = keep.tile([P, E, 2 * H], U8, name="w2_sb", align_bytes=64)
         w1_sb = keep.tile([P, E, 2 * K], U8, name="w1_sb", align_bytes=64)
         w3_sb = keep.tile([P, E, 2 * K], U8, name="w3_sb", align_bytes=64)
-        w2_sc = [keep.tile([P, n, H], U8, name=f"w2_sc{n}", align_bytes=64) for n in (1, E - 1)]
-        w1_sc = keep.tile([P, E, K], U8, name="w1_sc", align_bytes=64)
-        w3_sc = keep.tile([P, E, K], U8, name="w3_sc", align_bytes=64)
+        w2_sc = [keep.tile([P, n, H], U8, name=f"w2_sc{n}", align_bytes=64) for n in (1, 3, 2)]
+        w1_sc = [keep.tile([P, n, K], U8, name=f"w1_sc{n}", align_bytes=64) for n in (2, E - 2)]
+        w3_sc = [keep.tile([P, n, K], U8, name=f"w3_sc{n}", align_bytes=64) for n in (2, E - 2)]
         ident = keep.tile([P, P], F32, name="ident")
 
         make_identity(nc, ident[:])
-        for plane in (*w2_sc, w1_sc, w3_sc):
+        for plane in (*w2_sc, *w1_sc, *w3_sc):
             nc.vector.memset(plane[:].rearrange("p e i -> p (e i)").bitcast(U32), 0)
 
         dy_rows = dyT.rearrange("(p t) c -> t p c", t=W)
@@ -142,15 +142,15 @@ def tile_moe_bdx_glu_silu_kernel(
         load_a1(2, 4)
         load_share(2, C - SHARE[2], sbuf([P, EARLY], F32, "early_share"))
         load_words(w2_sb, w2_words, 1, 2)
-        load_scales(w2_sc[1], w2_scales, 1, E)
+        load_scales(w2_sc[1], w2_scales, 1, 4)
         load_a3(2, 4)
         load_gates(2, E, sbuf([P, 4 * (E - 2)], F32, "late_gates"))
         load_a1(4, 6)
         load_share(2, C - SHARE[2] + EARLY, sbuf([P, SHARE[2] - EARLY], F32, "late_share"))
         load_words(w3_sb, w3_words, 0, 2)
         load_words(w1_sb, w1_words, 0, 2)
-        load_scales(w3_sc, w3_scales)
-        load_scales(w1_sc, w1_scales)
+        load_scales(w3_sc[0], w3_scales, 0, 2)
+        load_scales(w1_sc[0], w1_scales, 0, 2)
         load_words(w2_sb, w2_words, 2, 3)
         load_a3(4, 6)
         load_a1(6, 8)
@@ -268,7 +268,7 @@ def tile_moe_bdx_glu_silu_kernel(
                 lhsT=codes[:, cols].bitcast(E5M2X4),
                 lhsT_scale=scales[:, cols],
                 rhs=w2_sb[:, e].bitcast(E2M1X4),
-                rhs_scale=w2_sc[1][:, e - 1] if e else w2_sc[0][:, 0],
+                rhs_scale=w2_sc[0][:, 0] if e == 0 else w2_sc[1][:, e - 1] if e < 4 else w2_sc[2][:, e - 4],
                 start=True,
                 stop=True,
             )
@@ -301,7 +301,7 @@ def tile_moe_bdx_glu_silu_kernel(
             nc.tensor.matmul_mx(
                 out=acc,
                 lhsT=w[:, e, 2 * P * kt : 2 * P * (kt + 1)].bitcast(E2M1X4),
-                lhsT_scale=sc[:, e, P * kt : P * (kt + 1)],
+                lhsT_scale=(sc[0][:, e] if e < 2 else sc[1][:, e - 2])[:, P * kt : P * (kt + 1)],
                 rhs=codes[:, i * C + c0 : i * C + c1].bitcast(E5M2X4),
                 rhs_scale=scales[:, i * C + c0 : i * C + c1],
                 start=step == 0,
@@ -381,8 +381,11 @@ def tile_moe_bdx_glu_silu_kernel(
                 load_words(w2_sb, w2_words, 4, E)
             if e == 1:
                 load_a3(8, 10)
+                load_scales(w2_sc[2], w2_scales, 4, E)
             if e == 2:
                 load_a1(10, 12)
+                load_scales(w3_sc[1], w3_scales, 2, E)
+                load_scales(w1_sc[1], w1_scales, 2, E)
                 load_a3(10, 12)
                 nc.sync.dma_start(pos1_sb[:], pos1)
                 nc.sync.dma_start(pos2_sb[:], pos2)

from contextlib import ExitStack

import concourse.mybir as mybir
from concourse.masks import make_identity

K, T, E, C, H, N = 384, 1536, 6, 512, 512, 512
S = E * C

FLOPS = 2 * S * (N * H + 2 * H * K)
BYTES = 4 * (N * T + 2 * H * S + S + K * T) + E * (N * H // 2 + H * K) + E * 16 * (H + 2 * K) + 2 * (S + 2 * T)

F32 = mybir.dt.float32
BF16 = mybir.dt.bfloat16
U32 = mybir.dt.uint32
I32 = mybir.dt.int32
U16 = mybir.dt.uint16
U8 = mybir.dt.uint8
E5M2X4 = mybir.dt.float8_e5m2_x4
E2M1X4 = mybir.dt.float4_e2m1fn_x4

ADD = mybir.AluOpType.add
MULT = mybir.AluOpType.mult
ACT = mybir.ActivationFunctionType

P = 128
W = 4
KT = K // P
HALF = C // 2
BLOCKS = C // P
HALVES = 2 * E
LEAD = 64
EARLY = 96
ASIDE = 80
SHARE = {2: 160, 5: 128}

WHOLE = 4 * W * C
A1_AT = 0
A3_AT = A1_AT + E * WHOLE
U_AT = A3_AT + 3 * WHOLE
TH_AT = U_AT + WHOLE
GV_AT = TH_AT + WHOLE
LANE_AT = GV_AT + WHOLE // 2
RING_AT = LANE_AT + (E + 2) * WHOLE // 2
DX_AT = RING_AT + WHOLE


def tile_moe_bdx_glu_silu_kernel(
    tc, dyT, a1, a3, w2_words, w2_scales, w1_words, w1_scales, w3_words, w3_scales, gate, offs, pos1, pos2, out
):
    nc = tc.nc
    with ExitStack() as ctx:
        keep = ctx.enter_context(tc.tile_pool(name="keep", bufs=1))
        flow = ctx.enter_context(tc.tile_pool(name="flow", bufs=1))
        yard = ctx.enter_context(tc.tile_pool(name="yard", bufs=1))
        psum = ctx.enter_context(tc.psum_pool(name="psum", bufs=1))

        def sbuf(shape, dtype, tag):
            return flow.tile(shape, dtype, name=tag, tag=tag, bufs=1, align_bytes=64)[:]

        def placed(shape, dtype, name, offset):
            return yard.tile(shape, dtype, name=name, tag=name, align_bytes=64, offset=offset)

        def bank(name, shape, index):
            return psum.tile(shape, F32, name=name, tag=name, offset=index * 4 * C)[:]

        offs_sb = keep.tile([P, S // 16], U16, name="offs_sb")
        pos1_sb = keep.tile([P, T // 16], U16, name="pos1_sb")
        pos2_sb = keep.tile([P, T // 16], U16, name="pos2_sb")
        dy = [keep.tile([P, T], F32, name=f"dy{t}") for t in range(W)]
        w2_sb = keep.tile([P, E, 2 * H], U8, name="w2_sb", align_bytes=64)
        w1_sb = keep.tile([P, E, 2 * K], U8, name="w1_sb", align_bytes=64)
        w3_sb = keep.tile([P, E, 2 * K], U8, name="w3_sb", align_bytes=64)
        w2_sc = [keep.tile([P, n, H], U8, name=f"w2_sc{n}", align_bytes=64) for n in (1, 3, 2)]
        w1_sc = [keep.tile([P, n, K], U8, name=f"w1_sc{n}", align_bytes=64) for n in (2, E - 2)]
        w3_sc = [keep.tile([P, n, K], U8, name=f"w3_sc{n}", align_bytes=64) for n in (2, E - 2)]
        ident = keep.tile([P, P], F32, name="ident")

        make_identity(nc, ident[:])
        for plane in (*w2_sc, *w1_sc, *w3_sc):
            nc.vector.memset(plane[:].rearrange("p e i -> p (e i)").bitcast(U32), 0)

        dy_rows = dyT.rearrange("(p t) c -> t p c", t=W)
        a1_rows = a1.rearrange("(p t) c -> p t c", t=W)
        a3_rows = a3.rearrange("(p t) c -> p t c", t=W)

        def load_words(dst, words, e0=0, e1=E):
            nc.sync.dma_start(
                out=dst[:, e0:e1].bitcast(I32), in_=words[e0:e1, 0].bitcast(I32).rearrange("e p b -> p e b")
            )

        def load_scales(dst, scales, e0=0, e1=E):
            rows = scales[e0:e1, 0].bitcast(I32).rearrange("e f i -> f e i")
            for r in range(4):
                nc.sync.dma_start(out=dst[r:P:32].bitcast(I32), in_=rows[r:16:4])

        a1_sb, a3_sb = {}, {}

        def load_halves(held, rows, name, place, k0, k1):
            tile = placed([P, W, (k1 - k0) * HALF], F32, f"{name}_{k0}", place)[:]
            nc.sync.dma_start(out=tile, in_=rows[:, :, k0 * HALF : k1 * HALF])
            for k in range(k0, k1):
                held[k] = tile[:, :, (k - k0) * HALF : (k - k0 + 1) * HALF]

        def load_a1(k0, k1):
            load_halves(a1_sb, a1_rows, "a1", A1_AT + k0 * WHOLE // 2, k0, k1)

        def load_a3(k0, k1):
            load_halves(a3_sb, a3_rows, "a3", A3_AT + k0 % 6 * WHOLE // 2, k0, k1)

        gate_cols = {}

        def load_gates(e0, e1, room):
            cols = room[:, : 4 * (e1 - e0)].rearrange("p (k i) -> p k i", i=2)
            nc.sync.dma_start(out=cols, in_=gate[0, e0 * C : e1 * C].rearrange("(k q i) -> q k i", q=P, i=2))
            for e in range(e0, e1):
                gate_cols[e] = cols[:, 2 * (e - e0) : 2 * (e - e0 + 1), :]

        gate_share = {}

        def load_share(e, c0, rows):
            nc.sync.dma_start(out=rows, in_=gate[:P, e * C + c0 : e * C + c0 + rows.shape[1]])
            gate_share[e, c0] = rows.rearrange("p (c i) -> p c i", i=2)

        def load_dy(t):
            nc.sync.dma_start(out=dy[t][:], in_=dy_rows[t])

        a1_sb[0] = placed([P, W, HALF], F32, "a1_0", A1_AT)[:]
        nc.sync.dma_start(out=a1_sb[0][:, 0, :LEAD], in_=a1_rows[:, 0, :LEAD])
        third = placed([P, W, C], F32, "g_val2", A1_AT + (E - 1) * WHOLE)[:]
        load_gates(0, 2, third[:, 0])
        load_dy(0)
        nc.sync.dma_start(offs_sb[:], offs)
        for t in range(1, W):
            load_dy(t)
        load_scales(w2_sc[0], w2_scales, 0, 1)
        nc.sync.dma_start(out=a1_sb[0][:, 0, LEAD:], in_=a1_rows[:, 0, LEAD:HALF])
        nc.sync.dma_start(out=a1_sb[0][:, 1:], in_=a1_rows[:, 1:, :HALF])
        load_a1(1, 2)
        load_words(w2_sb, w2_words, 0, 1)
        load_a3(0, 1)
        load_a3(1, 2)
        load_a1(2, 4)
        load_share(2, C - SHARE[2], sbuf([P, EARLY], F32, "early_share"))
        load_words(w2_sb, w2_words, 1, 2)
        load_scales(w2_sc[1], w2_scales, 1, 4)
        load_a3(2, 4)
        load_gates(2, E, sbuf([P, 4 * (E - 2)], F32, "late_gates"))
        load_a1(4, 6)
        load_share(2, C - SHARE[2] + EARLY, sbuf([P, SHARE[2] - EARLY], F32, "late_share"))
        load_words(w3_sb, w3_words, 0, 2)
        load_words(w1_sb, w1_words, 0, 2)
        load_scales(w3_sc[0], w3_scales, 0, 2)
        load_scales(w1_sc[0], w1_scales, 0, 2)
        load_words(w2_sb, w2_words, 2, 3)
        load_a3(4, 6)
        load_a1(6, 8)
        load_words(w2_sb, w2_words, 3, 4)
        load_share(E - 1, C - SHARE[E - 1], sbuf([P, SHARE[E - 1]], F32, "last_share"))

        def by_pairs(ap):
            return ap.rearrange("p t (c i) -> p c t i", i=2)

        def into_pairs(ap):
            return ap.rearrange("p (c i t) -> p c t i", i=2, t=W)

        def block_of(ap, b):
            return ap[:, :, b * P : (b + 1) * P]

        g_val, g_bf, g_q, d_q, gate_ps = {}, {}, {}, {}, {}
        u, x, th, dh, dr_ps, da = {}, {}, {}, {}, {}, {}

        def spread_gate(e, index):
            rows = bank(f"gate_ps{e}", [P, 2, 2, P], index)
            for i in range(2):
                for h in range(2):
                    column = gate_cols[e][:, h, i : i + 1].to_broadcast([P, P])
                    nc.tensor.transpose(rows[:, i, h, :], column, ident[:])
            gate_ps[e] = rows.rearrange("p i h q -> p (h q) i")

        def new_g(e, offset=GV_AT):
            g_val[e] = placed([P, W, C], F32, f"g_val{e}", offset)[:]

        def window(e, t, c0=0, c1=C):
            return dy[t][:].indirect(offs_sb[:, (e * C + c0) // 16 : (e * C + c1) // 16])

        def gather(e, t):
            nc.scalar.activation(g_val[e][:, t, :], window(e, t), ACT.Copy)

        def lane(e):
            return LANE_AT + e * WHOLE // 2

        def ring(e):
            return RING_AT + (e == 1) * WHOLE // 2

        def times_gate(engine, e, c0, c1, factor):
            if e not in g_bf:
                g_bf[e] = placed([P, W * C], BF16, f"g_bf{e}", ring(e))[:]
            engine.tensor_tensor(
                into_pairs(g_bf[e][:, W * c0 : W * c1]),
                by_pairs(g_val[e][:, :, c0:c1]),
                factor.unsqueeze(2).to_broadcast([P, (c1 - c0) // 2, W, 2]),
                MULT,
            )

        def round_first(b0, b1):
            nc.vector.tensor_copy(
                g_bf[0][:, W * P * b0 : W * P * b1].rearrange("p (c i t) -> p c t i", i=4, t=W),
                g_val[0][:, :, P * b0 : P * b1].rearrange("p t (c i) -> p c t i", i=4),
            )

        def quantize(q, c0, bf):
            cols = slice(c0, c0 + bf.shape[1] // W)
            nc.vector.quantize_mx(out=q[0][:, cols].bitcast(E5M2X4), scales=q[1][:, cols], in_=bf)

        def quantize_g(e, b0=0, b1=BLOCKS):
            if b0 == 0:
                codes = placed([P, C], U32, "g_codes1", A1_AT + WHOLE // 2)[:] if e == 1 else sbuf([P, C], U32, "g_codes")
                g_q[e] = codes, sbuf([P, C], U8, "g_scales")
            quantize(g_q[e], b0 * P, g_bf[e][:, W * P * b0 : W * P * b1])

        def new_d(e):
            codes = placed([P, 2 * C], U32, f"d_codes{e}", lane(e) if e < E - 1 else RING_AT)[:]
            d_q[e] = codes, sbuf([P, 2 * C], U8, f"d_scales{e}")

        def make_u(k, t0=0, t1=W):
            if t0 == 0:
                u[k] = placed([P, W, HALF], F32, f"u{k}", (GV_AT if k == HALVES - 1 else U_AT) + k % 2 * WHOLE // 2)[:]
            nc.scalar.activation(u[k][:, t0:t1], a1_sb[k][:, t0:t1], ACT.Silu, scale=-1.0)

        def new_x(k):
            e = k // 2
            place = lane(e) if k % 2 else ring(e)
            x[k] = placed([P, W, HALF], F32, f"x{k}", place)[:]

        def make_z_on_scalar(k):
            nc.scalar.activation(u[k], u[k], ACT.Identity, bias=1.0, scale=-1.0)

        def make_z_early(k):
            nc.scalar.activation(x[k], u[k], ACT.Identity, bias=1.0, scale=-1.0)

        def make_z_in_place(k):
            nc.gpsimd.tensor_scalar(u[k], u[k], -1.0, 1.0, MULT, ADD)

        def make_x(k):
            if k not in x:
                new_x(k)
                nc.gpsimd.tensor_tensor(x[k], u[k], a3_sb[k], MULT)
            else:
                nc.gpsimd.tensor_tensor(x[k], x[k], a3_sb[k], MULT)

        def turn(src, name, index):
            dst = bank(name, [P, W, P], index)
            for t in range(W):
                nc.tensor.transpose(dst[:, t, :], src[:, t, :], ident[:])
            return dst

        def make_th(e, b, index):
            th[e, b] = placed([P, W, P], F32, f"th{e}{b}", TH_AT + b * WHOLE // BLOCKS)[:]
            a1_ps = turn(block_of(a1_sb[2 * e + b // 2], b % 2), f"a1_ps{e}{b}", index)
            nc.scalar.activation(th[e, b], a1_ps, ACT.Tanh, scale=0.5)

        def first(e, b):
            codes, scales = g_q[e]
            cols = slice(b * P, (b + 1) * P)
            dh[e, b] = bank(f"dh{e}{b}", [P, H], b)
            nc.tensor.matmul_mx(
                out=dh[e, b],
                lhsT=codes[:, cols].bitcast(E5M2X4),
                lhsT_scale=scales[:, cols],
                rhs=w2_sb[:, e].bitcast(E2M1X4),
                rhs_scale=w2_sc[0][:, 0] if e == 0 else w2_sc[1][:, e - 1] if e < 4 else w2_sc[2][:, e - 4],
                start=True,
                stop=True,
            )

        def gated(e, b):
            dr = th[e, b]
            nc.vector.scalar_tensor_tensor(dr, dr, 1.0, dh[e, b].rearrange("s (m t) -> s t m", t=W), ADD, MULT)
            dr_ps[e, b] = turn(dr, f"dr_ps{e}{b}", BLOCKS + b)

        def da_of(e, i, b0, b1):
            return da[e][i][:, b0 * W * P : b1 * W * P]

        def delta(e, b, i):
            factor = block_of((a1_sb, x)[i][2 * e + b // 2], b % 2)
            nc.vector.tensor_tensor(into_pairs(da_of(e, i, b, b + 1)), by_pairs(factor), by_pairs(dr_ps[e, b]), MULT)

        def delta_aside(e, b):
            dr = placed([P, ASIDE // 2, W, 2], F32, "dr_aside", GV_AT)[:]
            nc.scalar.copy(dr, by_pairs(dr_ps[e, b][:, :, :ASIDE]))
            share = da_of(e, 0, b, b + 1)[:, : W * ASIDE]
            nc.gpsimd.tensor_tensor(into_pairs(share), dr, by_pairs(block_of(a1_sb[2 * e + b // 2], b % 2)[:, :, :ASIDE]), MULT)
            rest = da_of(e, 0, b, b + 1)[:, W * ASIDE :]
            a1_rest = block_of(a1_sb[2 * e + b // 2], b % 2)[:, :, ASIDE:]
            nc.vector.tensor_tensor(into_pairs(rest), by_pairs(a1_rest), by_pairs(dr_ps[e, b][:, :, ASIDE:]), MULT)

        def second_pass(e, kt, i, acc, c0=0, c1=C, step=None):
            step = i if step is None else step
            codes, scales = d_q[e]
            w, sc = ((w3_sb, w3_sc), (w1_sb, w1_sc))[i]
            nc.tensor.matmul_mx(
                out=acc,
                lhsT=w[:, e, 2 * P * kt : 2 * P * (kt + 1)].bitcast(E2M1X4),
                lhsT_scale=(sc[0][:, e] if e < 2 else sc[1][:, e - 2])[:, P * kt : P * (kt + 1)],
                rhs=codes[:, i * C + c0 : i * C + c1].bitcast(E5M2X4),
                rhs_scale=scales[:, i * C + c0 : i * C + c1],
                start=step == 0,
                stop=step == 1,
            )

        def take_dx(e, kt, acc, c0=0, c1=C):
            nc.scalar.activation(dx[kt][:, e * C + c0 : e * C + c1], acc, ACT.Copy, scale=0.5)

        def second(e, kt, index):
            acc = bank(f"acc{e}{kt}", [P, C], index)
            for i in range(2):
                second_pass(e, kt, i, acc)
            take_dx(e, kt, acc)

        u[0] = placed([P, W, HALF], F32, "u0", U_AT)[:]
        nc.scalar.activation(u[0][:, 0, :LEAD], a1_sb[0][:, 0, :LEAD], ACT.Silu, scale=-1.0)
        spread_gate(0, 0)
        gate_first = sbuf([P, C], F32, "gate_first")
        nc.vector.tensor_copy(gate_first.rearrange("p (c i) -> p c i", i=2), gate_ps[0])
        spread_gate(1, 2 * BLOCKS - 1)
        new_g(0, DX_AT + WHOLE)
        new_g(1, DX_AT + 3 * WHOLE)
        g_val[2] = third
        for t in range(W):
            for c0, c1 in ((0, C),) if t < W - 1 else ((0, HALF), (HALF, C)):
                nc.vector.tensor_tensor(g_val[0][:, t, c0:c1], window(0, t, c0, c1), gate_first[:, c0:c1], MULT)
            gather(1, t)
            if t == 0:
                nc.vector.tensor_copy(g_val[2][:, t, :], window(2, t))
            if t == 1:
                gather(2, t)
        nc.scalar.activation(u[0][:, 0, LEAD:], a1_sb[0][:, 0, LEAD:], ACT.Silu, scale=-1.0)
        make_u(0, 1, W)
        for b in range(BLOCKS):
            make_th(0, b, BLOCKS + b % 3)
        g_bf[0] = placed([P, W * C], BF16, "g_bf0", DX_AT)[:]
        round_first(0, 2)
        round_first(2, 4)
        quantize_g(0, 0, 2)
        first(0, 0)
        first(0, 1)
        quantize_g(0, 2, 4)
        first(0, 2)
        first(0, 3)
        times_gate(nc.vector, 1, 0, C, gate_ps[1])
        x[0] = placed([P, W, HALF], F32, "x0", DX_AT)[:]
        nc.gpsimd.tensor_scalar(x[0], u[0], -1.0, 1.0, MULT, ADD)
        make_x(0)
        u[1] = g_val[2][:, 2:, :].rearrange("p t c -> p (t c)").rearrange("p (t c) -> p t c", t=W)
        nc.scalar.activation(u[1], a1_sb[1], ACT.Silu, scale=-1.0)
        new_x(1)
        make_z_early(1)
        for t in range(2, W):
            gather(2, t)
        dx = [placed([P, S], F32, f"dx{kt}", DX_AT + kt * 4 * S) for kt in range(KT)]

        waiting = []
        for e in range(E):
            last = e == E - 1
            n = e + 1
            if e > 0:
                make_x(2 * e)
            if 1 < e < E - 1:
                new_x(2 * e + 1)
                nc.gpsimd.tensor_scalar(x[2 * e + 1], u[2 * e + 1], -1.0, 1.0, MULT, ADD)
            make_x(2 * e + 1)
            if not last:
                make_u(2 * n)
            if e == 0:
                make_z_on_scalar(2 * n)
                times_gate(nc.gpsimd, 2, C - SHARE[2], C - SHARE[2] + EARLY, gate_share[2, C - SHARE[2]])
                load_a3(6, 8)
                load_a1(8, 10)
                load_words(w3_sb, w3_words, 2, E)
                load_words(w1_sb, w1_words, 2, E)
                load_words(w2_sb, w2_words, 4, E)
            if e == 1:
                load_a3(8, 10)
                load_scales(w2_sc[2], w2_scales, 4, E)
            if e == 2:
                load_a1(10, 12)
                load_scales(w3_sc[1], w3_scales, 2, E)
                load_scales(w1_sc[1], w1_scales, 2, E)
                load_a3(10, 12)
                nc.sync.dma_start(pos1_sb[:], pos1)
                nc.sync.dma_start(pos2_sb[:], pos2)
            for b in range(BLOCKS):
                gated(e, b)
            if 0 < e < E - 1:
                spread_gate(n, 0)
            both = placed([P, 2 * W * C], BF16, f"da{e}", lane(n))[:]
            da[e] = [both[:, : W * C], both[:, W * C :]]
            steps = ((0, 0), (1, 0), (0, 1), (1, 1), (2, 0), (3, 0))
            if e == 0:
                steps = ((0, 0), (1, 0), (2, 0), (0, 1), (1, 1), (3, 0))
            if last:
                steps = steps[:-1]
            for b, i in steps:
                delta(e, b, i)
                if last and (b, i) == (1, 1):
                    for m, job in enumerate(waiting[:-1]):
                        second(*job, 1 + m)
                if not last and (b, i) == (0, 1):
                    for m in (1, 2, 3, 0) if e else range(BLOCKS):
                        make_th(n, m, m if m or not e else BLOCKS)
                    for index in ((), (1, 2), (), (), (1, 2))[e]:
                        second(*waiting.pop(0), index)
                    if n < E - 1:
                        make_u(2 * n + 1)
                    if n == 1:
                        make_z_on_scalar(2 * n + 1)
                if 0 < e < E - 1 and (b, i) == (1, 1):
                    second(*waiting.pop(0), BLOCKS + b)
            if 0 < e < E - 1:
                own = C - SHARE.get(n, 0)
                times_gate(nc.vector, n, 0, own, gate_ps[n][:, : own // 2])
                if own < C:
                    done = EARLY if n == 2 else 0
                    times_gate(nc.gpsimd, n, own + done, C, gate_share[n, own + done])
                if n < E - 1:
                    make_z_in_place(2 * n)
                else:
                    make_z_on_scalar(2 * n)
                    make_u(2 * n + 1)
                    make_z_on_scalar(2 * n + 1)
            if last:
                delta_aside(e, BLOCKS - 1)
            delta(e, 2, 1)
            if e == 0:
                quantize_g(n, 0, 2)
            new_d(e)
            if last:
                break
            delta(e, 3, 1)
            if 0 < e < E - 2:
                new_g(e + 2)
                for t in range(W):
                    gather(e + 2, t)
            quantize_g(n, 0 if e else 2)
            for b in range(BLOCKS):
                first(n, b)
            quantize(d_q[e], 0, both)
            waiting += [(e, kt) for kt in range(KT)]
            if n == E - 1:
                second(*waiting.pop(-KT), 2 * BLOCKS - 1)

        e = E - 1
        spare = bank("acc_spare", [P, C], BLOCKS + 2)
        for step in range(2):
            second_pass(*waiting[-1], step, spare)
        delta(e, 3, 1)
        for i, h in ((0, 0), (1, 0), (1, 1), (0, 1)):
            quantize(d_q[e], i * C + h * HALF, da_of(e, i, 2 * h, 2 * h + 2))
        places = ((0, 1), (2, 3), (BLOCKS + 1, BLOCKS + 3))
        accs = {}
        for kt, h in ((0, 0), (0, 1), (1, 0), (1, 1), (2, 0), (2, 1)):
            accs[kt, h] = bank(f"acc{e}{kt}{h}", [P, HALF], places[kt][h])
            for n in range(2):
                second_pass(e, kt, 1 - n if h else n, accs[kt, h], h * HALF, (h + 1) * HALF, n)
        for h in range(2):
            take_dx(e, 0, accs[0, h], h * HALF, (h + 1) * HALF)
        nc.vector.tensor_scalar(dx[KT - 1][:, (e - 1) * C : e * C], spare, 0.5, None, MULT)
        for kt in range(1, KT):
            for h in range(2):
                c0 = e * C + h * HALF
                nc.vector.tensor_scalar(dx[kt][:, c0 : c0 + HALF], accs[kt, h], 0.5, None, MULT)

        y = [placed([P, T], F32, f"y{n}", A1_AT + n * 4 * T)[:] for n in range(2 * KT)]
        ends = (
            (T // 4, T // 2, 3 * T // 4, T),
            (T // 4, T // 2, T - C, T - HALF, T),
            (T // 4, T // 2, T - C, T - 3 * P, T - P, T),
        )
        stores = ((T // 2, T), (T // 2, T), (T // 4, T // 2, T - C, T - P, T))
        nc.vector.tensor_copy(y[2][:, T - HALF :], dx[1][:].indirect(pos1_sb[:, (T - HALF) // 16 :]))
        for kt in range(KT):
            y1, y2 = y[2 * kt], y[2 * kt + 1]
            c0 = stored = 0
            for c1 in ends[kt]:
                lists = slice(c0 // 16, c1 // 16)
                if (kt, c1) != (1, T):
                    nc.scalar.activation(y1[:, c0:c1], dx[kt][:].indirect(pos1_sb[:, lists]), ACT.Copy)
                second_choice = dx[kt][:].indirect(pos2_sb[:, lists])
                if kt == KT - 1 and c1 >= T - P:
                    nc.scalar.activation(y2[:, c0:c1], second_choice, ACT.Copy)
                    second_choice = y2[:, c0:c1]
                nc.vector.tensor_tensor(y2[:, c0:c1], second_choice, y1[:, c0:c1], ADD)
                if c1 in stores[kt]:
                    nc.sync.dma_start(out=out[kt * P : (kt + 1) * P, stored:c1], in_=y2[:, stored:c1])
                    stored = c1
                c0 = c1
